import numpy as np, ml_dtypes
CORES = [40,41,42,43,44,45,46,47]
N = 8
BF = ml_dtypes.bfloat16
def gentries(a):
    return np.ascontiguousarray(a.reshape(8, 16, -1).transpose(0, 2, 1)).reshape(8, -1)
def gtable(e):
    e = np.asarray(e); return np.ascontiguousarray(e.reshape(8, -1, 16).transpose(0, 2, 1)).reshape(128, -1).astype(np.int32)
V, G, SL, VI, RO, TH, A = 2304, 256, 768, 3, 2, 20, 190
W = V + (N - 1) * G
def corners(rng, share, wild=False):
    cen = rng.integers(30, 226, (8, 3, 16)); k = np.arange(8)[None, :, None]; u = rng.random((N, 8, V))
    cen[6, 0] = rng.integers(246, 256, 16); cen[7, 0] = rng.integers(0, 10, 16)
    cl = (u > 0.6).astype(np.int64) + (u > 0.85)
    amp = np.exp2(7 * rng.random((N, 8, 1, V))).astype(np.int64) - 1 if wild else rng.integers(0, 25, (N, 8, 1, V))
    x = cen[k, cl].transpose(0, 1, 3, 2) + np.floor((2 * amp + 1) * rng.random((N, 8, 16, V))).astype(np.int64) - amp
    odd = (rng.random((N, 8, 1, V)) < 0.08) & (rng.random((N, 8, 16, V)) < 0.3)
    x = np.clip(np.where(odd, rng.integers(0, 256, x.shape), x), 0, 255)
    flat = rng.random((N, 8, 1, V)); x = np.where(flat < 0.01, 0, np.where(flat > 0.99, 255, x))
    ql = np.where(rng.random(cl.shape) < 0.85, cl, rng.integers(0, 3, cl.shape))
    q = np.ascontiguousarray(np.clip(cen[k, ql].transpose(0, 1, 3, 2) + rng.integers(-6, 7, (N, 8, 16, V)), 0, 255))
    lost = rng.random((N, 8, V)) < share
    nb = rng.integers(0, W, (N, 8, 4, W))
    snd = rng.integers(0, 4, (N, 8, (N - 1) * G)) * W + rng.integers(0, V, (N, 8, (N - 1) * G))
    return cen, np.ascontiguousarray(x), q, lost, nb, snd
def pack(x, q, lost, nb, snd):
    x = np.where(lost[:, :, None, :], -64, x)
    return {"xv": x.reshape(N, 128, V).astype(np.float32).astype(BF), "cq": q.reshape(N, 128, V).astype(np.float32).astype(BF),
            "nb": nb.reshape(N, 8, 4 * W).astype(np.int32), "snd": np.stack([gtable(a) for a in snd])}
def setup_inputs(rng):
    cen, x, q, lost, nb, snd = corners(rng, rng.choice(np.array([0.2, 0.3, 0.4, 0.5]), (N, 8, 1)))
    return pack(x, q, lost, nb, snd)
def setup_inputs_room(rng):
    cen, x, q, lost, nb, snd = corners(rng, 0.3)
    sizes = np.array([SL, SL + 1, SL - 1, 0, 1, V, SL + 64, SL + 2]); n = rng.choice(sizes, (N, 8)); n[:, 0] = SL; n[0] = sizes
    lost = np.argsort(rng.random((N, 8, V)), axis=-1) < n[..., None]
    return pack(x, q, lost, nb, snd)
def setup_inputs_chain(rng):
    cen, x, q, lost, nb, snd = corners(rng, 0.15); H = 32
    nb[:, 5] = np.where(rng.random((N, 4, W)) < 0.25, np.arange(W), nb[:, 5])
    nb[:, 6] = np.where(rng.random((N, 4, W)) < 0.125, rng.choice(np.array([0, V - 1, V, W - 1]), (N, 4, W)), nb[:, 6])
    for a in range(N):
        for g in range(8):
            o = rng.permutation(V); se = o[:128]; ci = o[128:128 + H * VI]; ta = o[128 + H * VI:192 + H * VI]; c = cen[g, 0][:, None]
            lost[a, g, se] = True; lost[a, g, ci] = True; lost[a, g, ta] = False
            x[a, g][:, ta] = np.clip(c + rng.integers(-4, 5, (16, 64)), 0, 255); q[a, g][:, se] = np.clip(c + rng.integers(-6, 7, (16, 128)), 0, 255)
            for k in range(4):
                ck = rng.permutation(ci).reshape(H, VI)
                nb[a, g, k][ck[:, :-1]] = ck[:, 1:]; nb[a, g, k][ck[:, -1]] = rng.choice(ta, H)
                i = rng.integers(1, VI + 1, 128); i[:32] = 1; i[32 + k:64:4] = 0
                nb[a, g, k][se] = np.where(i < VI, ck[rng.integers(0, H, 128), np.minimum(i, VI - 1)], rng.choice(ta, 128))
    return pack(x, q, lost, nb, snd)
def setup_inputs_ties(rng):
    cen, x, q, lost, nb, snd = corners(rng, 0.2); place = np.argsort(rng.random((N, 8, V)), axis=-1)
    for a in range(N):
        for g in range(8):
            lost[a, g, place[a, g, :48]] = True; lost[a, g, place[a, g, 48:240]] = False
    L = np.sum(lost, axis=(1, 2)); R = A - 8 * TH - 7
    base = np.array([TH] + [R // 8 + (1 if i < R % 8 else 0) for i in range(8)] + [TH + 1] * 7)
    for a in range(N):
        for g in range(8):
            for s in range(48):
                kind = s % 6; v = place[a, g, s]; mo = place[a, g, 48 + 4 * s:52 + 4 * s]
                if kind < 4:
                    c = rng.integers(30, 226, 16); e = np.array(base)
                    e[15] += (int(L[a]) & 7) + (1 if kind == 1 else 0)
                    e[0] += 1 if kind == 2 else 0
                    e = e[rng.permutation(16)]
                    m = np.stack([c + e, c - e, c, c + (1 if kind == 3 else 0)])[rng.permutation(4)]
                else:
                    m = np.zeros((4, 16), np.int64); c = np.zeros(16, np.int64); i = rng.permutation(16); kk = np.sort(rng.permutation(4)[:2])
                    m[kk[0], i[:7]] = rng.integers(160, 200, 7); m[kk[1], i[7:14]] = rng.integers(210, 256, 7)
                    if kind == 5: m = 255 - m; c = 255 - c
                x[a, g][:, mo] = m.T; q[a, g][:, v] = c; nb[a, g][:, v] = mo
    return pack(x, q, lost, nb, snd)
def point(rng, links, slots, bad):
    n = bad.size; S = (N - 1) * G
    pk = np.argsort(rng.random((4, n)), axis=1); back = np.argsort(pk, axis=1); links[:, bad] = bad[pk]
    t = rng.permutation(np.concatenate([np.arange(n), rng.integers(0, n, S - n)])); kk = rng.integers(0, 4, S)
    slots[:] = kk * W + bad[back[kk, t]]
def setup_inputs_flood(rng):
    cen, x, q, lost, nb, snd = corners(rng, 0.15); S = (N - 1) * G; B = 3 * S // 4; E = min(S, V - 2 * SL - 32); H = SL - SL % 256; M = min(SL, S)
    for a in range(N):
        for g in range(8):
            n = (SL + E if a == 0 else SL, 1, B if a == 0 else 0, 0, 8, 8, 8, B)[g]; m = G if g == 6 else SL; c = cen[g, 0][:, None]
            o = rng.permutation(V)
            if g == 0 and a == 0:
                s = int(rng.integers(0, V - SL + 1)); run = (o >= s) & (o < s + SL); rest = o[~run]
                o = np.concatenate([rest[:SL + 32], o[run], rest[SL + 32:]])
            se = o[:m]; good = o[SL:SL + 32]; bad = o[SL + 32:SL + 32 + n]
            lost[a, g] = False; lost[a, g, o[:SL]] = True
            x[a, g][:, good] = np.clip(c + rng.integers(-4, 5, (16, 32)), 0, 255); q[a, g][:, se] = np.clip(c + rng.integers(-6, 7, (16, m)), 0, 255)
            far = np.argsort(rng.random((16, n)), axis=0) < 6
            x[a, g][:, bad] = np.where(far, (c + 128) & 255, np.clip(c + rng.integers(-4, 5, (16, n)), 0, 255))
            nb[a, g][:, se] = rng.choice(good, (4, m)); k = rng.integers(0, 4, m)
            if g == 0:
                nb[a, g, k, se] = rng.permutation(bad[:SL])
                if a == 0: point(rng, nb[a, g], snd[a, g], bad[SL:])
                else: nb[a, g, k[:G], se[:G]] = V + (a - 1) * G + rng.permutation(G)
            elif g == 1: nb[a, g, k, se] = bad[0]
            elif g == 2 and a == 0: point(rng, nb[a, g], snd[a, g], bad)
            elif g == 2: nb[a, g, k[:G], se[:G]] = V + (a - 1) * G + rng.permutation(G)
            elif g == 4 or g == 5:
                sh = o[SL + 40:SL + 72]; kk = rng.integers(0, 4, 32); nb[a, g, kk, sh] = bad[0]
                snd[a, g] = (kk * W + sh)[rng.integers(0, 32, S)]
                if g == 4: nb[a, g, k[:G], se[:G]] = V + rng.permutation(G)
                else: nb[a, g, k[:H], se[:H]] = V + int(rng.integers(0, S))
            elif g == 6:
                sh = o[SL + 40:SL + 72]; kk = rng.integers(0, 4, 32); nb[a, g, kk, sh] = rng.choice(bad, 32)
                snd[a, g].reshape(N - 1, G)[:, :48] = (kk * W + sh)[rng.integers(0, 32, (N - 1, 48))]
                nb[a, g, k, se] = V + rng.integers(0, N - 1, G) * G + rng.integers(0, 4 if a & 1 else 48, G)
            elif g == 7:
                point(rng, nb[a, g], snd[a, g], bad)
                nb[a, g, k[:M], se[:M]] = V + rng.permutation(S)[:M]
    return pack(x, q, lost, nb, snd)
def setup_inputs_spread(rng):
    share = rng.choice(np.array([0.02, 0.1, 0.25, 0.4, 0.6, 0.9]), (N, 8, 1)); share[:, 3] = 0.3; share[int(rng.integers(0, N))] = 0
    cen, x, q, lost, nb, snd = corners(rng, share, True)
    return pack(x, q, lost, nb, snd)
def check_inputs(d):
    bad = []
    x = np.asarray(d["xv"]).astype(np.float32).reshape(N, 8, 16, V); q = np.asarray(d["cq"]).astype(np.float32)
    fine = (x >= 0) & (x <= 255) & (x == np.floor(x)); gone = x == -64
    if not np.all(np.all(fine, axis=2) | np.all(gone, axis=2)): bad.append("columns of xv")
    if not np.all((q >= 0) & (q <= 255) & (q == np.floor(q))): bad.append("range of cq")
    if np.min(d["nb"]) < 0 or np.max(d["nb"]) > W - 1: bad.append("range of nb")
    if np.min(d["snd"]) < 0 or np.max(d["snd"]) > 4 * W - 1 or np.max(np.asarray(d["snd"]) % W) > V - 1: bad.append("entries of snd")
    return bad
def reference(xv, cq, nb, snd):
    x = np.full((N, 8, 16, W), -64, np.int32); x[..., :V] = xv.astype(np.float32).astype(np.int32).reshape(N, 8, 16, V)
    q = cq.astype(np.float32).astype(np.int32).reshape(N, 8, 16, V)
    ln = nb.astype(np.int64).reshape(N, 8, 4, W); sl = np.stack([gentries(a) for a in snd]).astype(np.int64)
    for rnd in range(RO):
        shown = np.take_along_axis(ln.reshape(N, 8, 4 * W), sl, 2)
        col = np.take_along_axis(x, shown[:, :, None, :], 3).reshape(N, 8, 16, N - 1, G)
        x[..., V:] = np.stack([np.concatenate([col[(a - d) % N][:, :, d - 1] for d in range(1, N)], axis=2) for a in range(N)])
        lost = x[:, :, 0, :V] < 0; many = np.add.reduce(lost.astype(np.int64), axis=2)
        lim = A + (np.add.reduce(many, axis=1) & 7)
        nx = np.array(x); nl = np.array(ln); fall = np.zeros((N, 8, W), bool)
        for a in range(N):
            v = np.argsort(~lost[a], axis=1, kind="stable")[:, :SL]; there = np.arange(SL)[None, :] < many[a][:, None]
            qa = np.take_along_axis(q[a], v[:, None, :], 2)[:, :, None, :]
            j = np.take_along_axis(ln[a], np.broadcast_to(v[:, None, :], (8, 4, SL)), 2)
            for t in range(VI):
                m = np.take_along_axis(x[a], j.reshape(8, 1, 4 * SL), 2).reshape(8, 16, 4, SL)
                ok = np.add.reduce((np.abs(m - qa) <= TH).astype(np.int32), axis=1) >= 9
                if t < VI - 1: j = np.where(ok, j, np.take_along_axis(ln[a], j, 2))
            found = np.all(ok, axis=1) & there
            y = (np.add.reduce(m, axis=2) - np.max(m, axis=2) - np.min(m, axis=2)) >> 1
            D = np.add.reduce(np.abs(m - y[:, :, None, :]), axis=1)
            good = np.max(D, axis=1) <= lim[a]
            worst = np.take_along_axis(j, np.argmax(D, axis=1)[:, None, :], 1)[:, 0]
            for g in range(8):
                b = np.flatnonzero(found[g] & good[g]); c = v[g][b]
                nx[a, g][:, c] = y[g][:, b]; nl[a, g][:, c] = j[g][:, b]
                fall[a, g, worst[g][found[g] & ~good[g]]] = True
        for a in range(N):
            down = np.array(fall[a, :, :V])
            for d in range(1, N):
                flag = fall[(a + d) % N, :, V + (d - 1) * G:V + d * G]; s = shown[a, :, (d - 1) * G:d * G]
                for g in range(8):
                    h = s[g][flag[g]]; down[g, h[h < V]] = True
            nx[a, :, :, :V] = np.where(down[:, None, :], -64, nx[a, :, :, :V])
        x = nx; ln = nl
    return {"yx": np.ascontiguousarray(x[..., :V]).reshape(N, 128, V).astype(np.float32).astype(BF), "yn": np.ascontiguousarray(ln[..., :V]).reshape(N, 8, 4 * V).astype(np.float32)}

@@ -1,0 +1,689 @@
+from concourse.bass import DstId, RemoteDMATransfer
+from concourse.mybir import AluOpType as A, AxisListType as AX, ActivationFunctionType as AF
+
+N = 8
+V, GH, SL = 2304, 256, 768
+NG = (N - 1) * GH
+W = V + NG
+SCS = (256, 256, 256)
+SEEK = ((0, 256), (256, 768))
+NCH = len(SCS)
+Y1, LC1, O1, G1, O2, G2, Y2, LC2, XW = 0, 768, 784, 3088, 4880, 7184, 8976, 9744, 9760
+MAGIC = 12582912.0
+PERM = (0, 2, 1, 3)
+B16, F16, F32, I32, U16 = "bfloat16", "float16", "float32", "int32", "uint16"
+SIZE = {B16: 2, F16: 2, F32: 4, I32: 4, U16: 2}
+SCRATCH = {"H": ("sbuf", [128, 16, 128], B16)}
+PLACE = {}
+
+
+def _sb(names, cols, dt, tail=""):
+    for name in names.split():
+        if cols > 600:
+            SCRATCH[name + tail] = ("sbuf", [128, cols], dt)
+            PLACE[name + tail] = (name + tail, 0, cols)
+        else:
+            pool = "small_" + dt
+            at = SCRATCH[pool][1][1] if pool in SCRATCH else 0
+            SCRATCH[pool] = ("sbuf", [128, at + (cols + 15) // 16 * 16], dt)
+            PLACE[name + tail] = (pool, at, cols)
+
+
+for _a in [("XB", XW, B16), ("Q IB FX", V, B16), ("LB", W + SL, B16), ("CT", W + 16, B16), ("DN", 1024, I32), ("DH DL", 1024, B16),
+           ("SN SN2 SN3 DC", 112, I32), ("cU kU sU", 112, U16), ("MK GS SB", NG, B16), ("sa sb", 112, F32), ("T28", 32, B16),
+           ("pI LI", 8, I32), ("pF M4", 16, F32), ("IX", 256, B16), ("I32X ZO", 72, B16), ("WS W2 W6", 144, B16), ("WH", 144, F16),
+           ("W3 W4", 576, B16), ("W5", 720, F16), ("XP BO TB ID NI CI CN HI ON GX", 128, B16), ("SE", 16, B16), ("HF", 512, B16),
+           ("K1 VW VB CC CW dl fl ix", 144, F32), ("SIi", SL, F32), ("SI", SL, F16), ("VL", 288, F32), ("LW", 288, B16),
+           ("CH", 144, F16), ("T2", 17, F32), ("LM", 4, F32), ("IN1 QS GV LY", SL, B16), ("SW SW4 b9 nf n16 vf vN vS TH", 48, F32),
+           ("kU1 kU2 vU lU", 48, U16), ("xU", 144, U16), ("OA", 48 * 72, B16), ("OB", 48 * 256, B16), ("FL", 2 * NG, B16), ("YN", 576, F32)]:
+    _sb(*_a)
+for _h, _s in enumerate(SCS):
+    for _a in [("JU", _s, U16), ("JH", _s, F16), ("GL1 GL2 M0 M1 M2 I0 I1 I2 AB", 4 * _s, B16), ("se", 2 * _s, F16), ("jf", _s // 4, F32),
+               ("jh", _s // 2, B16), ("LO HX MD", 2 * _s, B16), ("JK", _s // 4, F32), ("vt", _s + _s // 4, F32), ("cI", _s // 16, U16),
+               ("CG", _s, B16), ("hc", 3 * _s // 16, F32)]:
+        _sb(*_a, tail=str(_h))
+for _b in range(8):
+    SCRATCH["P%d" % _b] = ("psum", [128, 512], F32)
+SEMAPHORES = ["qv", "qa", "qp", "qg"] + ["d%d" % _i for _i in range(30)] + ["r%d" % _i for _i in range(10)] + ["l%d" % _i for _i in range(10)]
+
+CY, PC, GA, SCA, SYNC, PASSES = 1.04, 0.52, 1.56, 3.8, 90.0, 3
+FLIP = ("ch110 ch112 ch210 ev00 ev05 ev07 ev12 ev13 ev15 gv10 jh02 jh12 oa011 oa101 oa102 oa110 oa111 oa112 oa202 oa211 oa212 oa301 oa302 oa310 oa311 "
+        "oa312 oa400 oa401 oa402 oa412 oa500 oa501 oa502 oa510 oa511 oa512 oa600 oa601 oa602 oa612 oa700 oa702 oa711 oa712 qs01 qs12 sc06 te0012 te0111 "
+        "te1102 te1112 te2001 te2010 te2011 te2012 te2101 te2102 te2111 te2112 up02 up10 up12 vi0100 vi0102 vi1000 vi1001 vi1010 vi1011 vi1100 vi1112 "
+        "vi2001 vi2011")
+ENG = {_k: "a" if _k[:2] in ("te", "oa") else "v" for _k in FLIP.split()}
+BIAS = {'a00': -800, 'b000': -100, 'a01': -900, 'b001': -4300, 'b101': -2500, 'c01': -2600, 'f01': -3600, 'v01': -3700, 'h01': -6100, 'a02': -5000,
+        'b002': -5000, 'b102': -5300, 'c02': -1400, 'f02': -3200, 'v02': -8800, 'h02': -4400, 'a10': 12300, 'v10': 500, 'a11': -3300, 'b011': 200,
+        'b111': -1400, 'c11': -2300, 'f11': -2500, 'v11': -2500, 'h11': -8500, 'a12': -3900, 'b012': -4200, 'b112': -4800, 'c12': -5000, 'f12': -4900,
+        'v12': -8700, 'h12': -6800, 'd02': -4500, 'd01': 2900, 'u1': 3000, 's1': 2200, 't1': 700, 'd12': -2100, 'k10': 100, 's0': 400, 'd10': 1300,
+        'e0': -4900, 't0': 1000, 'e1': 5200, 'd00': -3800, 'w1': 400, 'c': 600, 'm1': -3500, 'd11': -8400, 'z1': 3100, 'h00': -1800, 'f00': -400,
+        'b010': -700, 'm0': -7500, 'w0': 200, 'z0': 2200, 'k02': -200, 'l1': 10000}
+PLAN = {}
+
+
+def R(name, c0=None, c1=None, st=1, p0=0, p1=128, ps=1):
+    buf, at, cols = PLACE.get(name, (name, 0, 512))
+    if c0 is None:
+        c0, c1 = 0, cols
+    elif c1 is None:
+        c1 = c0 + 1
+    return (buf, at + c0, at + c1, st, p0, p1, ps)
+
+
+def HB(b0, b1, c0=0, c1=128, p1=128):
+    return ("H", b0, b1, 1, 0, p1, 1, c0, c1)
+
+
+def cnt(r):
+    if r[0] == "H":
+        return (r[2] - r[1]) * (r[8] - r[7])
+    return (r[2] - r[1] + r[3] - 1) // r[3]
+
+
+def build(g, core, T, topo, rank):
+    ops, tag, ntile, nrem = [], ["c"], [0], [0]
+    Q = {"v": g.vector, "a": g.scalar, "p": g.tensor, "g": g, "s": g.sync}
+
+    def tile():
+        ntile[0] += 1
+        return "P%d" % ntile[0]
+
+    def ap(r):
+        if not isinstance(r, tuple):
+            return r
+        if r[0] == "H":
+            if r[2] - r[1] == 1:
+                return T.H[r[4]:r[5], r[1], r[7]:r[8]]
+            return T.H[r[4]:r[5], r[1]:r[2], r[7]:r[8]]
+        return T[PLAN["bank"].get(r[0], r[0])][r[4]:r[5]:r[6], r[1]:r[2]:r[3]]
+
+    def two(*rs):
+        return all(r[0][0] != "P" and SIZE[SCRATCH[r[0]][2]] == 2 for r in rs)
+
+    def op(eng, emit, reads, writes, busy, lat=0.0, kind="c", extra=()):
+        ops.append({"eng": eng, "emit": emit, "r": [r for r in reads if isinstance(r, tuple)], "w": list(writes), "busy": busy,
+                    "lat": lat, "kind": kind, "tag": tag[0], "extra": list(extra)})
+        return len(ops) - 1
+
+    def vc(n):
+        return max(64.0, n) * CY
+
+    def ts(out, in0, s1, op0, s2=None, op1=None):
+        def e():
+            if op1 is None:
+                return g.vector.tensor_scalar(ap(out), ap(in0), ap(s1), None, op0)
+            return g.vector.tensor_scalar(ap(out), ap(in0), ap(s1), ap(s2), op0, op1)
+        return op("v", e, [in0, s1, s2], [out], vc(cnt(in0) * (0.5 if two(out, in0) else 1)))
+
+    def tt(out, a, b, o):
+        f = 1 if a[0][0] == "P" or two(out, a, b) else 2
+        return op("v", lambda: g.vector.tensor_tensor(ap(out), ap(a), ap(b), o), [a, b], [out], vc(cnt(a) * f))
+
+    def cp(out, a):
+        return op("v", lambda: g.vector.tensor_copy(ap(out), ap(a)), [a], [out], vc(cnt(a) * (0.5 if two(out, a) else 1)))
+
+    def ms(out, val):
+        return op("v", lambda: g.vector.memset(ap(out), val), [], [out], vc(cnt(out) * (0.5 if two(out) else 1)))
+
+    def act(out, a, f, bias=0.0, scale=1.0):
+        return op("a", lambda: g.scalar.activation(ap(out), ap(a), f, bias=ap(bias), scale=ap(scale)), [a, bias, scale], [out], vc(cnt(a)) + 30)
+
+    def move(out, a, key):
+        return act(out, a, AF.Identity) if ENG.get(key, "a") == "a" else cp(out, a)
+
+    def ind(win, off):
+        return ap(win).indirect(ap(off))
+
+    def gather(out, win, off, key):
+        if ENG.get(key, "a") == "a":
+            return op("a", lambda: g.scalar.activation(ap(out), ind(win, off), AF.Copy), [win, off], [out], 65 + cnt(out) * GA * CY)
+        return op("v", lambda: g.vector.tensor_copy(ap(out), ind(win, off)), [win, off], [out], 50 + cnt(out) * GA * CY)
+
+    def gtt(out, win, off, b, o):
+        return op("v", lambda: g.vector.tensor_tensor(ap(out), ind(win, off), ap(b), o), [win, off, b], [out], 50 + cnt(out) * GA * CY)
+
+    def mm(items):
+        def e():
+            for o, l, r, s0, s1 in items:
+                ins = g.tensor.matmul(ap(o), ap(l), ap(r), s0, s1)
+            return ins
+        return op("p", e, [x for it in items for x in it[1:3]], sorted({it[0] for it in items}), sum(max(64, cnt(it[2])) for it in items) * PC, 60)
+
+    def acc(out, pairs):
+        return [(out, l, r, i == 0, i == len(pairs) - 1) for i, (l, r) in enumerate(pairs)]
+
+    def iota(out, pat, base=0, cm=0):
+        def e():
+            if SCRATCH[out[0]][2] == I32:
+                return g.iota(ap(out), pat, base, cm)
+            return g.iota(ap(out), pat, base, cm, allow_small_or_imprecise_dtypes=True)
+        return op("g", e, [], [out], 130 + 2 * cnt(out) * CY)
+
+    def dma(q, out, in_, nbytes, extra=()):
+        return op(q, lambda: Q[q].dma_start(ap(out), ap(in_)), [in_], [out] if isinstance(out, tuple) else [], 100, 1900 + nbytes / 180.0, "d", extra)
+
+    def send(parts, extra=()):
+        i = nrem[0]
+        nrem[0] += 1
+        per = 4 if len(parts) <= 4 else 2
+
+        def e():
+            tr = []
+            for j, (d, src, dst) in enumerate(parts):
+                peer = T.cores[(rank + d) % N]
+                rid, pid = topo.addr(peer)[:2]
+                m = sum(1 << x for x in topo.engines(core, peer)[per * j:per * j + per])
+                tr.append(RemoteDMATransfer(dst_ids=[DstId(rid=rid, pnc=pid)], dma_engine_mask=m, remote_sem=T.sem["r%d" % i], src=ap(src), dst=ap(dst)))
+            return g.remote_dma_fused(tr, local_sem=T.sem["l%d" % i])
+        a = op("g", e, [p[1] for p in parts], [], 700, 1500 + 128 * 60.0 / per, "r", extra)
+        ops[a]["sem"] = ("l%d" % i, per * len(parts))
+        b = op(None, None, [], [p[2] for p in parts], 0, 300, "x", [a])
+        ops[b]["sem"] = ("r%d" % i, per * len(parts))
+        return b
+
+    def S(r, name="WS", k=0):
+        return R(name, 144 * k + 15 - r, 144 * k + 143 - r)
+
+    def wrap(src, c0, n, name="WS", byk=False):
+        out = R(tile(), 0, n // 16)
+        mm(acc(out, [(S(r, name, r % 4 if byk else 0), R(src, c0 + r, c0 + n, 16)) for r in range(16)]))
+        return out
+
+    for k in range(4):
+        dma("sa"[k % 2], R("DN", p0=32 * k, p1=32 * k + 32), T.nb[:, W * k:W * k + W], 131072)
+    dma("s", R("SN"), T.snd[:], 57344)
+    dma("s", R("XB", O1, O1 + V), T.xv[:], 589824)
+    for a in range(0, W, 1024):
+        ms(R("LB", a, a + 1024), 1.0)
+    cp(R("DH"), R("DN"))
+    for k in range(4):
+        dma("sa"[k % 2], R("LB", 0, W, p0=k, ps=16), R("DH", p0=32 * k, p1=32 * k + 32), 65536)
+    lo = tt(R("DL"), R("DN"), R("DH"), A.subtract)
+    for k in range(4):
+        dma("sa"[k % 2], R("LB", 0, W, p0=4 + k, ps=16), R("DL", p0=32 * k, p1=32 * k + 32), 65536)
+    dma("s", R("Q"), T.cq[:], 589824, [lo])
+
+    iota(R("pI", 0), [[0, 1]], 0, 1)
+    iota(R("IX"), [[1, 256]])
+    iota(R("XP"), [[1, 128]], 0, -1)
+    iota(R("DC"), [[4, 7], [0, 16]])
+    iota(R("GX"), [[16, 8], [0, 16]])
+    iota(R("I32X"), [[32, 72]])
+    iota(R("SIi"), [[1, SL]])
+    iota(R("SW"), [[16, 48]])
+    iota(R("VW"), [[16, 144]])
+    for a in range(0, 36, 9):
+        iota(R("CT", 64 * a, 64 * a + 576), [[8, 9], [0, 64]], 8 * a)
+        iota(R("IB", 64 * a, 64 * a + 576), [[0, 9], [1, 64]])
+    dma("s", R("CT", 0, V, p0=9, ps=16), R("IB", p0=0, p1=8), 36864)
+    ts(R("pI", 1), R("pI", 0), 15, A.bitwise_and)
+    ts(R("pI", 2), R("pI", 0), 112, A.bitwise_and)
+    ts(R("pI", 3), R("pI", 0), 3, A.bitwise_and)
+    ts(R("pI", 4), R("pI", 0), 15, A.bitwise_and, 2, A.arith_shift_right)
+    cp(R("pF", 0, 5), R("pI", 0, 5))
+    pi, pg, pk, pm = R("pF", 1), R("pF", 2), R("pF", 3), R("pF", 4)
+    lt8, ge8, big, eq8, c0w, c8w, tk, tm = [R("pF", j) for j in range(5, 13)]
+    ts(lt8, pi, 8.0, A.is_lt)
+    ts(ge8, pi, 8.0, A.is_ge)
+    ts(big, pi, 9.0, A.is_ge, 4096.0, A.mult)
+    ts(eq8, pi, 8.0, A.is_equal)
+    ts(tk, pg, pk, A.add)
+    ts(tm, pg, pm, A.add)
+    x144 = R("IX", 0, 144)
+    ts(R("WS"), x144, -15.0, A.add, pg, A.is_equal)
+    act(R("W6"), R("WS"), AF.Identity, scale=lt8)
+    ts(R("WH"), R("WS"), 0.0625, A.mult)
+    ts(R("M4", 0, 4), R("IX", 0, 4), pk, A.is_equal)
+    ts(R("M4", 4, 8), R("IX", 0, 4), pk, A.is_equal, lt8, A.mult)
+    ts(R("M4", 8, 12), R("IX", 0, 4), pm, A.is_equal)
+    ts(R("W2"), x144, -12.0, A.add, tk, A.is_equal)
+    act(R("W2"), R("W2"), AF.Identity, scale=lt8)
+    ts(R("W4", 0, 144), x144, -4.0, A.add, tk, A.is_equal)
+    ts(R("W5", 576, 720), x144, -12.0, A.add, tm, A.is_equal)
+    for k in (3, 2, 1, 0):
+        act(R("W3", 144 * k, 144 * k + 144), R("WS"), AF.Identity, scale=R("M4", 4 + k))
+        act(R("W4", 144 * k, 144 * k + 144), R("W4", 0, 144), AF.Identity, scale=R("M4", 8 + k))
+        ts(R("W5", 144 * k, 144 * k + 144), R("W5", 576, 720), R("M4", k), A.mult)
+    ts(R("BO"), R("GX"), pg, A.is_equal)
+    ts(R("ID"), R("XP"), 0.0, A.is_equal)
+    ts(R("TB"), R("XP"), 0.0, A.is_lt, -1.0, A.mult)
+    tt(R("TB"), R("TB"), R("BO"), A.mult)
+    for n, f in (("NI", -1.0), ("CI", 25.0 / 1024), ("CN", -25.0 / 1024), ("HI", 0.5)):
+        act(R(n), R("ID"), AF.Identity, scale=f)
+    for r, f in ((R("ON"), 1.0), (R("ZO"), 0.0), (R("HF"), -0.5), (R("K1"), 1024.0), (R("XB", LC1, LC1 + 16), -64.0), (R("XB", LC2, LC2 + 16), -64.0),
+                 (R("CT", W, W + 16), 512.0), (HB(0, 8), 0.0), (HB(8, 16), 0.0), (R("T28"), 0.0), (R("LB", W, W + SL), 0.0)):
+        ms(r, f)
+    ts(c0w, pi, 9.0, A.is_equal, lt8, A.add)
+    ts(c8w, pi, 10.0, A.is_equal, -1.0, A.mult)
+    ts(c8w, c8w, eq8, A.add, c0w, A.add)
+    ts(R("SE", 0, 8), R("BO", 0, 128, 16), c0w, A.mult)
+    ts(R("SE", 8, 16), R("BO", 0, 128, 16), c8w, A.mult)
+    cp(R("SI"), R("SIi"))
+    ts(R("SW"), R("SW"), pi, A.add)
+    ts(R("SW4"), R("SW"), float(W), A.add)
+    ts(R("VW"), R("VW"), pi, A.add)
+    ts(R("VB"), R("VW"), float(O1), A.add)
+    ts(R("VL", 0, 144), R("VW"), -1.0, A.mult, float(LC1 - O1), A.add)
+    ts(R("VL", 144, 288), R("VW"), -1.0, A.mult, float(LC2 - O2), A.add)
+    ts(R("SN2"), R("SN"), W - 1, A.bitwise_and)
+    cp(R("cU"), R("SN2"))
+    ts(R("SN3"), R("SN"), 12, A.arith_shift_right)
+    tt(R("SN3"), R("SN3"), R("DC"), A.add)
+    cp(R("kU"), R("SN3"))
+    ts(R("sa", 0, 28), R("DC", 0, 112, 4), 8.0, A.mult, 32.0, A.add)
+    for k in range(4):
+        ts(R("T28", k, 28, 4), R("sa", k, 28, 4), eq8, A.mult, R("M4", 4 + k), A.add)
+    HALF = ((0, 4), (4, 7))
+    for a, b in HALF:
+        gather(R("MK", GH * a, GH * b), R("T28"), R("kU", 16 * a, 16 * b), "mk%d" % a)
+
+    def show_links(rd):
+        tag[0] = "l%d" % rd
+        for a, b in HALF:
+            gtt(R("GS", GH * a, GH * b), R("LB", 0, V), R("cU", 16 * a, 16 * b), R("MK", GH * a, GH * b), A.mult)
+            ps = wrap("GS", GH * a, GH * (b - a), "W6")
+            ts(R("sa", 16 * a, 16 * b), ps, float(V), A.is_ge, -float(W), A.mult)
+            tt(R("sb", 16 * a, 16 * b), ps, R("sa", 16 * a, 16 * b), A.add)
+            ts(R("sU", 16 * a, 16 * b), R("sb", 16 * a, 16 * b), 16.0 if rd == 0 else float(NG), A.add)
+
+    def show_cols(rd, extra):
+        tag[0] = "w%d" % rd
+        win = R("XB", LC1, G1) if rd == 0 else R("XB", G1, G2)
+        gl = G1 if rd == 0 else G2
+        for a, b in HALF:
+            for x, y in ((a, a + 2), (a + 2, b)):
+                gather(R("SB", GH * x, GH * y), win, R("sU", 16 * x, 16 * y), "sc%d%d" % (rd, x))
+            send([(d + 1, R("SB", GH * d, GH * d + GH), R("XB", gl + GH * d, gl + GH * d + GH)) for d in range(a, b)])
+        tag[0] = "t%d" % rd
+        send([(d + 1, R("GS", GH * d, GH * d + GH), R("CT", V + GH * d, V + GH * d + GH)) for d in range(7)], extra)
+
+    def seekers(rd):
+        tag[0] = "s%d" % rd
+        lw = R("LW", 144 * rd, 144 * rd + 144)
+        if rd == 0:
+            ts(lw, wrap("XB", O1, V), 0.0, A.is_lt)
+        p, p2, p3 = tile(), tile(), tile()
+        mm([(R(p, 0, 144), R("BO"), lw, True, True), (R(p, 144, 288), R("TB"), lw, True, True)])
+        op("v", lambda: g.vector.tensor_tensor_scan(ap(R("CC")), ap(R(p, 0, 144)), ap(R("K1")), 0.0, A.add, A.min), [R(p, 0, 144), R("K1")], [R("CC")], vc(144))
+        cp(R("CH"), R("CC"))
+        tt(R("CW"), R(p, 144, 288), R("CC"), A.add)
+        mm(acc(R(p2, 16), [(S(r, "WH"), R("CH", 9 * r + 8)) for r in range(16)]) + acc(R(p2, 0, 16), [(S(r, "WH"), R("CH", r, 144, 9)) for r in range(9)]))
+        cp(R("T2", 16), R(p2, 16))
+        ts(R("T2", 0, 16), R(p2, 0, 16), big, A.add)
+        for s0, s1 in SEEK:
+            tag[0] = "k%d%d" % (rd, s0 // 128)
+            kc = lambda n: R(n, s0 // 16, s1 // 16)
+            i1, si = R("IN1", s0, s1), R("SI", s0, s1)
+            ts(i1, si, R("T2", 16), A.is_ge)
+            ps = wrap("IN1", s0, s1 - s0)
+            ts(kc("kU1"), ps, 15.0, A.min)
+            ts(kc("b9"), ps, 15.0, A.min, 9.0, A.mult)
+            gtt(i1, R("T2", 0, 16), kc("kU1"), si, A.is_le)
+            tt(kc("nf"), wrap("IN1", s0, s1 - s0), kc("b9"), A.add)
+            ts(kc("kU2"), kc("nf"), 143.0, A.min)
+            ts(kc("n16"), kc("nf"), 143.0, A.min, 16.0, A.mult)
+            gtt(i1, R("CW"), kc("kU2"), si, A.is_le)
+            tt(kc("vf"), wrap("IN1", s0, s1 - s0), kc("n16"), A.add)
+            ts(kc("vU"), kc("vf"), float(V - 1), A.min)
+        tag[0] = "z%d" % rd
+        ts(R("vN"), R("vf"), float(V - 1), A.min, -float(W), A.add)
+        tt(R("vS"), R("vN"), R("SW"), A.subtract)
+        ts(R("TH"), R("SW"), R("CC", 143), A.is_ge, 4.0, A.add)
+        mm([(R(p3, 0, 144), R("ON"), lw, True, True)])
+        op("v", lambda: g.vector.tensor_reduce(ap(R("LM", 0)), ap(R(p3, 0, 144)), AX.X, A.add), [R(p3, 0, 144)], [R("LM", 0)], vc(144))
+        cp(R("LI", 0), R("LM", 0))
+        ts(R("LI", 1), R("LI", 0), 7, A.bitwise_and)
+        ts(R("LM", 1), R("LI", 1), 190.0, A.add)
+        ts(R("dl"), R("CW"), -1.0 - SL, A.add)
+        tt(R("dl"), R("dl"), lw, A.mult)
+        tt(R("dl"), R("dl"), R("VL", 144 * rd, 144 * rd + 144), A.add)
+
+    def piece(rd, h, hb):
+        s, SC, s0 = str(h), SCS[h], sum(SCS[:h])
+        IC, KC, TC, key = SC // 4, SC // 16, SC // 128, "%d%d" % (rd, h)
+        xw = R("XB", O1, O2) if rd == 0 else R("XB", O2, Y2)
+        yb = (Y1 if rd == 0 else Y2) + s0
+        kc = lambda n: R(n, s0 // 16, s0 // 16 + KC)
+        ju = lambda j: R("JU" + s, IC * j, IC * j + IC)
+        jh = lambda j: R("JH" + s, IC * j, IC * j + IC)
+        se = lambda j: R("se" + s, IC * j, IC * j + IC)
+
+        def visit(j, l):
+            m, i = "M%d" % j + s, "I%d" % j + s
+            for t in range(TC):
+                gather(R(m, 512 * t, 512 * t + 512), xw, R("JU" + s, IC * l + 32 * t, IC * l + 32 * t + 32), "vi%d%d" % (j, t) + key)
+                p = tile()
+                mm([it for k in range(4) for it in acc(R(p, k, 512, 4), [(R("CI"), R(m, 512 * t + k, 512 * t + 512, 4)), (R("CN"), R("QS", s0 + 128 * t, s0 + 128 * t + 128))])])
+                o = R(i, 512 * t, 512 * t + 512)
+                if ENG.get("te%d%d" % (j, t) + key, "v") == "v":
+                    ts(o, R(p), MAGIC, A.add, MAGIC, A.is_equal)
+                else:
+                    act(o, R(p), AF.Abs)
+                    ts(o, o, 0.5, A.is_lt)
+            return wrap(i, 0, 4 * SC)
+
+        tag[0] = "a" + key
+        gather(R("GV", s0, s0 + SC), R("LB", 0, V), kc("vU"), "gv" + key)
+        gather(R("QS", s0, s0 + SC), R("Q"), kc("vU"), "qs" + key)
+        ps = R(tile(), 0, IC)
+        mm(acc(ps, [(R("W2", 12 - 4 * m, 140 - 4 * m), R("GV", s0 + m, s0 + SC, 4)) for m in range(4)]))
+        for j in range(3):
+            if j:
+                gather(R("GL%d" % j + s), R("LB", 0, W), ju(j - 1), "ch%d" % j + key)
+                ps = wrap("GL%d" % j + s, 0, 4 * SC, "W3", True)
+            if j < 2:
+                cp(ju(j), ps)
+            ts(jh(j), ps, -2048.0, A.add)
+        for j in range(2):
+            tag[0] = "b%d" % j + key
+            ps = visit(j, j)
+            ts(se(2 * j), ps, 9.0, A.is_ge)
+            ts(se(2 * j + 1), ps, 9.0, A.is_lt)
+            tt(se(4 + j), se(2 * j), jh(j), A.mult)
+        tt(se(6), se(3), jh(2), A.mult)
+        tt(se(6), se(6), se(5), A.add)
+        tt(se(6), se(6), se(1), A.mult)
+        tt(jh(3), se(6), se(4), A.add)
+        ts(ju(3), jh(3), 2048.0, A.add)
+        tag[0] = "c" + key
+        ts(se(7), visit(2, 3), 9.0, A.is_ge)
+        pf, pj = R(tile(), 0, KC), tile()
+        mm(acc(pf, [(R("W5", 588 - 4 * t, 716 - 4 * t), R("se" + s, 7 * IC + t, 8 * IC, 4)) for t in range(4)]))
+        mm([it for b, k in enumerate(PERM) for it in
+            acc(R(pj, KC * b, KC * b + KC), [(R("W5", 144 * k + 12 - 4 * t, 144 * k + 140 - 4 * t), R("JH" + s, 3 * IC + t, 4 * IC, 4)) for t in range(4)])])
+        ts(R("JK" + s), R(pj, 0, 4 * KC), -2048.0, A.add)
+        vt = lambda a, n=1: R("vt" + s, KC * a, KC * (a + n))
+        jk = lambda a, n=1: R("JK" + s, KC * a, KC * (a + n))
+        tt(vt(8), pf, kc("TH"), A.is_ge)
+        tt(vt(0, 2), jk(0, 2), jk(2, 2), A.subtract)
+        tag[0] = "f" + key
+        m2 = "M2" + s
+        tt(R("LO" + s), R(m2, 0, 4 * SC, 2), R(m2, 1, 4 * SC, 2), A.min)
+        tt(R("HX" + s), R(m2, 0, 4 * SC, 2), R(m2, 1, 4 * SC, 2), A.max)
+        tt(R("MD" + s, 0, SC), R("LO" + s, 0, 2 * SC, 2), R("LO" + s, 1, 2 * SC, 2), A.max)
+        tt(R("MD" + s, SC, 2 * SC), R("HX" + s, 0, 2 * SC, 2), R("HX" + s, 1, 2 * SC, 2), A.min)
+        ps = R(tile(), 0, SC)
+        mm(acc(ps, [(R("HI"), R("MD" + s, 0, SC)), (R("HI"), R("MD" + s, SC, 2 * SC)), (R("HI"), R("HF", 0, SC))]))
+        y = R("XB", yb, yb + SC)
+        ts(y, ps, MAGIC, A.add, MAGIC, A.subtract)
+        nk = 512 // SC
+        for b in range(0, 4, nk):
+            p = tile()
+            mm([it for x in range(nk) for it in acc(R(p, SC * x, SC * x + SC), [(R("ID"), R(m2, PERM[b + x], 4 * SC, 4)), (R("NI"), y)])])
+            act(R("AB" + s, SC * b, SC * (b + nk)), R(p, 0, SC * nk), AF.Abs)
+        pd = wrap("AB" + s, 0, 4 * SC)[0]
+        tag[0] = "v" + key
+        cp(vt(2, 2), R(pd, 2 * KC, 4 * KC))
+        tt(vt(4, 2), R(pd, 0, 2 * KC), vt(2, 2), A.is_ge)
+        tt(vt(6, 2), R(pd, 0, 2 * KC), vt(2, 2), A.max)
+        tt(vt(0, 2), vt(0, 2), vt(4, 2), A.mult)
+        tt(vt(9), vt(6), vt(7), A.is_ge)
+        tt(vt(10), vt(6), vt(7), A.max)
+        tt(vt(0, 2), vt(0, 2), jk(2, 2), A.add)
+        ts(vt(10), vt(10), R("LM", 1), A.is_le)
+        tt(vt(11), vt(0), vt(1), A.subtract)
+        tt(vt(12), vt(8), vt(10), A.mult)
+        tt(vt(11), vt(11), vt(9), A.mult)
+        tt(vt(13), vt(8), vt(12), A.subtract)
+        tt(vt(11), vt(11), vt(1), A.add)
+        tt(vt(14), vt(12), kc("vN"), A.mult)
+        tt(vt(11), vt(11), vt(13), A.mult)
+        tt(vt(11), vt(11), vt(14), A.add)
+        ts(R("cI" + s), vt(11), float(W), A.add)
+        gather(R("CG" + s), R("CT"), R("cI" + s), "cg" + key)
+        p = tile()
+        mm([(R(p, 8 * (TC * j + t), 8 * (TC * j + t) + 8), R("CG" + s, 128 * t, 128 * t + 128), R("SE", 8 * j, 8 * j + 8), True, True)
+            for j in range(2) for t in range(TC)])
+        hc = lambda a: R("hc" + s, 8 * TC * a, 8 * TC * (a + 1))
+        ts(hc(0), R(p, 0, 8 * TC), -15.5, A.add, MAGIC * 32, A.add)
+        ts(hc(1), hc(0), MAGIC * 32, A.subtract)
+        tt(hc(2), R(p, 8 * TC, 16 * TC), hc(1), A.subtract)
+        tag[0] = "h" + key
+        for gg in range(8):
+            bk, by_act = hb[gg // 2], ENG.get("oa%d" % gg + key, "v") == "a"
+            it = [(R(bk, p1=72), R("ZO"), R("IB", 0, 512), True, False)] if h == 0 and gg % 2 == 0 else []
+            for t in range(TC):
+                j = 6 * gg + s0 // 128 + t
+                if by_act:
+                    act(R("OA", 72 * j, 72 * j + 72), R("I32X"), AF.Abs, bias=R("hc" + s, 8 * TC + 8 * t + gg), scale=-1.0)
+                else:
+                    ts(R("OA", 72 * j, 72 * j + 72), R("I32X"), R("hc" + s, 8 * TC + 8 * t + gg), A.is_equal)
+                ts(R("OB", 256 * j, 256 * j + 256), R("IX"), R("hc" + s, 16 * TC + 8 * t + gg), A.is_equal)
+                it.append((R(bk, 256 * (gg % 2), 256 * (gg % 2) + 256, p1=72), R("OA", 72 * j, 72 * j + 72), R("OB", 256 * j, 256 * j + 256),
+                           False, h == NCH - 1 and gg % 2 == 1 and t == TC - 1))
+            if by_act:
+                oa = R("OA", 72 * (j + 1 - TC), 72 * j + 72)
+                act(oa, oa, AF.Relu, bias=R("K1", 0), scale=-1024.0)
+            mm(it)
+        tag[0] = "d" + key
+        tt(vt(15), vt(12), kc("vS"), A.mult)
+        tt(vt(15), vt(15), kc("SW4"), A.add)
+        cp(kc("lU"), vt(15))
+        ts(R("jf" + s), jh(3), 2048.0, A.add)
+        move(R("jh" + s, 0, IC), R("jf" + s), "jh" + key)
+        tt(R("jh" + s, IC, 2 * IC), R("jf" + s), R("jh" + s, 0, IC), A.subtract)
+        p = tile()
+        mm([it for m in range(4) for it in
+            acc(R(p, m, SC, 4), [(R("W4", 144 * m + 4, 144 * m + 132), R("jh" + s, 0, IC)), (R("W4", 144 * m, 144 * m + 128), R("jh" + s, IC, 2 * IC))])])
+        act(R("LY", s0, s0 + SC), R(p, 0, SC), AF.Identity, bias=ge8)
+
+    def relink(s0, s1):
+        ly, lu = R("LY", s0, s1), R("lU", s0 // 16, s1 // 16)
+        op("v", lambda: g.vector.tensor_copy(ind(R("LB"), lu), ap(ly)), [ly, lu], [R("LB")], 50 + (s1 - s0) * SCA * CY)
+
+    def marks(rd, hb):
+        tag[0] = "m%d" % rd
+        for gg in range(8):
+            move(HB(0, 16, 16 * gg, 16 * gg + 16, 72), R(hb[gg // 2], 256 * (gg % 2), 256 * (gg % 2) + 256, p1=72), "ev%d%d" % (rd, gg))
+        f0 = NG * rd
+        arr = send([(N - d, HB(2 * d, 2 * d + 2), R("FL", f0 + GH * (d - 1), f0 + GH * d)) for d in range(1, N)])
+        tag[0] = "e%d" % rd
+        for s0 in range(0, SL, 256):
+            relink(s0, s0 + 256)
+        if rd == 0:
+            show_links(1)
+        else:
+            for hh in range(2):
+                ps = R(tile(), 0, 288)
+                mm(acc(ps, [(R("W2", 12 - 4 * m, 140 - 4 * m), R("LB", 576 * m + 288 * hh, 576 * m + 288 * hh + 288)) for m in range(4)]))
+                act(R("YN", 288 * hh, 288 * hh + 288), ps, AF.Identity)
+            for k in range(4):
+                dma("s", T.yn[:, V * k:V * k + V], R("YN", p0=k, ps=4), 73728)
+        tag[0] = "u%d" % rd
+        p = tile()
+        mm([it for b in range(2) for it in acc(R(p, b, 144, 2), [(HB(b, b + 1, p1=72), R("ID", 0, 72, p1=72))] +
+            [(R("FL", f0 + 128 * j, f0 + 128 * j + 128, p1=72), R("ID", 0, 72, p1=72)) for j in range(b, 14, 2)])])
+        ts(R("fl"), R(p, 0, 144), 0.0, A.is_gt)
+        tt(R("ix"), R("fl"), R("dl"), A.mult)
+        if rd == 0:
+            tt(R("LW", 144, 288), R("fl"), R("LW", 0, 144), A.not_equal)
+        tt(R("ix"), R("ix"), R("VB" if rd == 0 else "VW"), A.add)
+        cp(R("xU"), R("ix"))
+        win = R("XB", Y1, G1) if rd == 0 else R("XB", O2, XW)
+        for a in range(0, 144, 36):
+            o = R("XB", O2 + 16 * a, O2 + 16 * a + 576) if rd == 0 else R("FX", 16 * a, 16 * a + 576)
+            gather(o, win, R("xU", a, a + 36), "up%d%d" % (rd, a // 36))
+            if rd == 1:
+                dma("s", T.yx[:, 16 * a:16 * a + 576], o, 147456)
+        return arr
+
+    show_links(0)
+    extra = ()
+    for rd in range(2):
+        show_cols(rd, extra)
+        seekers(rd)
+        hb = [tile() for _ in range(4)]
+        for h in range(NCH):
+            piece(rd, h, hb)
+        extra = [marks(rd, hb)]
+    return ops, Q
+
+
+def span(r):
+    if r[0][0] == "P":
+        return r[0], 0, 512, -1
+    m = sum(1 << p for p in range(r[4], r[5], r[6]))
+    if r[0] == "H":
+        return "H", 128 * r[1] + r[7], 128 * (r[2] - 1) + r[8], m
+    return r[0], r[1], r[2], m
+
+
+def hazards(ops):
+    seen = {}
+    for i, o in enumerate(ops):
+        deps = set(o["extra"])
+        acc = [(span(r), False) for r in o["r"]] + [(span(r), True) for r in o["w"]]
+        for sp, wr in acc:
+            for j, lo, hi, m, w2 in seen.get(sp[0], []):
+                if lo < sp[2] and sp[1] < hi and (m & sp[3]) and (wr or w2 or (sp[3] == -1 and ops[j]["eng"] != o["eng"])):
+                    if not (sp[0] == "H" and wr and w2 and ops[j]["tag"] == o["tag"]):
+                        deps.add(j)
+        for sp, wr in acc:
+            lst = seen.setdefault(sp[0], [])
+            if wr and sp[0] != "H":
+                lst[:] = [x for x in lst if not (sp[1] <= x[1] and x[2] <= sp[2] and (x[3] & ~sp[3]) == 0)]
+            lst.append((i, sp[1], sp[2], sp[3], wr))
+        deps.discard(i)
+        o["deps"] = o["base"] = sorted(deps)
+
+
+def place(ops, before, key, fwd):
+    n = len(ops)
+    after = [[] for _ in ops]
+    left = [len(b) for b in before]
+    for i, b in enumerate(before):
+        for j in b:
+            after[j].append(i)
+    est, st, used = [0.0] * n, [0.0] * n, {e: [] for e in "vapgs"}
+    ready = [i for i in range(n) if left[i] == 0]
+    while ready:
+        i = min(ready, key=key.get)
+        ready.remove(i)
+        o, t = ops[i], est[i]
+        if o["eng"]:
+            u = used[o["eng"]]
+            k = len(u)
+            while k and u[k - 1][1] > t:
+                k -= 1
+            while k < len(u) and u[k][0] < t + o["busy"]:
+                t = u[k][1]
+                k += 1
+            u.insert(k, (t, t + o["busy"]))
+        st[i] = t
+        for j in after[i]:
+            est[j] = max(est[j], t + o["busy"] + (o if fwd else ops[j])["lat"] + (0.0 if o["eng"] == "p" == ops[j]["eng"] else SYNC))
+            left[j] -= 1
+            if left[j] == 0:
+                ready.append(j)
+    return st
+
+
+def passes(ops, key):
+    n = len(ops)
+    fwd = [o["deps"] for o in ops]
+    bwd = [[] for _ in ops]
+    for i, o in enumerate(ops):
+        for j in o["deps"]:
+            bwd[j].append(i)
+    best = None
+    for _ in range(PASSES):
+        if key is None:
+            back = place([dict(o, eng=None) for o in ops], bwd, {i: -i for i in range(n)}, False)
+            key = {i: -back[i] - ops[i]["busy"] - BIAS.get(ops[i]["tag"], 0.0) for i in range(n)}
+        st = place(ops, fwd, key, True)
+        end = max(st[i] + ops[i]["busy"] + ops[i]["lat"] for i in range(n))
+        if best is None or end < best[0]:
+            best = (end, st)
+        back = place(ops, bwd, {i: -st[i] - ops[i]["busy"] - ops[i]["lat"] for i in range(n)}, False)
+        key = {i: -back[i] - ops[i]["busy"] for i in range(n)}
+    return best[1]
+
+
+def plan(ops):
+    n = len(ops)
+    for o in ops:
+        o["deps"] = o["base"]
+    st = passes(ops, None)
+    users = {}
+    for i, o in enumerate(ops):
+        for r in o["r"] + o["w"]:
+            if r[0][0] == "P" and i not in users.setdefault(r[0], []):
+                users[r[0]].append(i)
+    last = [[] for _ in range(8)]
+    bank = {}
+
+    def reaches(a, bs):
+        todo, seen = list(bs), set(bs)
+        while todo:
+            x = todo.pop()
+            if x == a:
+                return True
+            for j in ops[x]["deps"]:
+                if j not in seen:
+                    seen.add(j)
+                    todo.append(j)
+        return False
+    for t in sorted(users, key=lambda t: st[users[t][0]]):
+        f = users[t][0]
+        for b in sorted(range(8), key=lambda b: max([st[j] for j in last[b]] + [-1.0])):
+            if not reaches(f, last[b]):
+                break
+        ops[f]["deps"] = sorted(set(ops[f]["deps"]) | set(last[b]))
+        last[b] = users[t]
+        bank[t] = "P%d" % b
+    st = passes(ops, {i: st[i] for i in range(n)})
+    return [(i, st[i], st[i] + ops[i]["busy"] + ops[i]["lat"]) for i in sorted(range(n), key=lambda i: (st[i], i))], bank
+
+
+def rank_program(g, core, T, topo):
+    rank = T.rank_of(core)
+    if rank is None:
+        return
+    ops, Q = build(g, core, T, topo, rank)
+    if "order" not in PLAN:
+        hazards(ops)
+        PLAN["order"], PLAN["bank"] = plan(ops)
+        order = [x[0] for x in PLAN["order"]]
+        pos = {i: k for k, i in enumerate(order)}
+        need = PLAN["need"] = []
+        for o in ops:
+            last = {}
+            for j in o["deps"]:
+                p = ops[j]
+                if o["kind"] == "x" or (p["eng"] == "p" and o["eng"] == "p"):
+                    continue
+                k = p["eng"] if p["kind"] == "c" else j
+                if k not in last or pos[j] > pos[last[k]]:
+                    last[k] = j
+            need.append(sorted(last.values()))
+    need = PLAN["need"]
+    wanted = {j for x in need for j in x}
+    count, done, waited, nd = {e: 0 for e in Q}, {}, {e: {} for e in Q}, 0
+    for i, _s, _f in PLAN["order"]:
+        o = ops[i]
+        e = o["eng"]
+        if o["kind"] == "x":
+            done[i] = o["sem"]
+            continue
+        for j in need[i]:
+            name, val = done[j]
+            if waited[e].get(name, 0) < val:
+                Q[e].wait_ge(T.sem[name], val)
+                waited[e][name] = val
+        ins = o["emit"]()
+        if o["kind"] == "d":
+            done[i] = ("d%d" % nd, 16)
+            ins.then_inc(T.sem["d%d" % nd], 16)
+            nd += 1
+        elif o["kind"] == "r":
+            done[i] = o["sem"]
+        elif i in wanted:
+            count[e] += 1
+            done[i] = ("q" + e, count[e])
+            ins.then_inc(T.sem["q" + e], 1)
+    final = {}
+    for name, val in done.values():
+        final[name] = max(final.get(name, 0), val)
+    for name in sorted(final):
+        if all(waited[e].get(name, 0) < final[name] for e in Q):
+            g.sync.wait_ge(T.sem[name], final[name])

@@ -7,13 +7,13 @@ NG = (N - 1) * GH
 W = V + NG
 SCS = (256, 256, 256)
 SEEK = ((0, 256), (256, 768))
+LINK = ((0, 256), (256, 512), (512, 768))
 NCH = len(SCS)
-Y1, LC1, O1, G1, O2, G2, Y2, LC2, XW = 0, 768, 784, 3088, 4880, 7184, 8976, 9744, 9760
+LC1, Y1, O1, G1, O2, G2, LC2, Y2, XW = 0, 16, 784, 3088, 4880, 7184, 8976, 8992, 9760
 MAGIC = 12582912.0
-PERM = (0, 2, 1, 3)
 B16, F16, F32, I32, U16 = "bfloat16", "float16", "float32", "int32", "uint16"
 SIZE = {B16: 2, F16: 2, F32: 4, I32: 4, U16: 2}
-SCRATCH = {"H": ("sbuf", [128, 16, 128], B16)}
+SCRATCH = {"H": ("sbuf", [128, 8, 256], B16)}
 PLACE = {}
 
 
@@ -29,35 +29,31 @@ def _sb(names, cols, dt, tail=""):
             PLACE[name + tail] = (pool, at, cols)
 
 
-for _a in [("XB", XW, B16), ("Q IB FX", V, B16), ("LB", W + SL, B16), ("CT", W + 16, B16), ("DN", 1024, I32), ("DH DL", 1024, B16),
+KM = max(SCS) // 16
+for _a in [("XB", XW, B16), ("Q", V + 16, B16), ("IB FX XL", V, B16), ("LB", W + SL, B16), ("CT", W + 16, B16), ("DN", 1024, I32), ("DH DL RO", 1024, B16),
            ("SN SN2 SN3 DC", 112, I32), ("cU kU sU", 112, U16), ("MK GS SB", NG, B16), ("sa sb", 112, F32), ("T28", 32, B16),
-           ("pI LI", 8, I32), ("pF M4", 16, F32), ("IX", 256, B16), ("I32X ZO", 72, B16), ("WS W2 W6", 144, B16), ("WH", 144, F16),
-           ("W3 W4", 576, B16), ("W5", 720, F16), ("XP BO TB ID NI CI CN HI ON GX", 128, B16), ("SE", 16, B16), ("HF", 512, B16),
-           ("K1 VW VB CC CW dl fl ix", 144, F32), ("SIi", SL, F32), ("SI", SL, F16), ("VL", 288, F32), ("LW", 288, B16),
-           ("CH", 144, F16), ("T2", 17, F32), ("LM", 4, F32), ("IN1 QS GV LY", SL, B16), ("SW SW4 b9 nf n16 vf vN vS TH", 48, F32),
-           ("kU1 kU2 vU lU", 48, U16), ("xU", 144, U16), ("OA", 48 * 72, B16), ("OB", 48 * 256, B16), ("FL", 2 * NG, B16), ("YN", 576, F32)]:
+           ("pI LI", 8, I32), ("pF M4", 16, F32), ("IX IS WS WS8 W2 W6 W7 WZ W5b CA CB fl", 144, B16), ("ZO", 72, B16), ("WH", 144, F16),
+           ("W3 W4", 576, B16), ("W5", 720, F16), ("XP BO TB ID NI CI CN HI NH I9 I16 DPI MB PB LMD GX", 128, B16), ("IDh NX", 128, F16),
+           ("SE C75", 64, B16), ("RA RB", 512, B16), ("CZ", 4 * KM, B16), ("JP RP", 6 * KM, B16),
+           ("K1 CC CW TG ix LJ", 144, F32), ("SI", SL, F32), ("LW", 288, B16), ("CH", 144, F16), ("T2", 17, F32), ("LM", 4, F32),
+           ("IN1 QS GV LY", SL, B16), ("SW vF vS rs", 48, F32), ("k1h k2h", 48, B16), ("vH", 48, F16), ("SEL", 288, F32),
+           ("kU1 kU2 vU lU", 48, U16), ("xU", 144, U16), ("OA", 48 * 72, B16), ("HR", 1024, F32), ("OB", 48 * 128, B16), ("FL", 2 * NG, B16), ("YN", 576, F32)]:
     _sb(*_a)
 for _h, _s in enumerate(SCS):
-    for _a in [("JU", _s, U16), ("JH", _s, F16), ("GL1 GL2 M0 M1 M2 I0 I1 I2 AB", 4 * _s, B16), ("se", 2 * _s, F16), ("jf", _s // 4, F32),
-               ("jh", _s // 2, B16), ("LO HX MD", 2 * _s, B16), ("JK", _s // 4, F32), ("vt", _s + _s // 4, F32), ("cI", _s // 16, U16),
-               ("CG", _s, B16), ("hc", 3 * _s // 16, F32)]:
+    SCRATCH["AB%d" % _h] = ("sbuf", [128, _s // 16, 96], B16)
+    for _a in [("JU", _s, U16), ("JH", _s // 2, F16), ("GL1 GL2 M0 M1 M2 I0 I1 I2", 4 * _s, B16), ("MN", 4 * _s, B16), ("MX", 4 * _s, F16), ("S0 S1 SJ", 3 * _s // 4, F16),
+               ("ub", _s // 4, B16), ("jh", _s // 2, B16), ("RM tb lo", 6 * _s // 16, F32), ("cI", _s // 16, U16), ("CG", _s, B16), ("hc", _s // 4, F32)]:
         _sb(*_a, tail=str(_h))
 for _b in range(8):
     SCRATCH["P%d" % _b] = ("psum", [128, 512], F32)
-SEMAPHORES = ["qv", "qa", "qp", "qg"] + ["d%d" % _i for _i in range(30)] + ["r%d" % _i for _i in range(10)] + ["l%d" % _i for _i in range(10)]
+SEMAPHORES = ["qv", "qa", "qp", "qg"] + ["d%d" % _i for _i in range(44)] + ["r%d" % _i for _i in range(10)] + ["l%d" % _i for _i in range(10)]
 
-CY, PC, GA, SCA, SYNC, PASSES = 1.04, 0.52, 1.56, 3.8, 90.0, 3
-FLIP = ("ch110 ch112 ch210 ev00 ev05 ev07 ev12 ev13 ev15 gv10 jh02 jh12 oa011 oa101 oa102 oa110 oa111 oa112 oa202 oa211 oa212 oa301 oa302 oa310 oa311 "
-        "oa312 oa400 oa401 oa402 oa412 oa500 oa501 oa502 oa510 oa511 oa512 oa600 oa601 oa602 oa612 oa700 oa702 oa711 oa712 qs01 qs12 sc06 te0012 te0111 "
-        "te1102 te1112 te2001 te2010 te2011 te2012 te2101 te2102 te2111 te2112 up02 up10 up12 vi0100 vi0102 vi1000 vi1001 vi1010 vi1011 vi1100 vi1112 "
-        "vi2001 vi2011")
-ENG = {_k: "a" if _k[:2] in ("te", "oa") else "v" for _k in FLIP.split()}
-BIAS = {'a00': -800, 'b000': -100, 'a01': -900, 'b001': -4300, 'b101': -2500, 'c01': -2600, 'f01': -3600, 'v01': -3700, 'h01': -6100, 'a02': -5000,
-        'b002': -5000, 'b102': -5300, 'c02': -1400, 'f02': -3200, 'v02': -8800, 'h02': -4400, 'a10': 12300, 'v10': 500, 'a11': -3300, 'b011': 200,
-        'b111': -1400, 'c11': -2300, 'f11': -2500, 'v11': -2500, 'h11': -8500, 'a12': -3900, 'b012': -4200, 'b112': -4800, 'c12': -5000, 'f12': -4900,
-        'v12': -8700, 'h12': -6800, 'd02': -4500, 'd01': 2900, 'u1': 3000, 's1': 2200, 't1': 700, 'd12': -2100, 'k10': 100, 's0': 400, 'd10': 1300,
-        'e0': -4900, 't0': 1000, 'e1': 5200, 'd00': -3800, 'w1': 400, 'c': 600, 'm1': -3500, 'd11': -8400, 'z1': 3100, 'h00': -1800, 'f00': -400,
-        'b010': -700, 'm0': -7500, 'w0': 200, 'z0': 2200, 'k02': -200, 'l1': 10000}
+CY, PC, GA, SCA, SYNC, PASSES = 1.04, 0.52, 1.56, 3.8, 90.0, 1
+TIME = {'g0': 21.5, 'a10': -44.0, 'a20': 12.5, 'g1': 52.5, 'a11': -10.0, 'a21': -4.0, 'g2': 16.0, 'a12': -11.0, 'a22': 1.0, 'b00': 2.0, 'b10': 6.0, 'c0': 2.5, 'f0': 16.0, 'v0': 5.0, 'h0': 43.5, 'b01': 26.0, 'b11': 2.5, 'c1': 30.5, 'f1': 52.0, 'v1': 40.0, 'h1': 29.0, 'b02': 37.0, 'b12': 4.5, 'c2': 22.0, 'f2': 26.5, 'v2': 30.5, 'h2': 43.5, 'd0': -9.0, 'd1': -8.5, 'd2': 39.5, 'e0': 32.5, 'e2': 12.5, 'e4': 49.5, 'm': 40.0, 'o': -4.0, 'z': -10.5, 's': -51.5, 'k0': -55.5, 'k2': -14.5, 'w': -11.5, 't': -43.5, 'l': -1.5, 'u': 43.0, 'n': 73.5, 'c': -51.0}
+VEE = {'a10': 2, 'b00': 1, 'b01': 1, 'Tb00': 3, 'Tb10': 3, 'Tb01': 3, 'Tb11': 3, 'Tb12': 2, 'Tc0': 1, 'Tc1': 2, 'k0': 1, 'k2': 1, 'n': 1, 'u0': 0, 'u1': 5, 'c': 28485847872, 'a12': 1, 'w1': 1, 'w0': 0, 'b12': 2, 'a21': 2, 'Tc2': 3, 'g1': 2, 'c0': 1, 'g2': 2, 'Tb02': 3, 'c1': 2, 's': 1}
+SLACK, LATE = 100.0, 1.0
+CHN, VIS = 1, (1, 1, 1)
+EDGES = []
 PLAN = {}
 
 
@@ -70,13 +66,13 @@ def R(name, c0=None, c1=None, st=1, p0=0, p1=128, ps=1):
     return (buf, at + c0, at + c1, st, p0, p1, ps)
 
 
-def HB(b0, b1, c0=0, c1=128, p1=128):
-    return ("H", b0, b1, 1, 0, p1, 1, c0, c1)
+def R3(name, b0, b1, c0, c1, st=1, p1=128):
+    return (name, b0, b1, st, 0, p1, 1, c0, c1)
 
 
 def cnt(r):
-    if r[0] == "H":
-        return (r[2] - r[1]) * (r[8] - r[7])
+    if len(r) == 9:
+        return (r[2] - r[1]) * ((r[8] - r[7] + r[3] - 1) // r[3])
     return (r[2] - r[1] + r[3] - 1) // r[3]
 
 
@@ -91,76 +87,106 @@ def build(g, core, T, topo, rank):
     def ap(r):
         if not isinstance(r, tuple):
             return r
-        if r[0] == "H":
+        if len(r) == 9:
             if r[2] - r[1] == 1:
-                return T.H[r[4]:r[5], r[1], r[7]:r[8]]
-            return T.H[r[4]:r[5], r[1]:r[2], r[7]:r[8]]
+                return T[r[0]][r[4]:r[5], r[1], r[7]:r[8]:r[3]]
+            return T[r[0]][r[4]:r[5], r[1]:r[2], r[7]:r[8]:r[3]]
         return T[PLAN["bank"].get(r[0], r[0])][r[4]:r[5]:r[6], r[1]:r[2]:r[3]]
 
     def two(*rs):
         return all(r[0][0] != "P" and SIZE[SCRATCH[r[0]][2]] == 2 for r in rs)
 
-    def op(eng, emit, reads, writes, busy, lat=0.0, kind="c", extra=()):
-        ops.append({"eng": eng, "emit": emit, "r": [r for r in reads if isinstance(r, tuple)], "w": list(writes), "busy": busy,
-                    "lat": lat, "kind": kind, "tag": tag[0], "extra": list(extra)})
+    def op(ways, reads, writes, lat=0.0, kind="c", extra=()):
+        busy = {e: w[1] + (w[2] * (PC if e == "p" else CY) + (w[3] * GA + w[4] * SCA) * CY) for e, w in ways.items()}
+        ops.append({"ways": ways, "busy": busy, "r": [r for r in reads if isinstance(r, tuple)], "w": list(writes), "lat": lat, "kind": kind,
+                    "tag": tag[0], "extra": list(extra)})
         return len(ops) - 1
 
-    def vc(n):
-        return max(64.0, n) * CY
+    def vw(f, n):
+        return (f, 0.0, max(64.0, n), 0, 0)
 
     def ts(out, in0, s1, op0, s2=None, op1=None):
         def e():
             if op1 is None:
                 return g.vector.tensor_scalar(ap(out), ap(in0), ap(s1), None, op0)
             return g.vector.tensor_scalar(ap(out), ap(in0), ap(s1), ap(s2), op0, op1)
-        return op("v", e, [in0, s1, s2], [out], vc(cnt(in0) * (0.5 if two(out, in0) else 1)))
+        return op({"v": vw(e, cnt(in0) * (0.5 if two(out, in0) else 1))}, [in0, s1, s2], [out])
 
     def tt(out, a, b, o):
-        f = 1 if a[0][0] == "P" or two(out, a, b) else 2
-        return op("v", lambda: g.vector.tensor_tensor(ap(out), ap(a), ap(b), o), [a, b], [out], vc(cnt(a) * f))
+        f = 1 if "P" in (a[0][0], b[0][0]) else 2
+        return op({"v": vw(lambda: g.vector.tensor_tensor(ap(out), ap(a), ap(b), o), cnt(a) * f)}, [a, b], [out])
+
+    def cpw(out, a):
+        return vw(lambda: g.vector.tensor_copy(ap(out), ap(a)), cnt(a) * (0.5 if two(out, a) else 1))
 
     def cp(out, a):
-        return op("v", lambda: g.vector.tensor_copy(ap(out), ap(a)), [a], [out], vc(cnt(a) * (0.5 if two(out, a) else 1)))
+        return op({"v": cpw(out, a)}, [a], [out])
 
-    def ms(out, val):
-        return op("v", lambda: g.vector.memset(ap(out), val), [], [out], vc(cnt(out) * (0.5 if two(out) else 1)))
+    def ms(out, val, src=None):
+        ways = {"v": vw(lambda: g.vector.memset(ap(out), val), cnt(out) * (0.5 if two(out) else 1))}
+        if src:
+            ways["a"] = actw(out, src, AF.Identity, val, 0.0)
+        return op(ways, [src], [out])
+
+    def scan(out, d0, d1, first, op0, op1):
+        return op({"v": vw(lambda: g.vector.tensor_tensor_scan(ap(out), ap(d0), ap(d1), first, op0, op1), cnt(d0) * (0.5 if two(out, d0, d1) else 1))}, [d0, d1], [out])
+
+    def actw(out, a, f, bias=0.0, scale=1.0):
+        return (lambda: g.scalar.activation(ap(out), ap(a), f, bias=ap(bias), scale=ap(scale)), 60.0, max(64.0, cnt(a)), 0, 0)
 
     def act(out, a, f, bias=0.0, scale=1.0):
-        return op("a", lambda: g.scalar.activation(ap(out), ap(a), f, bias=ap(bias), scale=ap(scale)), [a, bias, scale], [out], vc(cnt(a)) + 30)
+        return op({"a": actw(out, a, f, bias, scale)}, [a, bias, scale], [out])
 
-    def move(out, a, key):
-        return act(out, a, AF.Identity) if ENG.get(key, "a") == "a" else cp(out, a)
+    def move(out, a):
+        return op({"v": cpw(out, a), "a": actw(out, a, AF.Identity)}, [a], [out])
+
+    def scaled(out, a, f):
+        v = vw(lambda: g.vector.tensor_scalar(ap(out), ap(a), ap(f), None, A.mult), cnt(a) * (0.5 if two(out, a) else 1))
+        return op({"v": v, "a": actw(out, a, AF.Identity, 0.0, f)}, [a, f], [out])
+
+    def shifted(out, a, f):
+        v = vw(lambda: g.vector.tensor_scalar(ap(out), ap(a), ap(f), None, A.add), cnt(a) * (0.5 if two(out, a) else 1))
+        return op({"v": v, "a": actw(out, a, AF.Identity, f)}, [a, f], [out])
+
+    def test(out, a):
+        v = vw(lambda: g.vector.tensor_scalar(ap(out), ap(a), MAGIC, MAGIC, A.add, A.is_equal), cnt(a))
+        i = op({"v": v, "a": actw(out, a, AF.Abs)}, [a], [out])
+        ops[i]["tag"] = "T" + tag[0]
+        ops[ts(out, out, 0.5, A.is_lt)]["after"] = i
 
     def ind(win, off):
         return ap(win).indirect(ap(off))
 
-    def gather(out, win, off, key):
-        if ENG.get(key, "a") == "a":
-            return op("a", lambda: g.scalar.activation(ap(out), ind(win, off), AF.Copy), [win, off], [out], 65 + cnt(out) * GA * CY)
-        return op("v", lambda: g.vector.tensor_copy(ap(out), ind(win, off)), [win, off], [out], 50 + cnt(out) * GA * CY)
+    def gather(out, win, off):
+        return op({"a": (lambda: g.scalar.activation(ap(out), ind(win, off), AF.Copy), 65.0, 0, cnt(out), 0),
+                   "v": (lambda: g.vector.tensor_copy(ap(out), ind(win, off)), 50.0, 0, cnt(out), 0)}, [win, off], [out])
 
     def gtt(out, win, off, b, o):
-        return op("v", lambda: g.vector.tensor_tensor(ap(out), ind(win, off), ap(b), o), [win, off, b], [out], 50 + cnt(out) * GA * CY)
+        return op({"v": (lambda: g.vector.tensor_tensor(ap(out), ind(win, off), ap(b), o), 50.0, 0, cnt(out), 0)}, [win, off, b], [out])
 
-    def mm(items):
+    def mm(items, extra=()):
         def e():
             for o, l, r, s0, s1 in items:
                 ins = g.tensor.matmul(ap(o), ap(l), ap(r), s0, s1)
             return ins
-        return op("p", e, [x for it in items for x in it[1:3]], sorted({it[0] for it in items}), sum(max(64, cnt(it[2])) for it in items) * PC, 60)
+        return op({"p": (e, 0.0, sum(max(min(64, cnt(it[1])), cnt(it[2])) for it in items), 0, 0)}, [x for it in items for x in it[1:3]],
+                  sorted({it[0] for it in items}), 60, "c", extra)
 
     def acc(out, pairs):
         return [(out, l, r, i == 0, i == len(pairs) - 1) for i, (l, r) in enumerate(pairs)]
+
+    def group(items):
+        return [(o, l, r, i == 0, i == len(items) - 1) for i, (o, l, r) in enumerate(items)]
 
     def iota(out, pat, base=0, cm=0):
         def e():
             if SCRATCH[out[0]][2] == I32:
                 return g.iota(ap(out), pat, base, cm)
             return g.iota(ap(out), pat, base, cm, allow_small_or_imprecise_dtypes=True)
-        return op("g", e, [], [out], 130 + 2 * cnt(out) * CY)
+        return op({"g": (e, 130.0, 2 * cnt(out), 0, 0)}, [], [out])
 
     def dma(q, out, in_, nbytes, extra=()):
-        return op(q, lambda: Q[q].dma_start(ap(out), ap(in_)), [in_], [out] if isinstance(out, tuple) else [], 100, 1900 + nbytes / 180.0, "d", extra)
+        return op({q: (lambda: Q[q].dma_start(ap(out), ap(in_)), 100.0, 0, 0, 0)}, [in_], [out] if isinstance(out, tuple) else [], 1400 + nbytes / 250.0, "d", extra)
 
     def send(parts, extra=()):
         i = nrem[0]
@@ -175,107 +201,126 @@ def build(g, core, T, topo, rank):
                 m = sum(1 << x for x in topo.engines(core, peer)[per * j:per * j + per])
                 tr.append(RemoteDMATransfer(dst_ids=[DstId(rid=rid, pnc=pid)], dma_engine_mask=m, remote_sem=T.sem["r%d" % i], src=ap(src), dst=ap(dst)))
             return g.remote_dma_fused(tr, local_sem=T.sem["l%d" % i])
-        a = op("g", e, [p[1] for p in parts], [], 700, 1500 + 128 * 60.0 / per, "r", extra)
+        a = op({"g": (e, 700.0, 0, 0, 0)}, [p[1] for p in parts], [], 1200 + 128 * 45.0 / per, "r", extra)
         ops[a]["sem"] = ("l%d" % i, per * len(parts))
-        b = op(None, None, [], [p[2] for p in parts], 0, 300, "x", [a])
+        b = op({None: (None, 0.0, 0, 0, 0)}, [], [p[2] for p in parts], 300, "x", [a])
         ops[b]["sem"] = ("r%d" % i, per * len(parts))
         return b
 
-    def S(r, name="WS", k=0):
-        return R(name, 144 * k + 15 - r, 144 * k + 143 - r)
+    def S(r, name="WS", k=0, p1=128):
+        return R(name, 144 * k + 15 - r, 144 * k + 143 - r, p1=p1)
 
-    def wrap(src, c0, n, name="WS", byk=False):
+    def wrap(src, c0, n, name="WS", byk=False, more=(), p1=128):
         out = R(tile(), 0, n // 16)
-        mm(acc(out, [(S(r, name, r % 4 if byk else 0), R(src, c0 + r, c0 + n, 16)) for r in range(16)]))
+        mm(acc(out, list(more) + [(S(r, name, r % 4 if byk else 0, p1), R(src, c0 + r, c0 + n, 16, p1=p1)) for r in range(16)]))
         return out
 
-    for k in range(4):
-        dma("sa"[k % 2], R("DN", p0=32 * k, p1=32 * k + 32), T.nb[:, W * k:W * k + W], 131072)
-    dma("s", R("SN"), T.snd[:], 57344)
-    dma("s", R("XB", O1, O1 + V), T.xv[:], 589824)
+    dma("s", R("XL", p1=8), T.xv[0:128:16, :], 36864)
+    nb = dma("s", R("DN"), T.nb[:], 524288)
+    dma("a", R("SN"), T.snd[:], 57344)
+    ms(R("RO"), 1.0)
     for a in range(0, W, 1024):
-        ms(R("LB", a, a + 1024), 1.0)
-    cp(R("DH"), R("DN"))
-    for k in range(4):
-        dma("sa"[k % 2], R("LB", 0, W, p0=k, ps=16), R("DH", p0=32 * k, p1=32 * k + 32), 65536)
-    lo = tt(R("DL"), R("DN"), R("DH"), A.subtract)
-    for k in range(4):
-        dma("sa"[k % 2], R("LB", 0, W, p0=4 + k, ps=16), R("DL", p0=32 * k, p1=32 * k + 32), 65536)
-    dma("s", R("Q"), T.cq[:], 589824, [lo])
+        move(R("LB", a, a + 1024), R("RO"))
+    dma("s", R("XB", O1, O1 + V), T.xv[:], 589824, [nb])
+    for a in (0, 512):
+        cp(R("DH", a, a + 512), R("DN", a, a + 512))
+    dma("s", R("LB", 0, W, ps=4), R("DH"), 262144)
+    for a in range(0, 1024, 256):
+        lo = tt(R("DL", a, a + 256), R("DN", a, a + 256), R("DH", a, a + 256), A.subtract)
+    dma("s", R("LB", 0, W, p0=1, ps=4), R("DL"), 262144)
+    dma("s", R("Q", 0, V), T.cq[:], 589824, [lo])
 
     iota(R("pI", 0), [[0, 1]], 0, 1)
-    iota(R("IX"), [[1, 256]])
+    iota(R("IX"), [[1, 144]])
     iota(R("XP"), [[1, 128]], 0, -1)
     iota(R("DC"), [[4, 7], [0, 16]])
     iota(R("GX"), [[16, 8], [0, 16]])
-    iota(R("I32X"), [[32, 72]])
-    iota(R("SIi"), [[1, SL]])
-    iota(R("SW"), [[16, 48]])
-    iota(R("VW"), [[16, 144]])
+    iota(R("IS"), [[16, 144]])
+    for s0, s1 in SEEK:
+        iota(R("SI", s0, s1), [[1, s1 - s0]], 15 + s0)
+    iota(R("SW"), [[16, 48]], W)
+    iota(R("CA"), [[16, 144]], O1)
+    iota(R("CB"), [[16, 144]], -W)
+    iota(R("RA"), [[0, 128], [512, 4]])
+    iota(R("RB"), [[0, 128], [-1024, 4]], 512)
+    late = []
     for a in range(0, 36, 9):
-        iota(R("CT", 64 * a, 64 * a + 576), [[8, 9], [0, 64]], 8 * a)
-        iota(R("IB", 64 * a, 64 * a + 576), [[0, 9], [1, 64]])
-    dma("s", R("CT", 0, V, p0=9, ps=16), R("IB", p0=0, p1=8), 36864)
+        late.append(iota(R("CT", 64 * a, 64 * a + 576), [[8, 9], [0, 64]], 8 * a))
+        late.append(iota(R("IB", 64 * a, 64 * a + 576), [[0, 9], [1, 64]]))
+    dma("s", R("CT", 0, V, p0=3, ps=16), R("IB", p0=0, p1=8), 36864)
     ts(R("pI", 1), R("pI", 0), 15, A.bitwise_and)
     ts(R("pI", 2), R("pI", 0), 112, A.bitwise_and)
     ts(R("pI", 3), R("pI", 0), 3, A.bitwise_and)
     ts(R("pI", 4), R("pI", 0), 15, A.bitwise_and, 2, A.arith_shift_right)
     cp(R("pF", 0, 5), R("pI", 0, 5))
     pi, pg, pk, pm = R("pF", 1), R("pF", 2), R("pF", 3), R("pF", 4)
-    lt8, ge8, big, eq8, c0w, c8w, tk, tm = [R("pF", j) for j in range(5, 13)]
-    ts(lt8, pi, 8.0, A.is_lt)
-    ts(ge8, pi, 8.0, A.is_ge)
+    lnk, lyb, big, eq2, c0w, c8w, tk, tm, p16, t4, hi0 = [R("pF", j) for j in range(5, 16)]
+    x144 = R("IX")
+    ts(p16, R("pF", 0), 16.0, A.mult)
+    ts(R("WS8"), x144, -15.0, A.add, p16, A.is_equal)
+    ts(lnk, pk, 2.0, A.is_lt)
+    ts(hi0, pk, 0.0, A.is_equal, 2048.0, A.mult)
+    ts(lyb, pk, 2.0, A.is_ge, hi0, A.add)
     ts(big, pi, 9.0, A.is_ge, 4096.0, A.mult)
-    ts(eq8, pi, 8.0, A.is_equal)
-    ts(tk, pg, pk, A.add)
+    ts(eq2, pi, 2.0, A.is_equal)
+    ts(tk, pk, 4.0, A.mult, pg, A.add)
     ts(tm, pg, pm, A.add)
-    x144 = R("IX", 0, 144)
+    ts(t4, pm, 4.0, A.mult, pg, A.add)
     ts(R("WS"), x144, -15.0, A.add, pg, A.is_equal)
-    act(R("W6"), R("WS"), AF.Identity, scale=lt8)
+    scaled(R("W6"), R("WS"), lnk)
+    scaled(R("WZ"), R("WS"), 4096.0)
     ts(R("WH"), R("WS"), 0.0625, A.mult)
     ts(R("M4", 0, 4), R("IX", 0, 4), pk, A.is_equal)
-    ts(R("M4", 4, 8), R("IX", 0, 4), pk, A.is_equal, lt8, A.mult)
+    ts(R("M4", 4, 8), R("IX", 0, 4), pm, A.is_equal, lnk, A.mult)
     ts(R("M4", 8, 12), R("IX", 0, 4), pm, A.is_equal)
-    ts(R("W2"), x144, -12.0, A.add, tk, A.is_equal)
-    act(R("W2"), R("W2"), AF.Identity, scale=lt8)
     ts(R("W4", 0, 144), x144, -4.0, A.add, tk, A.is_equal)
-    ts(R("W5", 576, 720), x144, -12.0, A.add, tm, A.is_equal)
+    ts(R("W5b"), x144, -12.0, A.add, tm, A.is_equal)
+    scaled(R("W2"), R("W5b"), lnk)
+    ts(R("W7"), x144, -12.0, A.add, t4, A.is_equal)
+    scaled(R("W7"), R("W7"), lnk)
     for k in (3, 2, 1, 0):
-        act(R("W3", 144 * k, 144 * k + 144), R("WS"), AF.Identity, scale=R("M4", 4 + k))
-        act(R("W4", 144 * k, 144 * k + 144), R("W4", 0, 144), AF.Identity, scale=R("M4", 8 + k))
-        ts(R("W5", 144 * k, 144 * k + 144), R("W5", 576, 720), R("M4", k), A.mult)
+        scaled(R("W3", 144 * k, 144 * k + 144), R("WS"), R("M4", 4 + k))
+        scaled(R("W4", 144 * k, 144 * k + 144), R("W4", 0, 144), R("M4", 8 + k))
+        ts(R("W5", 144 * k, 144 * k + 144), R("W5b"), R("M4", k), A.mult)
     ts(R("BO"), R("GX"), pg, A.is_equal)
     ts(R("ID"), R("XP"), 0.0, A.is_equal)
+    ts(R("IDh"), R("XP"), 0.0, A.is_equal)
+    ts(R("NX"), R("XP"), 0.0, A.is_equal, -0.5 - 1.0 / 512, A.mult)
     ts(R("TB"), R("XP"), 0.0, A.is_lt, -1.0, A.mult)
     tt(R("TB"), R("TB"), R("BO"), A.mult)
-    for n, f in (("NI", -1.0), ("CI", 25.0 / 1024), ("CN", -25.0 / 1024), ("HI", 0.5)):
-        act(R(n), R("ID"), AF.Identity, scale=f)
-    for r, f in ((R("ON"), 1.0), (R("ZO"), 0.0), (R("HF"), -0.5), (R("K1"), 1024.0), (R("XB", LC1, LC1 + 16), -64.0), (R("XB", LC2, LC2 + 16), -64.0),
-                 (R("CT", W, W + 16), 512.0), (HB(0, 8), 0.0), (HB(8, 16), 0.0), (R("T28"), 0.0), (R("LB", W, W + SL), 0.0)):
-        ms(r, f)
-    ts(c0w, pi, 9.0, A.is_equal, lt8, A.add)
-    ts(c8w, pi, 10.0, A.is_equal, -1.0, A.mult)
-    ts(c8w, c8w, eq8, A.add, c0w, A.add)
-    ts(R("SE", 0, 8), R("BO", 0, 128, 16), c0w, A.mult)
-    ts(R("SE", 8, 16), R("BO", 0, 128, 16), c8w, A.mult)
-    cp(R("SI"), R("SIi"))
-    ts(R("SW"), R("SW"), pi, A.add)
-    ts(R("SW4"), R("SW"), float(W), A.add)
-    ts(R("VW"), R("VW"), pi, A.add)
-    ts(R("VB"), R("VW"), float(O1), A.add)
-    ts(R("VL", 0, 144), R("VW"), -1.0, A.mult, float(LC1 - O1), A.add)
-    ts(R("VL", 144, 288), R("VW"), -1.0, A.mult, float(LC2 - O2), A.add)
+    for n, f in (("NI", -1.0), ("CI", 25.0 / 1024), ("CN", -25.0 / 1024), ("HI", 0.5), ("NH", -0.5), ("I9", 9.0), ("I16", 16.0), ("DPI", pi),
+                 ("MB", -8192.0), ("PB", 8192.0)):
+        scaled(R(n), R("ID"), f)
+    for r, f in ((R("K1"), 1024.0), (R("XB", LC1, O1), -64.0), (R("T28"), 0.0), (R("C75"), 0.0), (R("C75", 0, 64, 2), -15.0 / 256),
+                 (R("RP"), 2.0 ** 29), (R("RP", 0, 6 * KM, 6), 0.0)):
+        ms(r, f, R("RO", 0, cnt(r)))
+    for r, f in [(R("ZO"), 0), (R("XB", LC2, Y2), -64), (R("CT", W, W + 16), 512), (R("LB", W, W + SL), 0), (R("Q", V, V + 16), -1024), (R("CZ"), -34816)] + \
+                [(R3("H", d, d + 2, 0, 256), 0) for d in range(0, 8, 2)] + [(R3("AB%d" % h, 0, s // 16, 64, 96), 0) for h, s in enumerate(SCS)]:
+        i = iota(r, [[0, cnt(r)]], f)
+        if cnt(r) > 128:
+            late.append(i)
+    late = late[5:]
+    iota(R("JP"), [[0, 6 * KM]], 2048)
+    ms(R("JP", 5, 6 * KM, 6), 4096.0, R("RO", 0, KM))
+    for h, s in enumerate(SCS):
+        ms(R("S0%d" % h, 0, 3 * s // 4, 3), -4096.0)
+    ts(c0w, pi, 3.0, A.is_equal, lnk, A.add)
+    ts(c8w, pi, 6.0, A.is_equal, -1.0, A.mult)
+    ts(c8w, c8w, eq2, A.add, c0w, A.add)
+    scaled(R("SE", 0, 16, 2), R("BO", 0, 128, 16), c0w)
+    scaled(R("SE", 1, 16, 2), R("BO", 0, 128, 16), c8w)
+    shifted(R("SW"), R("SW"), pi)
     ts(R("SN2"), R("SN"), W - 1, A.bitwise_and)
     cp(R("cU"), R("SN2"))
     ts(R("SN3"), R("SN"), 12, A.arith_shift_right)
     tt(R("SN3"), R("SN3"), R("DC"), A.add)
     cp(R("kU"), R("SN3"))
-    ts(R("sa", 0, 28), R("DC", 0, 112, 4), 8.0, A.mult, 32.0, A.add)
+    ts(R("sa", 0, 28), R("DC", 0, 112, 4), 4.0, A.mult, 16.0, A.add)
     for k in range(4):
-        ts(R("T28", k, 28, 4), R("sa", k, 28, 4), eq8, A.mult, R("M4", 4 + k), A.add)
+        ts(R("T28", k, 28, 4), R("sa", k, 28, 4), eq2, A.mult, R("M4", 4 + k), A.add)
     HALF = ((0, 4), (4, 7))
     for a, b in HALF:
-        gather(R("MK", GH * a, GH * b), R("T28"), R("kU", 16 * a, 16 * b), "mk%d" % a)
+        gather(R("MK", GH * a, GH * b), R("T28"), R("kU", 16 * a, 16 * b))
 
     def show_links(rd):
         tag[0] = "l%d" % rd
@@ -284,7 +329,7 @@ def build(g, core, T, topo, rank):
             ps = wrap("GS", GH * a, GH * (b - a), "W6")
             ts(R("sa", 16 * a, 16 * b), ps, float(V), A.is_ge, -float(W), A.mult)
             tt(R("sb", 16 * a, 16 * b), ps, R("sa", 16 * a, 16 * b), A.add)
-            ts(R("sU", 16 * a, 16 * b), R("sb", 16 * a, 16 * b), 16.0 if rd == 0 else float(NG), A.add)
+            ts(R("sU", 16 * a, 16 * b), R("sb", 16 * a, 16 * b), float(O1) if rd == 0 else float(NG), A.add)
 
     def show_cols(rd, extra):
         tag[0] = "w%d" % rd
@@ -292,7 +337,7 @@ def build(g, core, T, topo, rank):
         gl = G1 if rd == 0 else G2
         for a, b in HALF:
             for x, y in ((a, a + 2), (a + 2, b)):
-                gather(R("SB", GH * x, GH * y), win, R("sU", 16 * x, 16 * y), "sc%d%d" % (rd, x))
+                gather(R("SB", GH * x, GH * y), win, R("sU", 16 * x, 16 * y))
             send([(d + 1, R("SB", GH * d, GH * d + GH), R("XB", gl + GH * d, gl + GH * d + GH)) for d in range(a, b)])
         tag[0] = "t%d" % rd
         send([(d + 1, R("GS", GH * d, GH * d + GH), R("CT", V + GH * d, V + GH * d + GH)) for d in range(7)], extra)
@@ -301,15 +346,17 @@ def build(g, core, T, topo, rank):
         tag[0] = "s%d" % rd
         lw = R("LW", 144 * rd, 144 * rd + 144)
         if rd == 0:
-            ts(lw, wrap("XB", O1, V), 0.0, A.is_lt)
+            ts(lw, wrap("XL", 0, V, "WS8", p1=8), 0.0, A.is_lt)
         p, p2, p3 = tile(), tile(), tile()
         mm([(R(p, 0, 144), R("BO"), lw, True, True), (R(p, 144, 288), R("TB"), lw, True, True)])
-        op("v", lambda: g.vector.tensor_tensor_scan(ap(R("CC")), ap(R(p, 0, 144)), ap(R("K1")), 0.0, A.add, A.min), [R(p, 0, 144), R("K1")], [R("CC")], vc(144))
+        scan(R("CC"), R(p, 0, 144), R("K1"), 15.0, A.add, A.min)
         cp(R("CH"), R("CC"))
         tt(R("CW"), R(p, 144, 288), R("CC"), A.add)
-        mm(acc(R(p2, 16), [(S(r, "WH"), R("CH", 9 * r + 8)) for r in range(16)]) + acc(R(p2, 0, 16), [(S(r, "WH"), R("CH", r, 144, 9)) for r in range(9)]))
+        p4 = tile()
+        mm(acc(R(p2, 16), [(S(r, "WH"), R("CH", 9 * r + 8)) for r in range(16)]))
+        mm(acc(R(p4, 0, 16), [(S(r, "WH"), R("CH", r, 144, 9)) for r in range(9)]))
         cp(R("T2", 16), R(p2, 16))
-        ts(R("T2", 0, 16), R(p2, 0, 16), big, A.add)
+        shifted(R("T2", 0, 16), R(p4, 0, 16), big)
         for s0, s1 in SEEK:
             tag[0] = "k%d%d" % (rd, s0 // 128)
             kc = lambda n: R(n, s0 // 16, s1 // 16)
@@ -317,192 +364,188 @@ def build(g, core, T, topo, rank):
             ts(i1, si, R("T2", 16), A.is_ge)
             ps = wrap("IN1", s0, s1 - s0)
             ts(kc("kU1"), ps, 15.0, A.min)
-            ts(kc("b9"), ps, 15.0, A.min, 9.0, A.mult)
+            ts(kc("k1h"), ps, 15.0, A.min)
             gtt(i1, R("T2", 0, 16), kc("kU1"), si, A.is_le)
-            tt(kc("nf"), wrap("IN1", s0, s1 - s0), kc("b9"), A.add)
-            ts(kc("kU2"), kc("nf"), 143.0, A.min)
-            ts(kc("n16"), kc("nf"), 143.0, A.min, 16.0, A.mult)
+            ps = wrap("IN1", s0, s1 - s0, more=[(R("I9"), kc("k1h"))])
+            ts(kc("kU2"), ps, 143.0, A.min)
+            ts(kc("k2h"), ps, 143.0, A.min)
             gtt(i1, R("CW"), kc("kU2"), si, A.is_le)
-            tt(kc("vf"), wrap("IN1", s0, s1 - s0), kc("n16"), A.add)
-            ts(kc("vU"), kc("vf"), float(V - 1), A.min)
+            ps = wrap("IN1", s0, s1 - s0, more=[(R("I16"), kc("k2h"))])
+            cp(kc("vU"), ps)
+            ts(kc("vH"), ps, -2048.0, A.add)
+            move(kc("vF"), ps)
         tag[0] = "z%d" % rd
-        ts(R("vN"), R("vf"), float(V - 1), A.min, -float(W), A.add)
-        tt(R("vS"), R("vN"), R("SW"), A.subtract)
-        ts(R("TH"), R("SW"), R("CC", 143), A.is_ge, 4.0, A.add)
-        mm([(R(p3, 0, 144), R("ON"), lw, True, True)])
-        op("v", lambda: g.vector.tensor_reduce(ap(R("LM", 0)), ap(R(p3, 0, 144)), AX.X, A.add), [R(p3, 0, 144)], [R("LM", 0)], vc(144))
+        tt(R("vS"), R("vF"), R("SW"), A.subtract)
+        mm([(R(p3, 0, 144), R("RO", 0, 128), lw, True, True)])
+        op({"a": (lambda: g.scalar.activation(ap(R("LJ")), ap(R(p3, 0, 144)), AF.Identity, accum_out=ap(R("LM", 0))), 50.0, 144, 0, 0)},
+           [R(p3, 0, 144)], [R("LJ"), R("LM", 0)])
         cp(R("LI", 0), R("LM", 0))
         ts(R("LI", 1), R("LI", 0), 7, A.bitwise_and)
-        ts(R("LM", 1), R("LI", 1), 190.0, A.add)
-        ts(R("dl"), R("CW"), -1.0 - SL, A.add)
-        tt(R("dl"), R("dl"), lw, A.mult)
-        tt(R("dl"), R("dl"), R("VL", 144 * rd, 144 * rd + 144), A.add)
+        ts(R("LM", 1), R("LI", 1), 190.0, A.add, 4096.0, A.mult)
+        scaled(R("LMD"), R("ID"), R("LM", 1))
+        tt(R("TG"), R("CW"), lw, A.mult)
 
     def piece(rd, h, hb):
         s, SC, s0 = str(h), SCS[h], sum(SCS[:h])
         IC, KC, TC, key = SC // 4, SC // 16, SC // 128, "%d%d" % (rd, h)
-        xw = R("XB", O1, O2) if rd == 0 else R("XB", O2, Y2)
+        xw = R("XB", O1, O2) if rd == 0 else R("XB", O2, LC2)
         yb = (Y1 if rd == 0 else Y2) + s0
         kc = lambda n: R(n, s0 // 16, s0 // 16 + KC)
         ju = lambda j: R("JU" + s, IC * j, IC * j + IC)
         jh = lambda j: R("JH" + s, IC * j, IC * j + IC)
-        se = lambda j: R("se" + s, IC * j, IC * j + IC)
+        third = lambda n, j: R(n + s, j, 3 * IC, 3)
 
-        def visit(j, l):
+        def visit(j, l, name, more):
             m, i = "M%d" % j + s, "I%d" % j + s
             for t in range(TC):
-                gather(R(m, 512 * t, 512 * t + 512), xw, R("JU" + s, IC * l + 32 * t, IC * l + 32 * t + 32), "vi%d%d" % (j, t) + key)
+                if t % VIS[j] == 0:
+                    u = min(t + VIS[j], TC)
+                    gather(R(m, 512 * t, 512 * u), xw, R("JU" + s, IC * l + 32 * t, IC * l + 32 * u))
                 p = tile()
                 mm([it for k in range(4) for it in acc(R(p, k, 512, 4), [(R("CI"), R(m, 512 * t + k, 512 * t + 512, 4)), (R("CN"), R("QS", s0 + 128 * t, s0 + 128 * t + 128))])])
                 o = R(i, 512 * t, 512 * t + 512)
-                if ENG.get("te%d%d" % (j, t) + key, "v") == "v":
-                    ts(o, R(p), MAGIC, A.add, MAGIC, A.is_equal)
-                else:
-                    act(o, R(p), AF.Abs)
-                    ts(o, o, 0.5, A.is_lt)
-            return wrap(i, 0, 4 * SC)
+                test(o, R(p))
+            return wrap(i, 0, 4 * SC, name, more=more)
 
-        tag[0] = "a" + key
-        gather(R("GV", s0, s0 + SC), R("LB", 0, V), kc("vU"), "gv" + key)
-        gather(R("QS", s0, s0 + SC), R("Q"), kc("vU"), "qs" + key)
+        tag[0] = "g" + key
+        first = [gather(R("GV", s0, s0 + SC), R("LB", 0, W), kc("vU"))]
+        gather(R("QS", s0, s0 + SC), R("Q"), kc("vU"))
         ps = R(tile(), 0, IC)
         mm(acc(ps, [(R("W2", 12 - 4 * m, 140 - 4 * m), R("GV", s0 + m, s0 + SC, 4)) for m in range(4)]))
         for j in range(3):
             if j:
-                gather(R("GL%d" % j + s), R("LB", 0, W), ju(j - 1), "ch%d" % j + key)
+                tag[0] = "a%d" % j + key
+                for t in range(0, TC, CHN):
+                    u = min(t + CHN, TC)
+                    gather(R("GL%d" % j + s, 512 * t, 512 * u), R("LB", 0, W), R("JU" + s, IC * (j - 1) + 32 * t, IC * (j - 1) + 32 * u))
                 ps = wrap("GL%d" % j + s, 0, 4 * SC, "W3", True)
             if j < 2:
                 cp(ju(j), ps)
-            ts(jh(j), ps, -2048.0, A.add)
+            ts(jh(j) if j < 2 else third("S1", 0), ps, -2048.0, A.add)
         for j in range(2):
             tag[0] = "b%d" % j + key
-            ps = visit(j, j)
-            ts(se(2 * j), ps, 9.0, A.is_ge)
-            ts(se(2 * j + 1), ps, 9.0, A.is_lt)
-            tt(se(4 + j), se(2 * j), jh(j), A.mult)
-        tt(se(6), se(3), jh(2), A.mult)
-        tt(se(6), se(6), se(5), A.add)
-        tt(se(6), se(6), se(1), A.mult)
-        tt(jh(3), se(6), se(4), A.add)
-        ts(ju(3), jh(3), 2048.0, A.add)
+            ps = visit(j, j, "WZ", [(R("ID"), R("CZ", 0, IC))])
+            ts(third("S0", 2 - j), ps, -1.0, A.mult)
+            tt(third("S1", 2 - j), ps, jh(j), A.min)
+        scan(R("SJ" + s), R("S0" + s), R("S1" + s), 0.0, A.min, A.max)
+        ts(ju(3), third("SJ", 2), 2048.0, A.add)
         tag[0] = "c" + key
-        ts(se(7), visit(2, 3), 9.0, A.is_ge)
-        pf, pj = R(tile(), 0, KC), tile()
-        mm(acc(pf, [(R("W5", 588 - 4 * t, 716 - 4 * t), R("se" + s, 7 * IC + t, 8 * IC, 4)) for t in range(4)]))
-        mm([it for b, k in enumerate(PERM) for it in
-            acc(R(pj, KC * b, KC * b + KC), [(R("W5", 144 * k + 12 - 4 * t, 144 * k + 140 - 4 * t), R("JH" + s, 3 * IC + t, 4 * IC, 4)) for t in range(4)])])
-        ts(R("JK" + s), R(pj, 0, 4 * KC), -2048.0, A.add)
-        vt = lambda a, n=1: R("vt" + s, KC * a, KC * (a + n))
-        jk = lambda a, n=1: R("JK" + s, KC * a, KC * (a + n))
-        tt(vt(8), pf, kc("TH"), A.is_ge)
-        tt(vt(0, 2), jk(0, 2), jk(2, 2), A.subtract)
+        ts(R("ub" + s), visit(2, 3, "WS", []), 9.0, A.is_lt, 2.0 ** 26, A.mult)
+        pj, pe = tile(), tile()
+        mm(group([(R(pj, 0, 6 * KC), R("ID"), R("JP", 0, 6 * KC)), (R(pj, 4, 6 * KC, 6), R("IDh"), kc("vH"))] +
+                 [(R(pj, 3 - k, 6 * KC, 6), R("W5", 144 * k + 12 - 4 * t, 144 * k + 140 - 4 * t), R("SJ" + s, 2 + 3 * t, 3 * IC, 12)) for k in range(4) for t in range(4)]))
         tag[0] = "f" + key
         m2 = "M2" + s
-        tt(R("LO" + s), R(m2, 0, 4 * SC, 2), R(m2, 1, 4 * SC, 2), A.min)
-        tt(R("HX" + s), R(m2, 0, 4 * SC, 2), R(m2, 1, 4 * SC, 2), A.max)
-        tt(R("MD" + s, 0, SC), R("LO" + s, 0, 2 * SC, 2), R("LO" + s, 1, 2 * SC, 2), A.max)
-        tt(R("MD" + s, SC, 2 * SC), R("HX" + s, 0, 2 * SC, 2), R("HX" + s, 1, 2 * SC, 2), A.min)
+        for t in range(TC):
+            c = (512 * t, 512 * t + 512)
+            scan(R("MX" + s, *c), R("RA"), R(m2, *c), 0.0, A.min, A.max)
+            scan(R("MN" + s, *c), R("RB"), R(m2, *c), 0.0, A.max, A.min)
         ps = R(tile(), 0, SC)
-        mm(acc(ps, [(R("HI"), R("MD" + s, 0, SC)), (R("HI"), R("MD" + s, SC, 2 * SC)), (R("HI"), R("HF", 0, SC))]))
+        mm(acc(ps, [(R("HI"), R(m2, k, 4 * SC, 4)) for k in range(4)] + [(R(w), R(n + s, 3, 4 * SC, 4)) for w, n in (("NX", "MX"), ("NH", "MN"))]))
         y = R("XB", yb, yb + SC)
         ts(y, ps, MAGIC, A.add, MAGIC, A.subtract)
         nk = 512 // SC
         for b in range(0, 4, nk):
             p = tile()
-            mm([it for x in range(nk) for it in acc(R(p, SC * x, SC * x + SC), [(R("ID"), R(m2, PERM[b + x], 4 * SC, 4)), (R("NI"), y)])])
-            act(R("AB" + s, SC * b, SC * (b + nk)), R(p, 0, SC * nk), AF.Abs)
-        pd = wrap("AB" + s, 0, 4 * SC)[0]
+            mm([it for x in range(nk) for it in acc(R(p, SC * x, SC * x + SC), [(R("ID"), R(m2, b + x, 4 * SC, 4)), (R("NI"), y)])])
+            for x in range(nk):
+                act(R3("AB" + s, 0, KC, 16 * (3 - b - x), 16 * (4 - b - x)), R(p, SC * x, SC * x + SC), AF.Abs)
+        e = R(pe, 0, 6 * KC)
+        mm(group([(e, S(r, "WZ"), R3("AB" + s, 0, KC, r, 96, 16)) for r in range(16)] + [(R(pe, 4, 6 * KC, 6), R("LMD"), R("RO", 0, KC))] +
+                 [(R(pe, 5, 6 * KC, 6), R("W5b", 12 - 4 * t, 140 - 4 * t), R("ub" + s, t, IC, 4)) for t in range(4)]))
         tag[0] = "v" + key
-        cp(vt(2, 2), R(pd, 2 * KC, 4 * KC))
-        tt(vt(4, 2), R(pd, 0, 2 * KC), vt(2, 2), A.is_ge)
-        tt(vt(6, 2), R(pd, 0, 2 * KC), vt(2, 2), A.max)
-        tt(vt(0, 2), vt(0, 2), vt(4, 2), A.mult)
-        tt(vt(9), vt(6), vt(7), A.is_ge)
-        tt(vt(10), vt(6), vt(7), A.max)
-        tt(vt(0, 2), vt(0, 2), jk(2, 2), A.add)
-        ts(vt(10), vt(10), R("LM", 1), A.is_le)
-        tt(vt(11), vt(0), vt(1), A.subtract)
-        tt(vt(12), vt(8), vt(10), A.mult)
-        tt(vt(11), vt(11), vt(9), A.mult)
-        tt(vt(13), vt(8), vt(12), A.subtract)
-        tt(vt(11), vt(11), vt(1), A.add)
-        tt(vt(14), vt(12), kc("vN"), A.mult)
-        tt(vt(11), vt(11), vt(13), A.mult)
-        tt(vt(11), vt(11), vt(14), A.add)
-        ts(R("cI" + s), vt(11), float(W), A.add)
-        gather(R("CG" + s), R("CT"), R("cI" + s), "cg" + key)
-        p = tile()
-        mm([(R(p, 8 * (TC * j + t), 8 * (TC * j + t) + 8), R("CG" + s, 128 * t, 128 * t + 128), R("SE", 8 * j, 8 * j + 8), True, True)
-            for j in range(2) for t in range(TC)])
-        hc = lambda a: R("hc" + s, 8 * TC * a, 8 * TC * (a + 1))
-        ts(hc(0), R(p, 0, 8 * TC), -15.5, A.add, MAGIC * 32, A.add)
-        ts(hc(1), hc(0), MAGIC * 32, A.subtract)
-        tt(hc(2), R(p, 8 * TC, 16 * TC), hc(1), A.subtract)
+        sel = R("SEL", 6 * s0 // 16, 6 * (s0 + SC) // 16)
+        scan(R("RM" + s), R("RP", 0, 6 * KC), e, 0.0, A.min, A.max)
+        tt(R("tb" + s), R("RM" + s), e, A.subtract)
+        tt(R("lo" + s), R(pj, 0, 6 * KC), R("tb" + s), A.subtract)
+        scan(sel, R("tb" + s), R("lo" + s), 0.0, A.min, A.max)
+        cp(R("cI" + s), R("SEL", 6 * s0 // 16 + 5, 6 * (s0 + SC) // 16, 6))
+        gather(R("CG" + s), R("CT"), R("cI" + s))
+        p, n8 = tile(), 8 * TC
+        mm(group([(R(p, 0, 2 * n8), R("RO", 0, 128), R("C75", 0, 2 * n8))] +
+                 [(R(p, 16 * t, 16 * t + 16), R("CG" + s, 128 * t, 128 * t + 128), R("SE", 0, 16)) for t in range(TC)]))
+        hc, low = lambda a: R("hc" + s, n8 * a, n8 * a + n8), R(p, 0, 2 * n8, 2)
+        ts(hc(0), low, MAGIC * 16, A.add, MAGIC * 16, A.subtract)
+        ts(hc(2), low, V / 2 - 8.0, A.is_ge, V / 2, A.mult)
+        ts(hc(3), low, V / 2 - 8.0, A.is_ge, 1.0 / 2048, A.add)
+        cp(hc(1), R(p, 1, 2 * n8, 2))
+        tt(hc(2), hc(0), hc(2), A.subtract)
+        if h == 0:
+            tag[0] = "o%d" % rd
+            for bk in hb:
+                mm([(R(bk, p1=72), R("ZO"), R("RO", 0, 512), True, False)], [first[0]])
         tag[0] = "h" + key
         for gg in range(8):
-            bk, by_act = hb[gg // 2], ENG.get("oa%d" % gg + key, "v") == "a"
-            it = [(R(bk, p1=72), R("ZO"), R("IB", 0, 512), True, False)] if h == 0 and gg % 2 == 0 else []
+            bk, c0 = hb[gg // 4], 128 * (gg % 4)
+            it = []
             for t in range(TC):
                 j = 6 * gg + s0 // 128 + t
-                if by_act:
-                    act(R("OA", 72 * j, 72 * j + 72), R("I32X"), AF.Abs, bias=R("hc" + s, 8 * TC + 8 * t + gg), scale=-1.0)
-                else:
-                    ts(R("OA", 72 * j, 72 * j + 72), R("I32X"), R("hc" + s, 8 * TC + 8 * t + gg), A.is_equal)
-                ts(R("OB", 256 * j, 256 * j + 256), R("IX"), R("hc" + s, 16 * TC + 8 * t + gg), A.is_equal)
-                it.append((R(bk, 256 * (gg % 2), 256 * (gg % 2) + 256, p1=72), R("OA", 72 * j, 72 * j + 72), R("OB", 256 * j, 256 * j + 256),
-                           False, h == NCH - 1 and gg % 2 == 1 and t == TC - 1))
-            if by_act:
-                oa = R("OA", 72 * (j + 1 - TC), 72 * j + 72)
-                act(oa, oa, AF.Relu, bias=R("K1", 0), scale=-1024.0)
+                col = lambda a: R("hc" + s, n8 * a + 8 * t + gg)
+                ts(R("OB", 128 * j, 128 * j + 128), R("IX", 0, 128), col(0), A.add, col(1), A.is_equal)
+                ts(R("OA", 72 * j, 72 * j + 72), R("IS", 0, 72), col(2), A.is_equal, col(3), A.mult)
+                it.append((R(bk, c0, c0 + 128, p1=72), R("OA", 72 * j, 72 * j + 72), R("OB", 128 * j, 128 * j + 128), False, h == NCH - 1 and gg % 4 == 3 and t == TC - 1))
             mm(it)
         tag[0] = "d" + key
-        tt(vt(15), vt(12), kc("vS"), A.mult)
-        tt(vt(15), vt(15), kc("SW4"), A.add)
-        cp(kc("lU"), vt(15))
-        ts(R("jf" + s), jh(3), 2048.0, A.add)
-        move(R("jh" + s, 0, IC), R("jf" + s), "jh" + key)
-        tt(R("jh" + s, IC, 2 * IC), R("jf" + s), R("jh" + s, 0, IC), A.subtract)
+        j3, hi, lo = third("SJ", 2), R("jh" + s, 0, IC), R("jh" + s, IC, 2 * IC)
+        ts(hi, j3, MAGIC * 64, A.add, MAGIC * 64, A.subtract)
+        tt(lo, j3, hi, A.subtract)
         p = tile()
-        mm([it for m in range(4) for it in
-            acc(R(p, m, SC, 4), [(R("W4", 144 * m + 4, 144 * m + 132), R("jh" + s, 0, IC)), (R("W4", 144 * m, 144 * m + 128), R("jh" + s, IC, 2 * IC))])])
-        act(R("LY", s0, s0 + SC), R(p, 0, SC), AF.Identity, bias=ge8)
+        mm([it for m in range(4) for it in acc(R(p, m, SC, 4), [(R("W4", 144 * m + 4, 144 * m + 132), hi), (R("W4", 144 * m + 3, 144 * m + 131), lo)])])
+        shifted(R("LY", s0, s0 + SC), R(p, 0, SC), lyb)
 
-    def relink(s0, s1):
-        ly, lu = R("LY", s0, s1), R("lU", s0 // 16, s1 // 16)
-        op("v", lambda: g.vector.tensor_copy(ind(R("LB"), lu), ap(ly)), [ly, lu], [R("LB")], 50 + (s1 - s0) * SCA * CY)
+    def relink(rd, s0, s1):
+        tag[0] = "e%d%d" % (rd, s0 // 128)
+        kc = lambda n: R(n, s0 // 16, s1 // 16)
+        tt(kc("rs"), R("SEL", 6 * s0 // 16 + 5, 6 * s1 // 16, 6), kc("vF"), A.is_equal)
+        tt(kc("rs"), kc("rs"), kc("vS"), A.mult)
+        tt(kc("rs"), kc("rs"), kc("SW"), A.add)
+        cp(kc("lU"), kc("rs"))
+        for a in range(s0, s1, 256):
+            b = min(a + 256, s1)
+            ly, lu = R("LY", a, b), R("lU", a // 16, b // 16)
+            op({"v": (lambda ly=ly, lu=lu: g.vector.tensor_copy(ind(R("LB"), lu), ap(ly)), 50.0, 0, 0, b - a)}, [ly, lu], [R("LB")])
 
     def marks(rd, hb):
         tag[0] = "m%d" % rd
-        for gg in range(8):
-            move(HB(0, 16, 16 * gg, 16 * gg + 16, 72), R(hb[gg // 2], 256 * (gg % 2), 256 * (gg % 2) + 256, p1=72), "ev%d%d" % (rd, gg))
+        for b, bk in enumerate(hb):
+            hr = R("HR", 512 * b, 512 * b + 512, p1=72)
+            if b == 0:
+                act(hr, R(bk, p1=72), AF.Identity, MAGIC)
+                act(hr, hr, AF.Identity, -MAGIC)
+            else:
+                ts(hr, R(bk, p1=72), MAGIC, A.add, MAGIC, A.subtract)
+            for x in range(4):
+                gg, whole = 4 * b + x, R("HR", 512 * b + 128 * x, 512 * b + 128 * x + 128, p1=72)
+                tt(R3("H", 0, 8, 16 * gg, 16 * gg + 16, p1=72), R(bk, 128 * x, 128 * x + 128, p1=72), whole, A.not_equal)
+                move(R3("H", 0, 8, 128 + 16 * gg, 144 + 16 * gg, p1=72), whole)
         f0 = NG * rd
-        arr = send([(N - d, HB(2 * d, 2 * d + 2), R("FL", f0 + GH * (d - 1), f0 + GH * d)) for d in range(1, N)])
-        tag[0] = "e%d" % rd
-        for s0 in range(0, SL, 256):
-            relink(s0, s0 + 256)
+        arr = send([(N - d, R3("H", d, d + 1, 0, 256), R("FL", f0 + GH * (d - 1), f0 + GH * d)) for d in range(1, N)])
+        for s0, s1 in LINK:
+            relink(rd, s0, s1)
         if rd == 0:
             show_links(1)
         else:
+            tag[0] = "n1"
             for hh in range(2):
                 ps = R(tile(), 0, 288)
-                mm(acc(ps, [(R("W2", 12 - 4 * m, 140 - 4 * m), R("LB", 576 * m + 288 * hh, 576 * m + 288 * hh + 288)) for m in range(4)]))
-                act(R("YN", 288 * hh, 288 * hh + 288), ps, AF.Identity)
-            for k in range(4):
-                dma("s", T.yn[:, V * k:V * k + V], R("YN", p0=k, ps=4), 73728)
+                mm(acc(ps, [(R("W7", 12 - m, 140 - m), R("LB", 576 * m + 288 * hh, 576 * m + 288 * hh + 288)) for m in range(4)]))
+                move(R("YN", 288 * hh, 288 * hh + 288), ps)
+            dma("s", T.yn[:], R("YN"), 294912)
         tag[0] = "u%d" % rd
         p = tile()
-        mm([it for b in range(2) for it in acc(R(p, b, 144, 2), [(HB(b, b + 1, p1=72), R("ID", 0, 72, p1=72))] +
-            [(R("FL", f0 + 128 * j, f0 + 128 * j + 128, p1=72), R("ID", 0, 72, p1=72)) for j in range(b, 14, 2)])])
-        ts(R("fl"), R(p, 0, 144), 0.0, A.is_gt)
-        tt(R("ix"), R("fl"), R("dl"), A.mult)
+        own, far = R(p, 0, 144), R("MB" if rd == 0 else "PB", 0, 72, p1=72)
+        mm(group([(own, R("ID"), R("CA" if rd == 0 else "CB")), (own, R("DPI"), R("RO", 0, 144))] +
+                 [(R(p, 72 * b, 72 * b + 72), src, far) for b in range(2) for src in
+                  [R3("H", 0, 1, 128 * b, 128 * b + 128, p1=72)] + [R("FL", f0 + GH * j + 128 * b, f0 + GH * j + 128 * b + 128, p1=72) for j in range(7)]]))
         if rd == 0:
+            ts(R("fl"), own, 0.0, A.is_lt)
             tt(R("LW", 144, 288), R("fl"), R("LW", 0, 144), A.not_equal)
-        tt(R("ix"), R("ix"), R("VB" if rd == 0 else "VW"), A.add)
-        cp(R("xU"), R("ix"))
-        win = R("XB", Y1, G1) if rd == 0 else R("XB", O2, XW)
+        tt(R("ix"), own, R("TG"), A.max if rd == 0 else A.min)
+        ts(R("xU"), R("ix"), 0.0 if rd == 0 else float(W), A.add)
+        win = R("XB", LC1, G1) if rd == 0 else R("XB", O2, XW)
         for a in range(0, 144, 36):
             o = R("XB", O2 + 16 * a, O2 + 16 * a + 576) if rd == 0 else R("FX", 16 * a, 16 * a + 576)
-            gather(o, win, R("xU", a, a + 36), "up%d%d" % (rd, a // 36))
+            gather(o, win, R("xU", a, a + 36))
             if rd == 1:
                 dma("s", T.yx[:, 16 * a:16 * a + 576], o, 147456)
         return arr
@@ -512,20 +555,26 @@ def build(g, core, T, topo, rank):
     for rd in range(2):
         show_cols(rd, extra)
         seekers(rd)
-        hb = [tile() for _ in range(4)]
+        hb = [tile() for _ in range(2)]
         for h in range(NCH):
             piece(rd, h, hb)
         extra = [marks(rd, hb)]
+    at = {}
+    for i, o in enumerate(ops):
+        at.setdefault(o["tag"], []).append(i)
+    for i in late:
+        ops[i]["extra"].append([j for j in at["w0"] if ops[j]["kind"] == "r"][-1])
+    for a, b in EDGES:
+        for rd in "01":
+            ops[at[b[:-1] + rd + b[-1]][0]]["extra"].append(at[a[:-1] + rd + a[-1]][0])
     return ops, Q
 
 
 def span(r):
     if r[0][0] == "P":
-        return r[0], 0, 512, -1
+        return r[0], 0, 512, -1, 0, 1
     m = sum(1 << p for p in range(r[4], r[5], r[6]))
-    if r[0] == "H":
-        return "H", 128 * r[1] + r[7], 128 * (r[2] - 1) + r[8], m
-    return r[0], r[1], r[2], m
+    return (r[0], r[1], r[2], m) + (r[7:9] if len(r) == 9 else (0, 1))
 
 
 def hazards(ops):
@@ -534,105 +583,122 @@ def hazards(ops):
         deps = set(o["extra"])
         acc = [(span(r), False) for r in o["r"]] + [(span(r), True) for r in o["w"]]
         for sp, wr in acc:
-            for j, lo, hi, m, w2 in seen.get(sp[0], []):
-                if lo < sp[2] and sp[1] < hi and (m & sp[3]) and (wr or w2 or (sp[3] == -1 and ops[j]["eng"] != o["eng"])):
-                    if not (sp[0] == "H" and wr and w2 and ops[j]["tag"] == o["tag"]):
+            for j, x, w2 in seen.get(sp[0], []):
+                if x[1] < sp[2] and sp[1] < x[2] and (x[3] & sp[3]) and x[4] < sp[5] and sp[4] < x[5]:
+                    same = len(o["ways"]) == 1 and ops[j]["ways"].keys() == o["ways"].keys()
+                    if wr or w2 or (sp[3] == -1 and not same):
                         deps.add(j)
         for sp, wr in acc:
             lst = seen.setdefault(sp[0], [])
-            if wr and sp[0] != "H":
-                lst[:] = [x for x in lst if not (sp[1] <= x[1] and x[2] <= sp[2] and (x[3] & ~sp[3]) == 0)]
-            lst.append((i, sp[1], sp[2], sp[3], wr))
+            if wr:
+                lst[:] = [y for y in lst if not (sp[1] <= y[1][1] and y[1][2] <= sp[2] and (y[1][3] & ~sp[3]) == 0 and sp[4] <= y[1][4] and y[1][5] <= sp[5])]
+            lst.append((i, sp, wr))
         deps.discard(i)
         o["deps"] = o["base"] = sorted(deps)
 
 
-def place(ops, before, key, fwd):
+def back(ops, key, eng):
     n = len(ops)
-    after = [[] for _ in ops]
-    left = [len(b) for b in before]
-    for i, b in enumerate(before):
-        for j in b:
-            after[j].append(i)
-    est, st, used = [0.0] * n, [0.0] * n, {e: [] for e in "vapgs"}
+    left = [0] * n
+    for o in ops:
+        for j in o["base"]:
+            left[j] += 1
+    est, out, used = [0.0] * n, [0.0] * n, {e: [] for e in "vapgs"}
     ready = [i for i in range(n) if left[i] == 0]
     while ready:
         i = min(ready, key=key.get)
         ready.remove(i)
-        o, t = ops[i], est[i]
-        if o["eng"]:
-            u = used[o["eng"]]
+        e = eng[i]
+        t, busy = est[i] + ops[i]["lat"], ops[i]["busy"][e]
+        if e:
+            u = used[e]
             k = len(u)
             while k and u[k - 1][1] > t:
                 k -= 1
-            while k < len(u) and u[k][0] < t + o["busy"]:
+            while k < len(u) and u[k][0] < t + busy:
                 t = u[k][1]
                 k += 1
-            u.insert(k, (t, t + o["busy"]))
-        st[i] = t
-        for j in after[i]:
-            est[j] = max(est[j], t + o["busy"] + (o if fwd else ops[j])["lat"] + (0.0 if o["eng"] == "p" == ops[j]["eng"] else SYNC))
+            u.insert(k, (t, t + busy))
+        out[i] = t + busy
+        for j in ops[i]["base"]:
+            est[j] = max(est[j], out[i] + (0.0 if e == "p" == eng[j] or (e is None and "after" in ops[i]) else SYNC))
             left[j] -= 1
             if left[j] == 0:
                 ready.append(j)
-    return st
+    return out
 
 
-def passes(ops, key):
+def forth(ops, urge, eng):
     n = len(ops)
-    fwd = [o["deps"] for o in ops]
-    bwd = [[] for _ in ops]
+    after, left, users, opens = [[] for _ in ops], [len(o["base"]) for o in ops], {}, [None] * n
     for i, o in enumerate(ops):
-        for j in o["deps"]:
-            bwd[j].append(i)
-    best = None
-    for _ in range(PASSES):
-        if key is None:
-            back = place([dict(o, eng=None) for o in ops], bwd, {i: -i for i in range(n)}, False)
-            key = {i: -back[i] - ops[i]["busy"] - BIAS.get(ops[i]["tag"], 0.0) for i in range(n)}
-        st = place(ops, fwd, key, True)
-        end = max(st[i] + ops[i]["busy"] + ops[i]["lat"] for i in range(n))
-        if best is None or end < best[0]:
-            best = (end, st)
-        back = place(ops, bwd, {i: -st[i] - ops[i]["busy"] - ops[i]["lat"] for i in range(n)}, False)
-        key = {i: -back[i] - ops[i]["busy"] for i in range(n)}
-    return best[1]
-
-
-def plan(ops):
-    n = len(ops)
-    for o in ops:
-        o["deps"] = o["base"]
-    st = passes(ops, None)
-    users = {}
-    for i, o in enumerate(ops):
+        for j in o["base"]:
+            after[j].append(i)
         for r in o["r"] + o["w"]:
             if r[0][0] == "P" and i not in users.setdefault(r[0], []):
                 users[r[0]].append(i)
-    last = [[] for _ in range(8)]
-    bank = {}
+    for t, u in users.items():
+        opens[u[0]] = t
+    fin, deps, order, bank = [None] * n, [list(o["base"]) for o in ops], [], {}
+    free, held = {e: 0.0 for e in ("v", "a", "p", "g", "s", None)}, [[] for _ in range(8)]
+    est = [0.0] * n
+    ready = [i for i in range(n) if left[i] == 0]
+    while ready:
+        idle = min([(max([fin[j] + SYNC for j in u] + [0.0]), b) for b, u in enumerate(held) if all(fin[j] is not None for j in u)] or [(None, None)])
+        can = []
+        for i in ready:
+            if not opens[i] or idle[0] is not None:
+                can.append((max(est[i], free[eng[i]], idle[0] if opens[i] else 0.0), i))
+        t0, e0 = min(can)[0], eng[min(can)[1]]
+        _, t, i = max((urge[i] - LATE * (t - t0), t, i) for t, i in can if eng[i] == e0 and t <= t0 + SLACK)
+        ready.remove(i)
+        if opens[i]:
+            deps[i] += held[idle[1]]
+            held[idle[1]] = users[opens[i]]
+            bank[opens[i]] = "P%d" % idle[1]
+        if e0:
+            free[e0] = t + ops[i]["busy"][e0]
+        fin[i] = t + ops[i]["busy"][e0] + ops[i]["lat"]
+        order.append(i)
+        for j in after[i]:
+            est[j] = max(est[j], fin[i] + (0.0 if e0 == "p" == eng[j] or (e0 is None and "after" in ops[i]) else SYNC))
+            left[j] -= 1
+            if left[j] == 0:
+                ready.append(j)
+    return order, bank, deps
 
-    def reaches(a, bs):
-        todo, seen = list(bs), set(bs)
-        while todo:
-            x = todo.pop()
-            if x == a:
-                return True
-            for j in ops[x]["deps"]:
-                if j not in seen:
-                    seen.add(j)
-                    todo.append(j)
-        return False
-    for t in sorted(users, key=lambda t: st[users[t][0]]):
-        f = users[t][0]
-        for b in sorted(range(8), key=lambda b: max([st[j] for j in last[b]] + [-1.0])):
-            if not reaches(f, last[b]):
-                break
-        ops[f]["deps"] = sorted(set(ops[f]["deps"]) | set(last[b]))
-        last[b] = users[t]
-        bank[t] = "P%d" % b
-    st = passes(ops, {i: st[i] for i in range(n)})
-    return [(i, st[i], st[i] + ops[i]["busy"] + ops[i]["lat"]) for i in sorted(range(n), key=lambda i: (st[i], i))], bank
+
+def stage(tag):
+    if tag == "c":
+        return tag, 0
+    return (tag[0], int(tag[1])) if len(tag) == 2 else (tag[:-2] + tag[-1], int(tag[-2]))
+
+
+def when(tag):
+    s, rd = stage(tag)
+    return TIME.get(s, TIME[s.strip("T")]) + 60 * rd
+
+
+def engines(ops):
+    eng, seen = [], {}
+    for o in ops:
+        if len(o["ways"]) == 2:
+            k = seen[o["tag"]] = seen.get(o["tag"], -1) + 1
+            eng.append("v" if VEE.get(o["tag"], VEE.get(stage(o["tag"])[0], 0)) >> k & 1 else "a")
+        elif "after" in o and eng[o["after"]] == "v":
+            eng.append(None)
+            o["busy"][None] = 0.0
+        else:
+            eng.append(next(iter(o["ways"])))
+    return eng
+
+
+def plan(ops):
+    eng = engines(ops)
+    order, bank, deps = forth(ops, back(ops, {i: -(when(o["tag"]) + i * 1e-3) for i, o in enumerate(ops)}, eng), eng)
+    for o, d in zip(ops, deps):
+        o["deps"] = sorted({ops[j]["after"] if eng[j] is None and "after" in ops[j] else j for j in d})
+    return order, eng, bank
 
 
 def rank_program(g, core, T, topo):
@@ -642,35 +708,35 @@ def rank_program(g, core, T, topo):
     ops, Q = build(g, core, T, topo, rank)
     if "order" not in PLAN:
         hazards(ops)
-        PLAN["order"], PLAN["bank"] = plan(ops)
-        order = [x[0] for x in PLAN["order"]]
-        pos = {i: k for k, i in enumerate(order)}
+        PLAN["order"], PLAN["eng"], PLAN["bank"] = plan(ops)
+        pos = {i: k for k, i in enumerate(PLAN["order"])}
+        eng = PLAN["eng"]
         need = PLAN["need"] = []
-        for o in ops:
+        for i, o in enumerate(ops):
             last = {}
             for j in o["deps"]:
-                p = ops[j]
-                if o["kind"] == "x" or (p["eng"] == "p" and o["eng"] == "p"):
+                if eng[i] is None or eng[j] == "p" == eng[i]:
                     continue
-                k = p["eng"] if p["kind"] == "c" else j
+                k = eng[j] if ops[j]["kind"] == "c" else j
                 if k not in last or pos[j] > pos[last[k]]:
                     last[k] = j
             need.append(sorted(last.values()))
     need = PLAN["need"]
     wanted = {j for x in need for j in x}
     count, done, waited, nd = {e: 0 for e in Q}, {}, {e: {} for e in Q}, 0
-    for i, _s, _f in PLAN["order"]:
-        o = ops[i]
-        e = o["eng"]
+    for i in PLAN["order"]:
+        o, e = ops[i], PLAN["eng"][i]
         if o["kind"] == "x":
             done[i] = o["sem"]
+            continue
+        if e is None:
             continue
         for j in need[i]:
             name, val = done[j]
             if waited[e].get(name, 0) < val:
                 Q[e].wait_ge(T.sem[name], val)
                 waited[e][name] = val
-        ins = o["emit"]()
+        ins = o["ways"][e][0]()
         if o["kind"] == "d":
             done[i] = ("d%d" % nd, 16)
             ins.then_inc(T.sem["d%d" % nd], 16)

@@ -1,3 +1,4 @@
+import math
 from concourse.bass import DstId, RemoteDMATransfer
 from concourse.mybir import AluOpType as A, AxisListType as AX, ActivationFunctionType as AF
 
@@ -32,16 +33,16 @@ def _sb(names, cols, dt, tail=""):
 KM = max(SCS) // 16
 for _a in [("XB", XW, B16), ("Q", V + 16, B16), ("IB FX XL", V, B16), ("LB", W + SL, B16), ("CT", W + 16, B16), ("DN", 1024, I32), ("DH DL RO", 1024, B16),
            ("SN SN2 SN3 DC", 112, I32), ("cU kU sU", 112, U16), ("MK GS SB", NG, B16), ("sa sb", 112, F32), ("T28", 32, B16),
-           ("pI LI", 8, I32), ("pF M4", 16, F32), ("IX IS WS WS8 W2 W6 W7 WZ W5b CA CB fl", 144, B16), ("ZO", 72, B16), ("WH", 144, F16),
+           ("pI LI", 8, I32), ("pF M4", 16, F32), ("IX IS WS WS8 W2 W6 W7 WZ W5b CA CB", 144, B16), ("ZO", 72, B16), ("WH", 144, F16),
            ("W3 W4", 576, B16), ("W5", 720, F16), ("XP BO TB ID NI CI CN HI NH I9 I16 DPI MB PB LMD GX", 128, B16), ("IDh NX", 128, F16),
-           ("SE C75", 64, B16), ("RA RB", 512, B16), ("CZ", 4 * KM, B16), ("JP RP", 6 * KM, B16),
-           ("K1 CC CW TG ix LJ", 144, F32), ("SI", SL, F32), ("LW", 288, B16), ("CH", 144, F16), ("T2", 17, F32), ("LM", 4, F32),
+           ("SE C75", 64, B16), ("RA RB", 512, B16), ("CZ", 4 * KM, B16), ("RP", 6 * KM, B16), ("JP", 288, B16), ("SJ", 576, F16),
+           ("K1 CC CW TG ix LJ OL", 144, F32), ("SI", SL, F32), ("LW", 288, B16), ("CH", 144, F16), ("T2", 17, F32), ("LM", 4, F32),
            ("IN1 QS GV LY", SL, B16), ("SW vF vS rs", 48, F32), ("k1h k2h", 48, B16), ("vH", 48, F16), ("SEL", 288, F32),
            ("kU1 kU2 vU lU", 48, U16), ("xU", 144, U16), ("OA", 48 * 72, B16), ("HR", 1024, F32), ("OB", 48 * 128, B16), ("FL", 2 * NG, B16), ("YN", 576, F32)]:
     _sb(*_a)
 for _h, _s in enumerate(SCS):
     SCRATCH["AB%d" % _h] = ("sbuf", [128, _s // 16, 96], B16)
-    for _a in [("JU", _s, U16), ("JH", _s // 2, F16), ("GL1 GL2 M0 M1 M2 I0 I1 I2", 4 * _s, B16), ("MN", 4 * _s, B16), ("MX", 4 * _s, F16), ("S0 S1 SJ", 3 * _s // 4, F16),
+    for _a in [("JU", _s, U16), ("JH", _s // 2, F16), ("GL1 GL2 M0 M1 M2 I0 I1 I2", 4 * _s, B16), ("MN", 4 * _s, B16), ("MX MD", 4 * _s, F16), ("S0 S1", 3 * _s // 4, F16),
                ("ub", _s // 4, B16), ("jh", _s // 2, B16), ("RM tb lo", 6 * _s // 16, F32), ("cI", _s // 16, U16), ("CG", _s, B16), ("hc", _s // 4, F32)]:
         _sb(*_a, tail=str(_h))
 for _b in range(8):
@@ -49,10 +50,14 @@ for _b in range(8):
 SEMAPHORES = ["qv", "qa", "qp", "qg"] + ["d%d" % _i for _i in range(44)] + ["r%d" % _i for _i in range(10)] + ["l%d" % _i for _i in range(10)]
 
 CY, PC, GA, SCA, SYNC, PASSES = 1.04, 0.52, 1.56, 3.8, 90.0, 1
-TIME = {'g0': 21.5, 'a10': -44.0, 'a20': 12.5, 'g1': 52.5, 'a11': -10.0, 'a21': -4.0, 'g2': 16.0, 'a12': -11.0, 'a22': 1.0, 'b00': 2.0, 'b10': 6.0, 'c0': 2.5, 'f0': 16.0, 'v0': 5.0, 'h0': 43.5, 'b01': 26.0, 'b11': 2.5, 'c1': 30.5, 'f1': 52.0, 'v1': 40.0, 'h1': 29.0, 'b02': 37.0, 'b12': 4.5, 'c2': 22.0, 'f2': 26.5, 'v2': 30.5, 'h2': 43.5, 'd0': -9.0, 'd1': -8.5, 'd2': 39.5, 'e0': 32.5, 'e2': 12.5, 'e4': 49.5, 'm': 40.0, 'o': -4.0, 'z': -10.5, 's': -51.5, 'k0': -55.5, 'k2': -14.5, 'w': -11.5, 't': -43.5, 'l': -1.5, 'u': 43.0, 'n': 73.5, 'c': -51.0}
-VEE = {'a10': 2, 'b00': 1, 'b01': 1, 'Tb00': 3, 'Tb10': 3, 'Tb01': 3, 'Tb11': 3, 'Tb12': 2, 'Tc0': 1, 'Tc1': 2, 'k0': 1, 'k2': 1, 'n': 1, 'u0': 0, 'u1': 5, 'c': 28485847872, 'a12': 1, 'w1': 1, 'w0': 0, 'b12': 2, 'a21': 2, 'Tc2': 3, 'g1': 2, 'c0': 1, 'g2': 2, 'Tb02': 3, 'c1': 2, 's': 1}
+TIME = {'j0': 13.5, 'j1': 10.0, 'j2': 26.5, 'g0': 17.5, 'a10': -37.0, 'a20': 25.0, 'g1': 56.5, 'a11': -7.0, 'a21': -1.0, 'g2': 9.0, 'a12': -14.5, 'a22': -3.5, 'b00': 2.5, 'b10': 22.0, 'c0': 1.0, 'f0': 20.5, 'v0': 11.0, 'h0': 53.5, 'b01': 26.5, 'b11': 5.0, 'c1': 27.0, 'f1': 58.5, 'v1': 36.0, 'h1': 22.5, 'b02': 32.5, 'b12': 2.0, 'c2': 28.5, 'f2': 17.5, 'v2': 34.0, 'h2': 43.5, 'd0': -7.0, 'd1': -6.0, 'd2': 33.5, 'e0': 29.0, 'e2': 14.0, 'e4': 59.5, 'm': 44.0, 'o': -5.0, 'z': -16.0, 's': -45.0, 'k0': -51.5, 'k2': -21.0, 'w': -9.0, 't': -40.0, 'l': -1.0, 'u': 31.0, 'n': 67.0, 'c': -47.0}
+VEE = {'a10': 2, 'b00': 1, 'b01': 1, 'Tb00': 3, 'Tb10': 3, 'Tb01': 3, 'Tb11': 3, 'Tb12': 2, 'Tc0': 1, 'Tc1': 1, 'k2': 1, 'n': 2, 'u0': 0, 'u1': 9, 'c': 27404439360, 'a12': 1, 'b12': 2, 'Tc2': 2, 'g1': 3, 'g2': 2, 'Tb02': 3, 'z': 1, 'g0': 2, 'w0': 0, 'w1': 0,
+       's': 3, 'c0': 6, 'c1': 6, 'c2': 4, 'f0': 1, 'f1': 1, 'f2': 1, 'h0': 0xffff, 'h1': 0xffff, 'h2': 0xffff, 'm': 32}
 SLACK, LATE = 100.0, 1.0
-CHN, VIS = 1, (1, 1, 1)
+CHN, VIS, CPB, PAIR, OAA = 1, (1, 1, 1), 4, 1, (0, 1, 2)
+PJG = ((0, 1), (2,))
+PACES = ((1.04, 1.56, 3.8, 90.0, 1.0, 0.7), (1.24, 2.0, 5.5, 150.0, 1.4, 0.3 / 1.38))
+STEPS, HEAT, SEED, LEFT, WHOLE = 36000, 100.0, 2, 15, 2
 EDGES = []
 PLAN = {}
 
@@ -154,6 +159,18 @@ def build(g, core, T, topo, rank):
         ops[i]["tag"] = "T" + tag[0]
         ops[ts(out, out, 0.5, A.is_lt)]["after"] = i
 
+    def either(v, reads, out, first, second):
+        i = op({"v": v, "a": actw(*first)}, reads, [out, first[0]])
+        ops[act(*second)]["after"] = i
+
+    def whole(out, a, tmp):
+        v = vw(lambda: g.vector.tensor_scalar(ap(out), ap(a), MAGIC, MAGIC, A.add, A.subtract), cnt(a))
+        either(v, [a], out, (tmp, a, AF.Identity, MAGIC), (out, tmp, AF.Identity, -MAGIC))
+
+    def under(out, a, edge, f):
+        v = vw(lambda: g.vector.tensor_scalar(ap(out), ap(a), edge, f, A.is_lt, A.mult), cnt(a))
+        return lambda s: op({"v": v, "a": actw(out, a, AF.Relu, edge * s, -s)}, [a], [out])
+
     def ind(win, off):
         return ap(win).indirect(ap(off))
 
@@ -164,12 +181,12 @@ def build(g, core, T, topo, rank):
     def gtt(out, win, off, b, o):
         return op({"v": (lambda: g.vector.tensor_tensor(ap(out), ind(win, off), ap(b), o), 50.0, 0, cnt(out), 0)}, [win, off, b], [out])
 
-    def mm(items, extra=()):
+    def mm(items, extra=(), slow=1):
         def e():
             for o, l, r, s0, s1 in items:
                 ins = g.tensor.matmul(ap(o), ap(l), ap(r), s0, s1)
             return ins
-        return op({"p": (e, 0.0, sum(max(min(64, cnt(it[1])), cnt(it[2])) for it in items), 0, 0)}, [x for it in items for x in it[1:3]],
+        return op({"p": (e, 0.0, slow * sum(max(min(64, cnt(it[1])), cnt(it[2])) for it in items), 0, 0)}, [x for it in items for x in it[1:3]],
                   sorted({it[0] for it in items}), 60, "c", extra)
 
     def acc(out, pairs):
@@ -194,11 +211,15 @@ def build(g, core, T, topo, rank):
         per = 4 if len(parts) <= 4 else 2
 
         def e():
-            tr = []
-            for j, (d, src, dst) in enumerate(parts):
+            tr, used = [], set()
+            far = lambda p: topo.die(T.cores[(rank + p[0]) % N]) != topo.die(core)
+            for d, src, dst in sorted(parts, key=lambda p: not far(p)):
                 peer = T.cores[(rank + d) % N]
                 rid, pid = topo.addr(peer)[:2]
-                m = sum(1 << x for x in topo.engines(core, peer)[per * j:per * j + per])
+                es = topo.engines(core, peer)
+                mine = [x for x in es[0::2] + es[1::2] if x not in used][:per]
+                used.update(mine)
+                m = sum(1 << x for x in mine)
                 tr.append(RemoteDMATransfer(dst_ids=[DstId(rid=rid, pnc=pid)], dma_engine_mask=m, remote_sem=T.sem["r%d" % i], src=ap(src), dst=ap(dst)))
             return g.remote_dma_fused(tr, local_sem=T.sem["l%d" % i])
         a = op({"g": (e, 700.0, 0, 0, 0)}, [p[1] for p in parts], [], 1200 + 128 * 45.0 / per, "r", extra)
@@ -222,6 +243,7 @@ def build(g, core, T, topo, rank):
     for a in range(0, W, 1024):
         move(R("LB", a, a + 1024), R("RO"))
     dma("s", R("XB", O1, O1 + V), T.xv[:], 589824, [nb])
+    iota(R("XP"), [[1, 128]], 0, -1)
     for a in (0, 512):
         cp(R("DH", a, a + 512), R("DN", a, a + 512))
     dma("s", R("LB", 0, W, ps=4), R("DH"), 262144)
@@ -232,7 +254,6 @@ def build(g, core, T, topo, rank):
 
     iota(R("pI", 0), [[0, 1]], 0, 1)
     iota(R("IX"), [[1, 144]])
-    iota(R("XP"), [[1, 128]], 0, -1)
     iota(R("DC"), [[4, 7], [0, 16]])
     iota(R("GX"), [[16, 8], [0, 16]])
     iota(R("IS"), [[16, 144]])
@@ -241,8 +262,8 @@ def build(g, core, T, topo, rank):
     iota(R("SW"), [[16, 48]], W)
     iota(R("CA"), [[16, 144]], O1)
     iota(R("CB"), [[16, 144]], -W)
-    iota(R("RA"), [[0, 128], [512, 4]])
-    iota(R("RB"), [[0, 128], [-1024, 4]], 512)
+    iota(R("RA"), [[0, 256], [512, 2]] if PAIR else [[0, 128], [512, 4]])
+    iota(R("RB"), [[0, 256], [-1024, 2]] if PAIR else [[0, 128], [-1024, 4]], 512)
     late = []
     for a in range(0, 36, 9):
         late.append(iota(R("CT", 64 * a, 64 * a + 576), [[8, 9], [0, 64]], 8 * a))
@@ -285,7 +306,7 @@ def build(g, core, T, topo, rank):
     ts(R("BO"), R("GX"), pg, A.is_equal)
     ts(R("ID"), R("XP"), 0.0, A.is_equal)
     ts(R("IDh"), R("XP"), 0.0, A.is_equal)
-    ts(R("NX"), R("XP"), 0.0, A.is_equal, -0.5 - 1.0 / 512, A.mult)
+    ts(R("NX"), R("XP"), 0.0, A.is_equal, 0.5 - 1.0 / 2048 if PAIR else -0.5 - 1.0 / 512, A.mult)
     ts(R("TB"), R("XP"), 0.0, A.is_lt, -1.0, A.mult)
     tt(R("TB"), R("TB"), R("BO"), A.mult)
     for n, f in (("NI", -1.0), ("CI", 25.0 / 1024), ("CN", -25.0 / 1024), ("HI", 0.5), ("NH", -0.5), ("I9", 9.0), ("I16", 16.0), ("DPI", pi),
@@ -300,8 +321,8 @@ def build(g, core, T, topo, rank):
         if cnt(r) > 128:
             late.append(i)
     late = late[5:]
-    iota(R("JP"), [[0, 6 * KM]], 2048)
-    ms(R("JP", 5, 6 * KM, 6), 4096.0, R("RO", 0, KM))
+    iota(R("JP"), [[0, 288]], 2048)
+    ms(R("JP", 5, 288, 6), 4096.0, R("RO", 0, 48))
     for h, s in enumerate(SCS):
         ms(R("S0%d" % h, 0, 3 * s // 4, 3), -4096.0)
     ts(c0w, pi, 3.0, A.is_equal, lnk, A.add)
@@ -346,7 +367,7 @@ def build(g, core, T, topo, rank):
         tag[0] = "s%d" % rd
         lw = R("LW", 144 * rd, 144 * rd + 144)
         if rd == 0:
-            ts(lw, wrap("XL", 0, V, "WS8", p1=8), 0.0, A.is_lt)
+            under(lw, wrap("XL", 0, V, "WS8", p1=8), 0.0, 1.0)(1.0 / 64)
         p, p2, p3 = tile(), tile(), tile()
         mm([(R(p, 0, 144), R("BO"), lw, True, True), (R(p, 144, 288), R("TB"), lw, True, True)])
         scan(R("CC"), R(p, 0, 144), R("K1"), 15.0, A.add, A.min)
@@ -383,6 +404,10 @@ def build(g, core, T, topo, rank):
         ts(R("LI", 1), R("LI", 0), 7, A.bitwise_and)
         ts(R("LM", 1), R("LI", 1), 190.0, A.add, 4096.0, A.mult)
         scaled(R("LMD"), R("ID"), R("LM", 1))
+        if rd == 0:
+            p5 = R(tile(), 0, 144)
+            mm(acc(p5, [(R("ID"), R("CA")), (R("DPI"), R("RO", 0, 144)), (R("MB"), lw)]))
+            move(R("OL"), p5)
         tt(R("TG"), R("CW"), lw, A.mult)
 
     def piece(rd, h, hb):
@@ -427,13 +452,13 @@ def build(g, core, T, topo, rank):
             ps = visit(j, j, "WZ", [(R("ID"), R("CZ", 0, IC))])
             ts(third("S0", 2 - j), ps, -1.0, A.mult)
             tt(third("S1", 2 - j), ps, jh(j), A.min)
-        scan(R("SJ" + s), R("S0" + s), R("S1" + s), 0.0, A.min, A.max)
-        ts(ju(3), third("SJ", 2), 2048.0, A.add)
+        j3 = R("SJ", 3 * s0 // 4 + 2, 3 * (s0 + SC) // 4, 3)
+        scan(R("SJ", 3 * s0 // 4, 3 * (s0 + SC) // 4), R("S0" + s), R("S1" + s), 0.0, A.min, A.max)
+        ts(ju(3), j3, 2048.0, A.add)
+        pj = yield
         tag[0] = "c" + key
-        ts(R("ub" + s), visit(2, 3, "WS", []), 9.0, A.is_lt, 2.0 ** 26, A.mult)
-        pj, pe = tile(), tile()
-        mm(group([(R(pj, 0, 6 * KC), R("ID"), R("JP", 0, 6 * KC)), (R(pj, 4, 6 * KC, 6), R("IDh"), kc("vH"))] +
-                 [(R(pj, 3 - k, 6 * KC, 6), R("W5", 144 * k + 12 - 4 * t, 144 * k + 140 - 4 * t), R("SJ" + s, 2 + 3 * t, 3 * IC, 12)) for k in range(4) for t in range(4)]))
+        under(R("ub" + s), visit(2, 3, "WS", []), 9.0, 2.0 ** 26)(2.0 ** 26)
+        pe = tile()
         tag[0] = "f" + key
         m2 = "M2" + s
         for t in range(TC):
@@ -441,9 +466,16 @@ def build(g, core, T, topo, rank):
             scan(R("MX" + s, *c), R("RA"), R(m2, *c), 0.0, A.min, A.max)
             scan(R("MN" + s, *c), R("RB"), R(m2, *c), 0.0, A.max, A.min)
         ps = R(tile(), 0, SC)
-        mm(acc(ps, [(R("HI"), R(m2, k, 4 * SC, 4)) for k in range(4)] + [(R(w), R(n + s, 3, 4 * SC, 4)) for w, n in (("NX", "MX"), ("NH", "MN"))]))
+        if PAIR:
+            for a in range(0, 2 * SC, 512):
+                b = min(a + 512, 2 * SC)
+                scan(R("MD" + s, a, b), R("RA", 0, b - a), R("MN" + s, 2 * a + 1, 2 * b, 2), 0.0, A.min, A.max)
+                scan(R("MD" + s, 2 * SC + a, 2 * SC + b), R("RB", 0, b - a), R("MX" + s, 2 * a + 1, 2 * b, 2), 0.0, A.max, A.min)
+            mm(acc(ps, [(R("NX"), R("MD" + s, 2 * SC * x + 1, 2 * SC * (x + 1), 2)) for x in range(2)]))
+        else:
+            mm(acc(ps, [(R("HI"), R(m2, k, 4 * SC, 4)) for k in range(4)] + [(R(w), R(n + s, 3, 4 * SC, 4)) for w, n in (("NX", "MX"), ("NH", "MN"))]))
         y = R("XB", yb, yb + SC)
-        ts(y, ps, MAGIC, A.add, MAGIC, A.subtract)
+        whole(y, ps, R("HR", s0, s0 + SC))
         nk = 512 // SC
         for b in range(0, 4, nk):
             p = tile()
@@ -457,7 +489,7 @@ def build(g, core, T, topo, rank):
         sel = R("SEL", 6 * s0 // 16, 6 * (s0 + SC) // 16)
         scan(R("RM" + s), R("RP", 0, 6 * KC), e, 0.0, A.min, A.max)
         tt(R("tb" + s), R("RM" + s), e, A.subtract)
-        tt(R("lo" + s), R(pj, 0, 6 * KC), R("tb" + s), A.subtract)
+        tt(R("lo" + s), pj, R("tb" + s), A.subtract)
         scan(sel, R("tb" + s), R("lo" + s), 0.0, A.min, A.max)
         cp(R("cI" + s), R("SEL", 6 * s0 // 16 + 5, 6 * (s0 + SC) // 16, 6))
         gather(R("CG" + s), R("CT"), R("cI" + s))
@@ -473,25 +505,46 @@ def build(g, core, T, topo, rank):
         if h == 0:
             tag[0] = "o%d" % rd
             for bk in hb:
-                mm([(R(bk, p1=72), R("ZO"), R("RO", 0, 512), True, False)], [first[0]])
+                mm([(R(bk, 0, 128 * CPB, p1=72), R("ZO"), R("RO", 0, 128 * CPB), True, False)], [first[0]])
         tag[0] = "h" + key
         for gg in range(8):
-            bk, c0 = hb[gg // 4], 128 * (gg % 4)
+            bk, c0 = hb[gg // CPB], 128 * (gg % CPB)
             it = []
             for t in range(TC):
                 j = 6 * gg + s0 // 128 + t
                 col = lambda a: R("hc" + s, n8 * a + 8 * t + gg)
                 ts(R("OB", 128 * j, 128 * j + 128), R("IX", 0, 128), col(0), A.add, col(1), A.is_equal)
-                ts(R("OA", 72 * j, 72 * j + 72), R("IS", 0, 72), col(2), A.is_equal, col(3), A.mult)
-                it.append((R(bk, c0, c0 + 128, p1=72), R("OA", 72 * j, 72 * j + 72), R("OB", 128 * j, 128 * j + 128), False, h == NCH - 1 and gg % 4 == 3 and t == TC - 1))
-            mm(it)
+                oa, xs, at, wt = R("OA", 72 * j, 72 * j + 72), R("IS", 0, 72), col(2), col(3)
+                if h in OAA:
+                    v = vw(lambda oa=oa, at=at, wt=wt: g.vector.tensor_scalar(ap(oa), ap(xs), ap(at), ap(wt), A.is_equal, A.mult), 36)
+                    either(v, [xs, at, wt], oa, (oa, xs, AF.Abs, at, -1.0), (oa, oa, AF.Relu, wt, -1.0))
+                else:
+                    ts(oa, xs, at, A.is_equal, wt, A.mult)
+                it.append((R(bk, c0, c0 + 128, p1=72), R("OA", 72 * j, 72 * j + 72), R("OB", 128 * j, 128 * j + 128), False, False))
+            i = mm(it)
+            ops[i]["r"] += ops[i]["w"]
+            ops[i]["w"] = []
         tag[0] = "d" + key
-        j3, hi, lo = third("SJ", 2), R("jh" + s, 0, IC), R("jh" + s, IC, 2 * IC)
+        hi, lo = R("jh" + s, 0, IC), R("jh" + s, IC, 2 * IC)
         ts(hi, j3, MAGIC * 64, A.add, MAGIC * 64, A.subtract)
         tt(lo, j3, hi, A.subtract)
         p = tile()
         mm([it for m in range(4) for it in acc(R(p, m, SC, 4), [(R("W4", 144 * m + 4, 144 * m + 132), hi), (R("W4", 144 * m + 3, 144 * m + 131), lo)])])
         shifted(R("LY", s0, s0 + SC), R(p, 0, SC), lyb)
+        yield
+
+    def pieces(rd, hs, hb):
+        runs = [piece(rd, h, hb) for h in hs]
+        for x in runs:
+            next(x)
+        tag[0] = "j%d%d" % (rd, hs[0])
+        a, b, pj = sum(SCS[:hs[0]]) // 16, sum(SCS[:hs[-1] + 1]) // 16, tile()
+        n = 6 * (b - a)
+        mm(group([(R(pj, 0, n), R("ID"), R("JP", 0, n)), (R(pj, 4, n, 6), R("IDh"), R("vH", a, b))] +
+                 [(R(pj, 3 - k, n, 6), R("W5", 144 * k + 12 - 4 * t, 144 * k + 140 - 4 * t), R("SJ", 12 * a + 2 + 3 * t, 12 * b, 12)) for k in range(4) for t in range(4)]))
+        for h, x in zip(hs, runs):
+            c = 6 * (sum(SCS[:h]) // 16 - a)
+            x.send(R(pj, c, c + 6 * SCS[h] // 16))
 
     def relink(rd, s0, s1):
         tag[0] = "e%d%d" % (rd, s0 // 128)
@@ -508,16 +561,14 @@ def build(g, core, T, topo, rank):
     def marks(rd, hb):
         tag[0] = "m%d" % rd
         for b, bk in enumerate(hb):
-            hr = R("HR", 512 * b, 512 * b + 512, p1=72)
-            if b == 0:
-                act(hr, R(bk, p1=72), AF.Identity, MAGIC)
-                act(hr, hr, AF.Identity, -MAGIC)
-            else:
-                ts(hr, R(bk, p1=72), MAGIC, A.add, MAGIC, A.subtract)
-            for x in range(4):
-                gg, whole = 4 * b + x, R("HR", 512 * b + 128 * x, 512 * b + 128 * x + 128, p1=72)
-                tt(R3("H", 0, 8, 16 * gg, 16 * gg + 16, p1=72), R(bk, 128 * x, 128 * x + 128, p1=72), whole, A.not_equal)
-                move(R3("H", 0, 8, 128 + 16 * gg, 144 + 16 * gg, p1=72), whole)
+            hr, src = R("HR", 128 * CPB * b, 128 * CPB * (b + 1), p1=72), R(bk, 0, 128 * CPB, p1=72)
+            mm([(R(bk, 0, 64, p1=72), R("ZO"), R("RO", 0, 64), False, True)])
+            whole(hr, src, hr)
+            for x in range(CPB):
+                gg = CPB * b + x
+                up = R("HR", 128 * gg, 128 * gg + 128, p1=72)
+                tt(R3("H", 0, 8, 16 * gg, 16 * gg + 16, p1=72), R(bk, 128 * x, 128 * x + 128, p1=72), up, A.not_equal)
+                move(R3("H", 0, 8, 128 + 16 * gg, 144 + 16 * gg, p1=72), up)
         f0 = NG * rd
         arr = send([(N - d, R3("H", d, d + 1, 0, 256), R("FL", f0 + GH * (d - 1), f0 + GH * d)) for d in range(1, N)])
         for s0, s1 in LINK:
@@ -538,8 +589,7 @@ def build(g, core, T, topo, rank):
                  [(R(p, 72 * b, 72 * b + 72), src, far) for b in range(2) for src in
                   [R3("H", 0, 1, 128 * b, 128 * b + 128, p1=72)] + [R("FL", f0 + GH * j + 128 * b, f0 + GH * j + 128 * b + 128, p1=72) for j in range(7)]]))
         if rd == 0:
-            ts(R("fl"), own, 0.0, A.is_lt)
-            tt(R("LW", 144, 288), R("fl"), R("LW", 0, 144), A.not_equal)
+            tt(R("LW", 144, 288), own, R("OL"), A.not_equal)
         tt(R("ix"), own, R("TG"), A.max if rd == 0 else A.min)
         ts(R("xU"), R("ix"), 0.0 if rd == 0 else float(W), A.add)
         win = R("XB", LC1, G1) if rd == 0 else R("XB", O2, XW)
@@ -555,9 +605,9 @@ def build(g, core, T, topo, rank):
     for rd in range(2):
         show_cols(rd, extra)
         seekers(rd)
-        hb = [tile() for _ in range(2)]
-        for h in range(NCH):
-            piece(rd, h, hb)
+        hb = [tile() for _ in range(8 // CPB)]
+        for hs in PJG:
+            pieces(rd, hs, hb)
         extra = [marks(rd, hb)]
     at = {}
     for i, o in enumerate(ops):
@@ -696,9 +746,182 @@ def engines(ops):
 def plan(ops):
     eng = engines(ops)
     order, bank, deps = forth(ops, back(ops, {i: -(when(o["tag"]) + i * 1e-3) for i, o in enumerate(ops)}, eng), eng)
+    order, eng, bank, deps = refine(ops, order, eng, bank)
     for o, d in zip(ops, deps):
         o["deps"] = sorted({ops[j]["after"] if eng[j] is None and "after" in ops[j] else j for j in d})
     return order, eng, bank
+
+
+def refine(ops, order, eng, bank):
+    n, eng = len(ops), list(eng)
+    base, after, users = [o["base"] for o in ops], [[] for _ in ops], {}
+    for i, o in enumerate(ops):
+        for j in base[i]:
+            after[j].append(i)
+        for r in o["r"] + o["w"]:
+            if r[0][0] == "P" and i not in users.setdefault(r[0], []):
+                users[r[0]].append(i)
+    opens = {u[0]: t for t, u in users.items()}
+    pos = {i: k for k, i in enumerate(order)}
+    seq = {e: [i for i in order if eng[i] == e] for e in "vapgs"}
+    for b in range(8):
+        seq[b] = sorted([t for t in bank if bank[t] == "P%d" % b], key=lambda t: pos[users[t][0]])
+    ways = [[dict({None: 0.0}, **{e: w[1] + cy * (w[2] * (PC / CY if e == "p" else 1) + w[3] * ga + w[4] * sca) for e, w in o["ways"].items() if e}) for o in ops]
+            for cy, ga, sca, _, _, _ in PACES]
+    lats = [[o["lat"] * (p[4] if o["kind"] in "dr" else 1.0) for o in ops] for p in PACES]
+    half = {o["after"]: i for i, o in enumerate(ops) if "after" in o}
+    flex = [i for i, o in enumerate(ops) if len(o["ways"]) == 2]
+    pe, count, seed = [e == "p" for e in eng], [len(d) for d in base], [SEED]
+
+    def rnd(k):
+        seed[0] = (seed[0] * 6364136223846793005 + 1442695040888963407) % 2 ** 64
+        return (seed[0] >> 33) % k
+
+    def times(limit):
+        left, nxt, prv, dep, more = list(count), [-1] * n, [-1] * n, list(base), {}
+        for e, q in seq.items():
+            if isinstance(e, str):
+                for a, b in zip(q, q[1:]):
+                    nxt[a], prv[b] = b, a
+                    left[b] += 1
+            else:
+                for a, b in zip(q, q[1:]):
+                    f = users[b][0]
+                    dep[f] = dep[f] + users[a]
+                    left[f] += len(users[a])
+                    for x in users[a]:
+                        more[x] = more.get(x, after[x]) + [f]
+        todo = [i for i in range(n) if not left[i]]
+        for i in todo:
+            for j in more[i] if i in more else after[i]:
+                left[j] -= 1
+                if not left[j]:
+                    todo.append(j)
+            j = nxt[i]
+            if j >= 0:
+                left[j] -= 1
+                if not left[j]:
+                    todo.append(j)
+        if len(todo) < n:
+            return None
+        mean, runs = 0.0, []
+        for way, lat, pace in zip(ways, lats, PACES):
+            sync, end, fin, by = pace[3], [0.0] * n, [0.0] * n, [-1] * n
+            for i in todo:
+                e, t, w = eng[i], -1e9, -1
+                if pe[i]:
+                    for j in dep[i]:
+                        x = fin[j] - sync if pe[j] else fin[j]
+                        if x > t:
+                            t, w = x, j
+                else:
+                    for j in dep[i]:
+                        if fin[j] > t:
+                            t, w = fin[j], j
+                if e or ops[i]["kind"] == "x":
+                    t += sync
+                p = prv[i]
+                if p >= 0 and end[p] >= t:
+                    t, w = end[p], p
+                by[i] = w
+                end[i] = t = max(t, 0.0) + way[i][e]
+                fin[i] = t + lat[i]
+            mean += max(fin) * pace[5]
+            if not runs and mean > limit:
+                return None
+            runs.append((fin, end, by, mean))
+        return mean, runs, prv, todo, dep
+
+    tags = sorted({o["tag"] for o in ops})
+    runs = [[i for i, o in enumerate(ops) if o["tag"].strip("T") == t] for t in tags if t[0] not in "cT" or len(t) == 3 and t[0] == "c"]
+    runs += [[i for i, o in enumerate(ops) if o["tag"].strip("T")[0] in x and len(o["tag"]) > 2 and o["tag"][-2:] == "%d%d" % (rd, h)]
+             for x in ("vh", "fvh", "cfvh", "vhd", "ga", "ab", "bc") for rd in range(2) for h in range(NCH)]
+    cur = times(1e9)
+    best = (cur, dict((e, list(q)) for e, q in seq.items()), list(eng))
+    for step in range(STEPS):
+        k = rnd(len(PACES))
+        (fin, end, by, _), prv, way = cur[1][k], cur[2], ways[k]
+        i, chain = fin.index(max(fin)), []
+        while i >= 0:
+            chain.append(i)
+            i = by[i]
+        old, x = {}, rnd(100)
+
+        def put(e, item, p):
+            old.setdefault(e, list(seq[e]))
+            seq[e].insert(p, item)
+
+        def take(e, item):
+            old.setdefault(e, list(seq[e]))
+            seq[e].remove(item)
+        was = list(eng)
+        if x < 12:
+            can = [i for i in chain if len(ops[i]["ways"]) == 2] if x < 7 else flex
+            if not can:
+                continue
+            i = can[rnd(len(can))]
+            e, f = eng[i], "a" if eng[i] == "v" else "v"
+            take(e, i)
+            put(f, i, sum(1 for j in seq[f] if end[j] - 0.5 * way[j][f] < end[i] - way[i][e]))
+            eng[i] = f
+            if i in half and f == "a":
+                e = eng[half[i]] = next(iter(ops[half[i]]["ways"]))
+                put(e, half[i], sum(1 for j in seq["v"] if end[j] < end[i] + 100) if e == "v" else min(seq["a"].index(i) + 1 + rnd(2), len(seq["a"])))
+            elif i in half:
+                take(eng[half[i]], half[i])
+                eng[half[i]] = None
+        elif x < 22:
+            can = [i for i in chain if i in opens and by[i] >= 0 and by[i] != prv[i] and by[i] not in base[i]] or list(opens)
+            i = can[rnd(len(can))]
+            take([b for b in range(8) if opens[i] in seq[b]][0], opens[i])
+            b = rnd(8)
+            put(b, opens[i], sum(1 for t in seq[b] if end[users[t][0]] < end[i]))
+        elif x < 22 + LEFT:
+            i = rnd(n)
+            e = eng[i]
+            if by[i] < 0 or by[i] != prv[i]:
+                continue
+            ready = max([fin[j] for j in cur[4][i]] + [0.0])
+            p = sum(1 for j in seq[e] if end[j] - way[j][e] < ready + 100)
+            if p >= seq[e].index(i):
+                continue
+            take(e, i)
+            put(e, i, p)
+        elif x < 22 + LEFT + WHOLE:
+            new = {}
+            for i in runs[rnd(len(runs))]:
+                e = eng[i]
+                ready = max([new.get(j, fin[j]) for j in cur[4][i]] + [0.0]) + 100
+                if e and ready < end[i] - way[i][e] - 200:
+                    take(e, i)
+                    put(e, i, sum(1 for j in seq[e] if new.get(j, end[j]) - way[j][e] < ready))
+                    new[i] = ready + way[i][e]
+                elif not e:
+                    new[i] = ready - 100
+        else:
+            can = [i for i in chain if by[i] >= 0 and by[i] == prv[i]]
+            if not can:
+                continue
+            i = can[rnd(len(can))]
+            e, d = eng[i], (1, 1, 1, 2, 3, 5, 8, 13)[rnd(8)]
+            p = seq[e].index(i)
+            if rnd(2):
+                take(e, i)
+                put(e, i, max(0, p - d))
+            else:
+                take(e, prv[i])
+                put(e, prv[i], p - 1 + d)
+        rise = -(HEAT * (1 - step / STEPS) + 2) * math.log((rnd(10 ** 6) + 1) / 1e6)
+        new = times(cur[1][0][3] + rise + 150)
+        if new is not None and new[0] - cur[0] <= rise:
+            cur = new
+            if cur[0] < best[0][0]:
+                best = (cur, dict((e, list(q)) for e, q in seq.items()), list(eng))
+        else:
+            seq.update(old)
+            eng[:] = was
+    cur, seq, eng = best
+    return cur[3], eng, {t: "P%d" % b for b in range(8) for t in seq[b]}, cur[4]
 
 
 def rank_program(g, core, T, topo):

import math
from concourse.bass import DstId, RemoteDMATransfer
from concourse.mybir import AluOpType as A, AxisListType as AX, ActivationFunctionType as AF

N = 8
V, GH, SL = 2304, 256, 768
NG = (N - 1) * GH
W = V + NG
SCS = (256, 256, 256)
SEEK = ((0, 256), (256, 768))
LINK = ((0, 256), (256, 512), (512, 768))
NCH = len(SCS)
LC1, Y1, O1, G1, O2, G2, LC2, Y2, XW = 0, 16, 784, 3088, 4880, 7184, 8976, 8992, 9760
MAGIC = 12582912.0
B16, F16, F32, I32, U16 = "bfloat16", "float16", "float32", "int32", "uint16"
SIZE = {B16: 2, F16: 2, F32: 4, I32: 4, U16: 2}
SCRATCH = {"H": ("sbuf", [128, 8, 256], B16)}
PLACE = {}


def _sb(names, cols, dt, tail=""):
    for name in names.split():
        if cols > 600:
            SCRATCH[name + tail] = ("sbuf", [128, cols], dt)
            PLACE[name + tail] = (name + tail, 0, cols)
        else:
            pool = "small_" + dt
            at = SCRATCH[pool][1][1] if pool in SCRATCH else 0
            SCRATCH[pool] = ("sbuf", [128, at + (cols + 15) // 16 * 16], dt)
            PLACE[name + tail] = (pool, at, cols)


KM = max(SCS) // 16
for _a in [("XB", XW, B16), ("Q", V + 16, B16), ("IB FX XL", V, B16), ("LB", W + SL, B16), ("CT", W + 16, B16), ("DN", 1024, I32), ("DH DL RO", 1024, B16),
           ("SN SN2 SN3 DC", 112, I32), ("cU kU sU", 112, U16), ("MK GS SB", NG, B16), ("sa sb", 112, F32), ("T28", 32, B16),
           ("pI LI", 8, I32), ("pF M4", 16, F32), ("IX IS WS WS8 W2 W6 W7 WZ W5b CA CB", 144, B16), ("ZO", 72, B16), ("WH", 144, F16),
           ("W3 W4", 576, B16), ("W5", 720, F16), ("XP BO TB ID NI CI CN HI NH I9 I16 DPI MB PB LMD GX", 128, B16), ("IDh NX", 128, F16),
           ("SE C75", 64, B16), ("RA RB", 512, B16), ("CZ", 4 * KM, B16), ("RP", 6 * KM, B16), ("JP", 288, B16), ("SJ", 576, F16),
           ("K1 CC CW TG ix LJ OL", 144, F32), ("SI", SL, F32), ("LW", 288, B16), ("CH", 144, F16), ("T2", 17, F32), ("LM", 4, F32),
           ("IN1 QS GV LY", SL, B16), ("SW vF vS rs", 48, F32), ("k1h k2h", 48, B16), ("vH", 48, F16), ("SEL", 288, F32),
           ("kU1 kU2 vU lU", 48, U16), ("xU", 144, U16), ("OA", 48 * 72, B16), ("HR", 1024, F32), ("OB", 48 * 128, B16), ("FL", 2 * NG, B16), ("YN", 576, F32)]:
    _sb(*_a)
for _h, _s in enumerate(SCS):
    SCRATCH["AB%d" % _h] = ("sbuf", [128, _s // 16, 96], B16)
    for _a in [("JU", _s, U16), ("JH", _s // 2, F16), ("GL1 GL2 M0 M1 M2 I0 I1 I2", 4 * _s, B16), ("MN", 4 * _s, B16), ("MX MD", 4 * _s, F16), ("S0 S1", 3 * _s // 4, F16),
               ("ub", _s // 4, B16), ("jh", _s // 2, B16), ("RM tb lo", 6 * _s // 16, F32), ("cI", _s // 16, U16), ("CG", _s, B16), ("hc", _s // 4, F32)]:
        _sb(*_a, tail=str(_h))
for _b in range(8):
    SCRATCH["P%d" % _b] = ("psum", [128, 512], F32)
SEMAPHORES = ["qv", "qa", "qp", "qg"] + ["d%d" % _i for _i in range(44)] + ["r%d" % _i for _i in range(10)] + ["l%d" % _i for _i in range(10)]

CY, PC, GA, SCA, SYNC, PASSES = 1.04, 0.52, 1.56, 3.8, 90.0, 1
TIME = {'j0': 13.5, 'j1': 10.0, 'j2': 26.5, 'g0': 17.5, 'a10': -37.0, 'a20': 25.0, 'g1': 56.5, 'a11': -7.0, 'a21': -1.0, 'g2': 9.0, 'a12': -14.5, 'a22': -3.5, 'b00': 2.5, 'b10': 22.0, 'c0': 1.0, 'f0': 20.5, 'v0': 11.0, 'h0': 53.5, 'b01': 26.5, 'b11': 5.0, 'c1': 27.0, 'f1': 58.5, 'v1': 36.0, 'h1': 22.5, 'b02': 32.5, 'b12': 2.0, 'c2': 28.5, 'f2': 17.5, 'v2': 34.0, 'h2': 43.5, 'd0': -7.0, 'd1': -6.0, 'd2': 33.5, 'e0': 29.0, 'e2': 14.0, 'e4': 59.5, 'm': 44.0, 'o': -5.0, 'z': -16.0, 's': -45.0, 'k0': -51.5, 'k2': -21.0, 'w': -9.0, 't': -40.0, 'l': -1.0, 'u': 31.0, 'n': 67.0, 'c': -47.0}
VEE = {'a10': 2, 'b00': 1, 'b01': 1, 'Tb00': 3, 'Tb10': 3, 'Tb01': 3, 'Tb11': 3, 'Tb12': 2, 'Tc0': 1, 'Tc1': 1, 'k2': 1, 'n': 2, 'u0': 0, 'u1': 9, 'c': 27404439360, 'a12': 1, 'b12': 2, 'Tc2': 2, 'g1': 3, 'g2': 2, 'Tb02': 3, 'z': 1, 'g0': 2, 'w0': 0, 'w1': 0,
       's': 3, 'c0': 6, 'c1': 6, 'c2': 4, 'f0': 1, 'f1': 1, 'f2': 1, 'h0': 0xffff, 'h1': 0xffff, 'h2': 0xffff, 'm': 32}
SLACK, LATE = 100.0, 1.0
CHN, VIS, CPB, PAIR, OAA = 1, (1, 1, 1), 4, 1, (0, 1, 2)
PJG = ((0, 1), (2,))
PACES = ((1.04, 1.56, 3.8, 90.0, 1.0, 0.7), (1.24, 2.0, 5.5, 150.0, 1.4, 0.3 / 1.38))
STEPS, HEAT, SEED, LEFT, WHOLE = 36000, 100.0, 2, 15, 2
EDGES = []
PLAN = {}


def R(name, c0=None, c1=None, st=1, p0=0, p1=128, ps=1):
    buf, at, cols = PLACE.get(name, (name, 0, 512))
    if c0 is None:
        c0, c1 = 0, cols
    elif c1 is None:
        c1 = c0 + 1
    return (buf, at + c0, at + c1, st, p0, p1, ps)


def R3(name, b0, b1, c0, c1, st=1, p1=128):
    return (name, b0, b1, st, 0, p1, 1, c0, c1)


def cnt(r):
    if len(r) == 9:
        return (r[2] - r[1]) * ((r[8] - r[7] + r[3] - 1) // r[3])
    return (r[2] - r[1] + r[3] - 1) // r[3]


def build(g, core, T, topo, rank):
    ops, tag, ntile, nrem = [], ["c"], [0], [0]
    Q = {"v": g.vector, "a": g.scalar, "p": g.tensor, "g": g, "s": g.sync}

    def tile():
        ntile[0] += 1
        return "P%d" % ntile[0]

    def ap(r):
        if not isinstance(r, tuple):
            return r
        if len(r) == 9:
            if r[2] - r[1] == 1:
                return T[r[0]][r[4]:r[5], r[1], r[7]:r[8]:r[3]]
            return T[r[0]][r[4]:r[5], r[1]:r[2], r[7]:r[8]:r[3]]
        return T[PLAN["bank"].get(r[0], r[0])][r[4]:r[5]:r[6], r[1]:r[2]:r[3]]

    def two(*rs):
        return all(r[0][0] != "P" and SIZE[SCRATCH[r[0]][2]] == 2 for r in rs)

    def op(ways, reads, writes, lat=0.0, kind="c", extra=()):
        busy = {e: w[1] + (w[2] * (PC if e == "p" else CY) + (w[3] * GA + w[4] * SCA) * CY) for e, w in ways.items()}
        ops.append({"ways": ways, "busy": busy, "r": [r for r in reads if isinstance(r, tuple)], "w": list(writes), "lat": lat, "kind": kind,
                    "tag": tag[0], "extra": list(extra)})
        return len(ops) - 1

    def vw(f, n):
        return (f, 0.0, max(64.0, n), 0, 0)

    def ts(out, in0, s1, op0, s2=None, op1=None):
        def e():
            if op1 is None:
                return g.vector.tensor_scalar(ap(out), ap(in0), ap(s1), None, op0)
            return g.vector.tensor_scalar(ap(out), ap(in0), ap(s1), ap(s2), op0, op1)
        return op({"v": vw(e, cnt(in0) * (0.5 if two(out, in0) else 1))}, [in0, s1, s2], [out])

    def tt(out, a, b, o):
        f = 1 if "P" in (a[0][0], b[0][0]) else 2
        return op({"v": vw(lambda: g.vector.tensor_tensor(ap(out), ap(a), ap(b), o), cnt(a) * f)}, [a, b], [out])

    def cpw(out, a):
        return vw(lambda: g.vector.tensor_copy(ap(out), ap(a)), cnt(a) * (0.5 if two(out, a) else 1))

    def cp(out, a):
        return op({"v": cpw(out, a)}, [a], [out])

    def ms(out, val, src=None):
        ways = {"v": vw(lambda: g.vector.memset(ap(out), val), cnt(out) * (0.5 if two(out) else 1))}
        if src:
            ways["a"] = actw(out, src, AF.Identity, val, 0.0)
        return op(ways, [src], [out])

    def scan(out, d0, d1, first, op0, op1):
        return op({"v": vw(lambda: g.vector.tensor_tensor_scan(ap(out), ap(d0), ap(d1), first, op0, op1), cnt(d0) * (0.5 if two(out, d0, d1) else 1))}, [d0, d1], [out])

    def actw(out, a, f, bias=0.0, scale=1.0):
        return (lambda: g.scalar.activation(ap(out), ap(a), f, bias=ap(bias), scale=ap(scale)), 60.0, max(64.0, cnt(a)), 0, 0)

    def act(out, a, f, bias=0.0, scale=1.0):
        return op({"a": actw(out, a, f, bias, scale)}, [a, bias, scale], [out])

    def move(out, a):
        return op({"v": cpw(out, a), "a": actw(out, a, AF.Identity)}, [a], [out])

    def scaled(out, a, f):
        v = vw(lambda: g.vector.tensor_scalar(ap(out), ap(a), ap(f), None, A.mult), cnt(a) * (0.5 if two(out, a) else 1))
        return op({"v": v, "a": actw(out, a, AF.Identity, 0.0, f)}, [a, f], [out])

    def shifted(out, a, f):
        v = vw(lambda: g.vector.tensor_scalar(ap(out), ap(a), ap(f), None, A.add), cnt(a) * (0.5 if two(out, a) else 1))
        return op({"v": v, "a": actw(out, a, AF.Identity, f)}, [a, f], [out])

    def test(out, a):
        v = vw(lambda: g.vector.tensor_scalar(ap(out), ap(a), MAGIC, MAGIC, A.add, A.is_equal), cnt(a))
        i = op({"v": v, "a": actw(out, a, AF.Abs)}, [a], [out])
        ops[i]["tag"] = "T" + tag[0]
        ops[ts(out, out, 0.5, A.is_lt)]["after"] = i

    def either(v, reads, out, first, second):
        i = op({"v": v, "a": actw(*first)}, reads, [out, first[0]])
        ops[act(*second)]["after"] = i

    def whole(out, a, tmp):
        v = vw(lambda: g.vector.tensor_scalar(ap(out), ap(a), MAGIC, MAGIC, A.add, A.subtract), cnt(a))
        either(v, [a], out, (tmp, a, AF.Identity, MAGIC), (out, tmp, AF.Identity, -MAGIC))

    def under(out, a, edge, f):
        v = vw(lambda: g.vector.tensor_scalar(ap(out), ap(a), edge, f, A.is_lt, A.mult), cnt(a))
        return lambda s: op({"v": v, "a": actw(out, a, AF.Relu, edge * s, -s)}, [a], [out])

    def ind(win, off):
        return ap(win).indirect(ap(off))

    def gather(out, win, off):
        return op({"a": (lambda: g.scalar.activation(ap(out), ind(win, off), AF.Copy), 65.0, 0, cnt(out), 0),
                   "v": (lambda: g.vector.tensor_copy(ap(out), ind(win, off)), 50.0, 0, cnt(out), 0)}, [win, off], [out])

    def gtt(out, win, off, b, o):
        return op({"v": (lambda: g.vector.tensor_tensor(ap(out), ind(win, off), ap(b), o), 50.0, 0, cnt(out), 0)}, [win, off, b], [out])

    def mm(items, extra=(), slow=1):
        def e():
            for o, l, r, s0, s1 in items:
                ins = g.tensor.matmul(ap(o), ap(l), ap(r), s0, s1)
            return ins
        return op({"p": (e, 0.0, slow * sum(max(min(64, cnt(it[1])), cnt(it[2])) for it in items), 0, 0)}, [x for it in items for x in it[1:3]],
                  sorted({it[0] for it in items}), 60, "c", extra)

    def acc(out, pairs):
        return [(out, l, r, i == 0, i == len(pairs) - 1) for i, (l, r) in enumerate(pairs)]

    def group(items):
        return [(o, l, r, i == 0, i == len(items) - 1) for i, (o, l, r) in enumerate(items)]

    def iota(out, pat, base=0, cm=0):
        def e():
            if SCRATCH[out[0]][2] == I32:
                return g.iota(ap(out), pat, base, cm)
            return g.iota(ap(out), pat, base, cm, allow_small_or_imprecise_dtypes=True)
        return op({"g": (e, 130.0, 2 * cnt(out), 0, 0)}, [], [out])

    def dma(q, out, in_, nbytes, extra=()):
        return op({q: (lambda: Q[q].dma_start(ap(out), ap(in_)), 100.0, 0, 0, 0)}, [in_], [out] if isinstance(out, tuple) else [], 1400 + nbytes / 250.0, "d", extra)

    def send(parts, extra=()):
        i = nrem[0]
        nrem[0] += 1
        per = 4 if len(parts) <= 4 else 2

        def e():
            tr, used = [], set()
            far = lambda p: topo.die(T.cores[(rank + p[0]) % N]) != topo.die(core)
            for d, src, dst in sorted(parts, key=lambda p: not far(p)):
                peer = T.cores[(rank + d) % N]
                rid, pid = topo.addr(peer)[:2]
                es = topo.engines(core, peer)
                mine = [x for x in es[0::2] + es[1::2] if x not in used][:per]
                used.update(mine)
                m = sum(1 << x for x in mine)
                tr.append(RemoteDMATransfer(dst_ids=[DstId(rid=rid, pnc=pid)], dma_engine_mask=m, remote_sem=T.sem["r%d" % i], src=ap(src), dst=ap(dst)))
            return g.remote_dma_fused(tr, local_sem=T.sem["l%d" % i])
        a = op({"g": (e, 700.0, 0, 0, 0)}, [p[1] for p in parts], [], 1200 + 128 * 45.0 / per, "r", extra)
        ops[a]["sem"] = ("l%d" % i, per * len(parts))
        b = op({None: (None, 0.0, 0, 0, 0)}, [], [p[2] for p in parts], 300, "x", [a])
        ops[b]["sem"] = ("r%d" % i, per * len(parts))
        return b

    def S(r, name="WS", k=0, p1=128):
        return R(name, 144 * k + 15 - r, 144 * k + 143 - r, p1=p1)

    def wrap(src, c0, n, name="WS", byk=False, more=(), p1=128):
        out = R(tile(), 0, n // 16)
        mm(acc(out, list(more) + [(S(r, name, r % 4 if byk else 0, p1), R(src, c0 + r, c0 + n, 16, p1=p1)) for r in range(16)]))
        return out

    dma("s", R("XL", p1=8), T.xv[0:128:16, :], 36864)
    nb = dma("s", R("DN"), T.nb[:], 524288)
    dma("a", R("SN"), T.snd[:], 57344)
    ms(R("RO"), 1.0)
    for a in range(0, W, 1024):
        move(R("LB", a, a + 1024), R("RO"))
    dma("s", R("XB", O1, O1 + V), T.xv[:], 589824, [nb])
    iota(R("XP"), [[1, 128]], 0, -1)
    for a in (0, 512):
        cp(R("DH", a, a + 512), R("DN", a, a + 512))
    dma("s", R("LB", 0, W, ps=4), R("DH"), 262144)
    for a in range(0, 1024, 256):
        lo = tt(R("DL", a, a + 256), R("DN", a, a + 256), R("DH", a, a + 256), A.subtract)
    dma("s", R("LB", 0, W, p0=1, ps=4), R("DL"), 262144)
    dma("s", R("Q", 0, V), T.cq[:], 589824, [lo])

    iota(R("pI", 0), [[0, 1]], 0, 1)
    iota(R("IX"), [[1, 144]])
    iota(R("DC"), [[4, 7], [0, 16]])
    iota(R("GX"), [[16, 8], [0, 16]])
    iota(R("IS"), [[16, 144]])
    for s0, s1 in SEEK:
        iota(R("SI", s0, s1), [[1, s1 - s0]], 15 + s0)
    iota(R("SW"), [[16, 48]], W)
    iota(R("CA"), [[16, 144]], O1)
    iota(R("CB"), [[16, 144]], -W)
    iota(R("RA"), [[0, 256], [512, 2]] if PAIR else [[0, 128], [512, 4]])
    iota(R("RB"), [[0, 256], [-1024, 2]] if PAIR else [[0, 128], [-1024, 4]], 512)
    late = []
    for a in range(0, 36, 9):
        late.append(iota(R("CT", 64 * a, 64 * a + 576), [[8, 9], [0, 64]], 8 * a))
        late.append(iota(R("IB", 64 * a, 64 * a + 576), [[0, 9], [1, 64]]))
    dma("s", R("CT", 0, V, p0=3, ps=16), R("IB", p0=0, p1=8), 36864)
    ts(R("pI", 1), R("pI", 0), 15, A.bitwise_and)
    ts(R("pI", 2), R("pI", 0), 112, A.bitwise_and)
    ts(R("pI", 3), R("pI", 0), 3, A.bitwise_and)
    ts(R("pI", 4), R("pI", 0), 15, A.bitwise_and, 2, A.arith_shift_right)
    cp(R("pF", 0, 5), R("pI", 0, 5))
    pi, pg, pk, pm = R("pF", 1), R("pF", 2), R("pF", 3), R("pF", 4)
    lnk, lyb, big, eq2, c0w, c8w, tk, tm, p16, t4, hi0 = [R("pF", j) for j in range(5, 16)]
    x144 = R("IX")
    ts(p16, R("pF", 0), 16.0, A.mult)
    ts(R("WS8"), x144, -15.0, A.add, p16, A.is_equal)
    ts(lnk, pk, 2.0, A.is_lt)
    ts(hi0, pk, 0.0, A.is_equal, 2048.0, A.mult)
    ts(lyb, pk, 2.0, A.is_ge, hi0, A.add)
    ts(big, pi, 9.0, A.is_ge, 4096.0, A.mult)
    ts(eq2, pi, 2.0, A.is_equal)
    ts(tk, pk, 4.0, A.mult, pg, A.add)
    ts(tm, pg, pm, A.add)
    ts(t4, pm, 4.0, A.mult, pg, A.add)
    ts(R("WS"), x144, -15.0, A.add, pg, A.is_equal)
    scaled(R("W6"), R("WS"), lnk)
    scaled(R("WZ"), R("WS"), 4096.0)
    ts(R("WH"), R("WS"), 0.0625, A.mult)
    ts(R("M4", 0, 4), R("IX", 0, 4), pk, A.is_equal)
    ts(R("M4", 4, 8), R("IX", 0, 4), pm, A.is_equal, lnk, A.mult)
    ts(R("M4", 8, 12), R("IX", 0, 4), pm, A.is_equal)
    ts(R("W4", 0, 144), x144, -4.0, A.add, tk, A.is_equal)
    ts(R("W5b"), x144, -12.0, A.add, tm, A.is_equal)
    scaled(R("W2"), R("W5b"), lnk)
    ts(R("W7"), x144, -12.0, A.add, t4, A.is_equal)
    scaled(R("W7"), R("W7"), lnk)
    for k in (3, 2, 1, 0):
        scaled(R("W3", 144 * k, 144 * k + 144), R("WS"), R("M4", 4 + k))
        scaled(R("W4", 144 * k, 144 * k + 144), R("W4", 0, 144), R("M4", 8 + k))
        ts(R("W5", 144 * k, 144 * k + 144), R("W5b"), R("M4", k), A.mult)
    ts(R("BO"), R("GX"), pg, A.is_equal)
    ts(R("ID"), R("XP"), 0.0, A.is_equal)
    ts(R("IDh"), R("XP"), 0.0, A.is_equal)
    ts(R("NX"), R("XP"), 0.0, A.is_equal, 0.5 - 1.0 / 2048 if PAIR else -0.5 - 1.0 / 512, A.mult)
    ts(R("TB"), R("XP"), 0.0, A.is_lt, -1.0, A.mult)
    tt(R("TB"), R("TB"), R("BO"), A.mult)
    for n, f in (("NI", -1.0), ("CI", 25.0 / 1024), ("CN", -25.0 / 1024), ("HI", 0.5), ("NH", -0.5), ("I9", 9.0), ("I16", 16.0), ("DPI", pi),
                 ("MB", -8192.0), ("PB", 8192.0)):
        scaled(R(n), R("ID"), f)
    for r, f in ((R("K1"), 1024.0), (R("XB", LC1, O1), -64.0), (R("T28"), 0.0), (R("C75"), 0.0), (R("C75", 0, 64, 2), -15.0 / 256),
                 (R("RP"), 2.0 ** 29), (R("RP", 0, 6 * KM, 6), 0.0)):
        ms(r, f, R("RO", 0, cnt(r)))
    for r, f in [(R("ZO"), 0), (R("XB", LC2, Y2), -64), (R("CT", W, W + 16), 512), (R("LB", W, W + SL), 0), (R("Q", V, V + 16), -1024), (R("CZ"), -34816)] + \
                [(R3("H", d, d + 2, 0, 256), 0) for d in range(0, 8, 2)] + [(R3("AB%d" % h, 0, s // 16, 64, 96), 0) for h, s in enumerate(SCS)]:
        i = iota(r, [[0, cnt(r)]], f)
        if cnt(r) > 128:
            late.append(i)
    late = late[5:]
    iota(R("JP"), [[0, 288]], 2048)
    ms(R("JP", 5, 288, 6), 4096.0, R("RO", 0, 48))
    for h, s in enumerate(SCS):
        ms(R("S0%d" % h, 0, 3 * s // 4, 3), -4096.0)
    ts(c0w, pi, 3.0, A.is_equal, lnk, A.add)
    ts(c8w, pi, 6.0, A.is_equal, -1.0, A.mult)
    ts(c8w, c8w, eq2, A.add, c0w, A.add)
    scaled(R("SE", 0, 16, 2), R("BO", 0, 128, 16), c0w)
    scaled(R("SE", 1, 16, 2), R("BO", 0, 128, 16), c8w)
    shifted(R("SW"), R("SW"), pi)
    ts(R("SN2"), R("SN"), W - 1, A.bitwise_and)
    cp(R("cU"), R("SN2"))
    ts(R("SN3"), R("SN"), 12, A.arith_shift_right)
    tt(R("SN3"), R("SN3"), R("DC"), A.add)
    cp(R("kU"), R("SN3"))
    ts(R("sa", 0, 28), R("DC", 0, 112, 4), 4.0, A.mult, 16.0, A.add)
    for k in range(4):
        ts(R("T28", k, 28, 4), R("sa", k, 28, 4), eq2, A.mult, R("M4", 4 + k), A.add)
    HALF = ((0, 4), (4, 7))
    for a, b in HALF:
        gather(R("MK", GH * a, GH * b), R("T28"), R("kU", 16 * a, 16 * b))

    def show_links(rd):
        tag[0] = "l%d" % rd
        for a, b in HALF:
            gtt(R("GS", GH * a, GH * b), R("LB", 0, V), R("cU", 16 * a, 16 * b), R("MK", GH * a, GH * b), A.mult)
            ps = wrap("GS", GH * a, GH * (b - a), "W6")
            ts(R("sa", 16 * a, 16 * b), ps, float(V), A.is_ge, -float(W), A.mult)
            tt(R("sb", 16 * a, 16 * b), ps, R("sa", 16 * a, 16 * b), A.add)
            ts(R("sU", 16 * a, 16 * b), R("sb", 16 * a, 16 * b), float(O1) if rd == 0 else float(NG), A.add)

    def show_cols(rd, extra):
        tag[0] = "w%d" % rd
        win = R("XB", LC1, G1) if rd == 0 else R("XB", G1, G2)
        gl = G1 if rd == 0 else G2
        for a, b in HALF:
            for x, y in ((a, a + 2), (a + 2, b)):
                gather(R("SB", GH * x, GH * y), win, R("sU", 16 * x, 16 * y))
            send([(d + 1, R("SB", GH * d, GH * d + GH), R("XB", gl + GH * d, gl + GH * d + GH)) for d in range(a, b)])
        tag[0] = "t%d" % rd
        send([(d + 1, R("GS", GH * d, GH * d + GH), R("CT", V + GH * d, V + GH * d + GH)) for d in range(7)], extra)

    def seekers(rd):
        tag[0] = "s%d" % rd
        lw = R("LW", 144 * rd, 144 * rd + 144)
        if rd == 0:
            under(lw, wrap("XL", 0, V, "WS8", p1=8), 0.0, 1.0)(1.0 / 64)
        p, p2, p3 = tile(), tile(), tile()
        mm([(R(p, 0, 144), R("BO"), lw, True, True), (R(p, 144, 288), R("TB"), lw, True, True)])
        scan(R("CC"), R(p, 0, 144), R("K1"), 15.0, A.add, A.min)
        cp(R("CH"), R("CC"))
        tt(R("CW"), R(p, 144, 288), R("CC"), A.add)
        p4 = tile()
        mm(acc(R(p2, 16), [(S(r, "WH"), R("CH", 9 * r + 8)) for r in range(16)]))
        mm(acc(R(p4, 0, 16), [(S(r, "WH"), R("CH", r, 144, 9)) for r in range(9)]))
        cp(R("T2", 16), R(p2, 16))
        shifted(R("T2", 0, 16), R(p4, 0, 16), big)
        for s0, s1 in SEEK:
            tag[0] = "k%d%d" % (rd, s0 // 128)
            kc = lambda n: R(n, s0 // 16, s1 // 16)
            i1, si = R("IN1", s0, s1), R("SI", s0, s1)
            ts(i1, si, R("T2", 16), A.is_ge)
            ps = wrap("IN1", s0, s1 - s0)
            ts(kc("kU1"), ps, 15.0, A.min)
            ts(kc("k1h"), ps, 15.0, A.min)
            gtt(i1, R("T2", 0, 16), kc("kU1"), si, A.is_le)
            ps = wrap("IN1", s0, s1 - s0, more=[(R("I9"), kc("k1h"))])
            ts(kc("kU2"), ps, 143.0, A.min)
            ts(kc("k2h"), ps, 143.0, A.min)
            gtt(i1, R("CW"), kc("kU2"), si, A.is_le)
            ps = wrap("IN1", s0, s1 - s0, more=[(R("I16"), kc("k2h"))])
            cp(kc("vU"), ps)
            ts(kc("vH"), ps, -2048.0, A.add)
            move(kc("vF"), ps)
        tag[0] = "z%d" % rd
        tt(R("vS"), R("vF"), R("SW"), A.subtract)
        mm([(R(p3, 0, 144), R("RO", 0, 128), lw, True, True)])
        op({"a": (lambda: g.scalar.activation(ap(R("LJ")), ap(R(p3, 0, 144)), AF.Identity, accum_out=ap(R("LM", 0))), 50.0, 144, 0, 0)},
           [R(p3, 0, 144)], [R("LJ"), R("LM", 0)])
        cp(R("LI", 0), R("LM", 0))
        ts(R("LI", 1), R("LI", 0), 7, A.bitwise_and)
        ts(R("LM", 1), R("LI", 1), 190.0, A.add, 4096.0, A.mult)
        scaled(R("LMD"), R("ID"), R("LM", 1))
        if rd == 0:
            p5 = R(tile(), 0, 144)
            mm(acc(p5, [(R("ID"), R("CA")), (R("DPI"), R("RO", 0, 144)), (R("MB"), lw)]))
            move(R("OL"), p5)
        tt(R("TG"), R("CW"), lw, A.mult)

    def piece(rd, h, hb):
        s, SC, s0 = str(h), SCS[h], sum(SCS[:h])
        IC, KC, TC, key = SC // 4, SC // 16, SC // 128, "%d%d" % (rd, h)
        xw = R("XB", O1, O2) if rd == 0 else R("XB", O2, LC2)
        yb = (Y1 if rd == 0 else Y2) + s0
        kc = lambda n: R(n, s0 // 16, s0 // 16 + KC)
        ju = lambda j: R("JU" + s, IC * j, IC * j + IC)
        jh = lambda j: R("JH" + s, IC * j, IC * j + IC)
        third = lambda n, j: R(n + s, j, 3 * IC, 3)

        def visit(j, l, name, more):
            m, i = "M%d" % j + s, "I%d" % j + s
            for t in range(TC):
                if t % VIS[j] == 0:
                    u = min(t + VIS[j], TC)
                    gather(R(m, 512 * t, 512 * u), xw, R("JU" + s, IC * l + 32 * t, IC * l + 32 * u))
                p = tile()
                mm([it for k in range(4) for it in acc(R(p, k, 512, 4), [(R("CI"), R(m, 512 * t + k, 512 * t + 512, 4)), (R("CN"), R("QS", s0 + 128 * t, s0 + 128 * t + 128))])])
                o = R(i, 512 * t, 512 * t + 512)
                test(o, R(p))
            return wrap(i, 0, 4 * SC, name, more=more)

        tag[0] = "g" + key
        first = [gather(R("GV", s0, s0 + SC), R("LB", 0, W), kc("vU"))]
        gather(R("QS", s0, s0 + SC), R("Q"), kc("vU"))
        ps = R(tile(), 0, IC)
        mm(acc(ps, [(R("W2", 12 - 4 * m, 140 - 4 * m), R("GV", s0 + m, s0 + SC, 4)) for m in range(4)]))
        for j in range(3):
            if j:
                tag[0] = "a%d" % j + key
                for t in range(0, TC, CHN):
                    u = min(t + CHN, TC)
                    gather(R("GL%d" % j + s, 512 * t, 512 * u), R("LB", 0, W), R("JU" + s, IC * (j - 1) + 32 * t, IC * (j - 1) + 32 * u))
                ps = wrap("GL%d" % j + s, 0, 4 * SC, "W3", True)
            if j < 2:
                cp(ju(j), ps)
            ts(jh(j) if j < 2 else third("S1", 0), ps, -2048.0, A.add)
        for j in range(2):
            tag[0] = "b%d" % j + key
            ps = visit(j, j, "WZ", [(R("ID"), R("CZ", 0, IC))])
            ts(third("S0", 2 - j), ps, -1.0, A.mult)
            tt(third("S1", 2 - j), ps, jh(j), A.min)
        j3 = R("SJ", 3 * s0 // 4 + 2, 3 * (s0 + SC) // 4, 3)
        scan(R("SJ", 3 * s0 // 4, 3 * (s0 + SC) // 4), R("S0" + s), R("S1" + s), 0.0, A.min, A.max)
        ts(ju(3), j3, 2048.0, A.add)
        pj = yield
        tag[0] = "c" + key
        under(R("ub" + s), visit(2, 3, "WS", []), 9.0, 2.0 ** 26)(2.0 ** 26)
        pe = tile()
        tag[0] = "f" + key
        m2 = "M2" + s
        for t in range(TC):
            c = (512 * t, 512 * t + 512)
            scan(R("MX" + s, *c), R("RA"), R(m2, *c), 0.0, A.min, A.max)
            scan(R("MN" + s, *c), R("RB"), R(m2, *c), 0.0, A.max, A.min)
        ps = R(tile(), 0, SC)
        if PAIR:
            for a in range(0, 2 * SC, 512):
                b = min(a + 512, 2 * SC)
                scan(R("MD" + s, a, b), R("RA", 0, b - a), R("MN" + s, 2 * a + 1, 2 * b, 2), 0.0, A.min, A.max)
                scan(R("MD" + s, 2 * SC + a, 2 * SC + b), R("RB", 0, b - a), R("MX" + s, 2 * a + 1, 2 * b, 2), 0.0, A.max, A.min)
            mm(acc(ps, [(R("NX"), R("MD" + s, 2 * SC * x + 1, 2 * SC * (x + 1), 2)) for x in range(2)]))
        else:
            mm(acc(ps, [(R("HI"), R(m2, k, 4 * SC, 4)) for k in range(4)] + [(R(w), R(n + s, 3, 4 * SC, 4)) for w, n in (("NX", "MX"), ("NH", "MN"))]))
        y = R("XB", yb, yb + SC)
        whole(y, ps, R("HR", s0, s0 + SC))
        nk = 512 // SC
        for b in range(0, 4, nk):
            p = tile()
            mm([it for x in range(nk) for it in acc(R(p, SC * x, SC * x + SC), [(R("ID"), R(m2, b + x, 4 * SC, 4)), (R("NI"), y)])])
            for x in range(nk):
                act(R3("AB" + s, 0, KC, 16 * (3 - b - x), 16 * (4 - b - x)), R(p, SC * x, SC * x + SC), AF.Abs)
        e = R(pe, 0, 6 * KC)
        mm(group([(e, S(r, "WZ"), R3("AB" + s, 0, KC, r, 96, 16)) for r in range(16)] + [(R(pe, 4, 6 * KC, 6), R("LMD"), R("RO", 0, KC))] +
                 [(R(pe, 5, 6 * KC, 6), R("W5b", 12 - 4 * t, 140 - 4 * t), R("ub" + s, t, IC, 4)) for t in range(4)]))
        tag[0] = "v" + key
        sel = R("SEL", 6 * s0 // 16, 6 * (s0 + SC) // 16)
        scan(R("RM" + s), R("RP", 0, 6 * KC), e, 0.0, A.min, A.max)
        tt(R("tb" + s), R("RM" + s), e, A.subtract)
        tt(R("lo" + s), pj, R("tb" + s), A.subtract)
        scan(sel, R("tb" + s), R("lo" + s), 0.0, A.min, A.max)
        cp(R("cI" + s), R("SEL", 6 * s0 // 16 + 5, 6 * (s0 + SC) // 16, 6))
        gather(R("CG" + s), R("CT"), R("cI" + s))
        p, n8 = tile(), 8 * TC
        mm(group([(R(p, 0, 2 * n8), R("RO", 0, 128), R("C75", 0, 2 * n8))] +
                 [(R(p, 16 * t, 16 * t + 16), R("CG" + s, 128 * t, 128 * t + 128), R("SE", 0, 16)) for t in range(TC)]))
        hc, low = lambda a: R("hc" + s, n8 * a, n8 * a + n8), R(p, 0, 2 * n8, 2)
        ts(hc(0), low, MAGIC * 16, A.add, MAGIC * 16, A.subtract)
        ts(hc(2), low, V / 2 - 8.0, A.is_ge, V / 2, A.mult)
        ts(hc(3), low, V / 2 - 8.0, A.is_ge, 1.0 / 2048, A.add)
        cp(hc(1), R(p, 1, 2 * n8, 2))
        tt(hc(2), hc(0), hc(2), A.subtract)
        if h == 0:
            tag[0] = "o%d" % rd
            for bk in hb:
                mm([(R(bk, 0, 128 * CPB, p1=72), R("ZO"), R("RO", 0, 128 * CPB), True, False)], [first[0]])
        tag[0] = "h" + key
        for gg in range(8):
            bk, c0 = hb[gg // CPB], 128 * (gg % CPB)
            it = []
            for t in range(TC):
                j = 6 * gg + s0 // 128 + t
                col = lambda a: R("hc" + s, n8 * a + 8 * t + gg)
                ts(R("OB", 128 * j, 128 * j + 128), R("IX", 0, 128), col(0), A.add, col(1), A.is_equal)
                oa, xs, at, wt = R("OA", 72 * j, 72 * j + 72), R("IS", 0, 72), col(2), col(3)
                if h in OAA:
                    v = vw(lambda oa=oa, at=at, wt=wt: g.vector.tensor_scalar(ap(oa), ap(xs), ap(at), ap(wt), A.is_equal, A.mult), 36)
                    either(v, [xs, at, wt], oa, (oa, xs, AF.Abs, at, -1.0), (oa, oa, AF.Relu, wt, -1.0))
                else:
                    ts(oa, xs, at, A.is_equal, wt, A.mult)
                it.append((R(bk, c0, c0 + 128, p1=72), R("OA", 72 * j, 72 * j + 72), R("OB", 128 * j, 128 * j + 128), False, False))
            i = mm(it)
            ops[i]["r"] += ops[i]["w"]
            ops[i]["w"] = []
        tag[0] = "d" + key
        hi, lo = R("jh" + s, 0, IC), R("jh" + s, IC, 2 * IC)
        ts(hi, j3, MAGIC * 64, A.add, MAGIC * 64, A.subtract)
        tt(lo, j3, hi, A.subtract)
        p = tile()
        mm([it for m in range(4) for it in acc(R(p, m, SC, 4), [(R("W4", 144 * m + 4, 144 * m + 132), hi), (R("W4", 144 * m + 3, 144 * m + 131), lo)])])
        shifted(R("LY", s0, s0 + SC), R(p, 0, SC), lyb)
        yield

    def pieces(rd, hs, hb):
        runs = [piece(rd, h, hb) for h in hs]
        for x in runs:
            next(x)
        tag[0] = "j%d%d" % (rd, hs[0])
        a, b, pj = sum(SCS[:hs[0]]) // 16, sum(SCS[:hs[-1] + 1]) // 16, tile()
        n = 6 * (b - a)
        mm(group([(R(pj, 0, n), R("ID"), R("JP", 0, n)), (R(pj, 4, n, 6), R("IDh"), R("vH", a, b))] +
                 [(R(pj, 3 - k, n, 6), R("W5", 144 * k + 12 - 4 * t, 144 * k + 140 - 4 * t), R("SJ", 12 * a + 2 + 3 * t, 12 * b, 12)) for k in range(4) for t in range(4)]))
        for h, x in zip(hs, runs):
            c = 6 * (sum(SCS[:h]) // 16 - a)
            x.send(R(pj, c, c + 6 * SCS[h] // 16))

    def relink(rd, s0, s1):
        tag[0] = "e%d%d" % (rd, s0 // 128)
        kc = lambda n: R(n, s0 // 16, s1 // 16)
        tt(kc("rs"), R("SEL", 6 * s0 // 16 + 5, 6 * s1 // 16, 6), kc("vF"), A.is_equal)
        tt(kc("rs"), kc("rs"), kc("vS"), A.mult)
        tt(kc("rs"), kc("rs"), kc("SW"), A.add)
        cp(kc("lU"), kc("rs"))
        for a in range(s0, s1, 256):
            b = min(a + 256, s1)
            ly, lu = R("LY", a, b), R("lU", a // 16, b // 16)
            op({"v": (lambda ly=ly, lu=lu: g.vector.tensor_copy(ind(R("LB"), lu), ap(ly)), 50.0, 0, 0, b - a)}, [ly, lu], [R("LB")])

    def marks(rd, hb):
        tag[0] = "m%d" % rd
        for b, bk in enumerate(hb):
            hr, src = R("HR", 128 * CPB * b, 128 * CPB * (b + 1), p1=72), R(bk, 0, 128 * CPB, p1=72)
            mm([(R(bk, 0, 64, p1=72), R("ZO"), R("RO", 0, 64), False, True)])
            whole(hr, src, hr)
            for x in range(CPB):
                gg = CPB * b + x
                up = R("HR", 128 * gg, 128 * gg + 128, p1=72)
                tt(R3("H", 0, 8, 16 * gg, 16 * gg + 16, p1=72), R(bk, 128 * x, 128 * x + 128, p1=72), up, A.not_equal)
                move(R3("H", 0, 8, 128 + 16 * gg, 144 + 16 * gg, p1=72), up)
        f0 = NG * rd
        arr = send([(N - d, R3("H", d, d + 1, 0, 256), R("FL", f0 + GH * (d - 1), f0 + GH * d)) for d in range(1, N)])
        for s0, s1 in LINK:
            relink(rd, s0, s1)
        if rd == 0:
            show_links(1)
        else:
            tag[0] = "n1"
            for hh in range(2):
                ps = R(tile(), 0, 288)
                mm(acc(ps, [(R("W7", 12 - m, 140 - m), R("LB", 576 * m + 288 * hh, 576 * m + 288 * hh + 288)) for m in range(4)]))
                move(R("YN", 288 * hh, 288 * hh + 288), ps)
            dma("s", T.yn[:], R("YN"), 294912)
        tag[0] = "u%d" % rd
        p = tile()
        own, far = R(p, 0, 144), R("MB" if rd == 0 else "PB", 0, 72, p1=72)
        mm(group([(own, R("ID"), R("CA" if rd == 0 else "CB")), (own, R("DPI"), R("RO", 0, 144))] +
                 [(R(p, 72 * b, 72 * b + 72), src, far) for b in range(2) for src in
                  [R3("H", 0, 1, 128 * b, 128 * b + 128, p1=72)] + [R("FL", f0 + GH * j + 128 * b, f0 + GH * j + 128 * b + 128, p1=72) for j in range(7)]]))
        if rd == 0:
            tt(R("LW", 144, 288), own, R("OL"), A.not_equal)
        tt(R("ix"), own, R("TG"), A.max if rd == 0 else A.min)
        ts(R("xU"), R("ix"), 0.0 if rd == 0 else float(W), A.add)
        win = R("XB", LC1, G1) if rd == 0 else R("XB", O2, XW)
        for a in range(0, 144, 36):
            o = R("XB", O2 + 16 * a, O2 + 16 * a + 576) if rd == 0 else R("FX", 16 * a, 16 * a + 576)
            gather(o, win, R("xU", a, a + 36))
            if rd == 1:
                dma("s", T.yx[:, 16 * a:16 * a + 576], o, 147456)
        return arr

    show_links(0)
    extra = ()
    for rd in range(2):
        show_cols(rd, extra)
        seekers(rd)
        hb = [tile() for _ in range(8 // CPB)]
        for hs in PJG:
            pieces(rd, hs, hb)
        extra = [marks(rd, hb)]
    at = {}
    for i, o in enumerate(ops):
        at.setdefault(o["tag"], []).append(i)
    for i in late:
        ops[i]["extra"].append([j for j in at["w0"] if ops[j]["kind"] == "r"][-1])
    for a, b in EDGES:
        for rd in "01":
            ops[at[b[:-1] + rd + b[-1]][0]]["extra"].append(at[a[:-1] + rd + a[-1]][0])
    return ops, Q


def span(r):
    if r[0][0] == "P":
        return r[0], 0, 512, -1, 0, 1
    m = sum(1 << p for p in range(r[4], r[5], r[6]))
    return (r[0], r[1], r[2], m) + (r[7:9] if len(r) == 9 else (0, 1))


def hazards(ops):
    seen = {}
    for i, o in enumerate(ops):
        deps = set(o["extra"])
        acc = [(span(r), False) for r in o["r"]] + [(span(r), True) for r in o["w"]]
        for sp, wr in acc:
            for j, x, w2 in seen.get(sp[0], []):
                if x[1] < sp[2] and sp[1] < x[2] and (x[3] & sp[3]) and x[4] < sp[5] and sp[4] < x[5]:
                    same = len(o["ways"]) == 1 and ops[j]["ways"].keys() == o["ways"].keys()
                    if wr or w2 or (sp[3] == -1 and not same):
                        deps.add(j)
        for sp, wr in acc:
            lst = seen.setdefault(sp[0], [])
            if wr:
                lst[:] = [y for y in lst if not (sp[1] <= y[1][1] and y[1][2] <= sp[2] and (y[1][3] & ~sp[3]) == 0 and sp[4] <= y[1][4] and y[1][5] <= sp[5])]
            lst.append((i, sp, wr))
        deps.discard(i)
        o["deps"] = o["base"] = sorted(deps)


def back(ops, key, eng):
    n = len(ops)
    left = [0] * n
    for o in ops:
        for j in o["base"]:
            left[j] += 1
    est, out, used = [0.0] * n, [0.0] * n, {e: [] for e in "vapgs"}
    ready = [i for i in range(n) if left[i] == 0]
    while ready:
        i = min(ready, key=key.get)
        ready.remove(i)
        e = eng[i]
        t, busy = est[i] + ops[i]["lat"], ops[i]["busy"][e]
        if e:
            u = used[e]
            k = len(u)
            while k and u[k - 1][1] > t:
                k -= 1
            while k < len(u) and u[k][0] < t + busy:
                t = u[k][1]
                k += 1
            u.insert(k, (t, t + busy))
        out[i] = t + busy
        for j in ops[i]["base"]:
            est[j] = max(est[j], out[i] + (0.0 if e == "p" == eng[j] or (e is None and "after" in ops[i]) else SYNC))
            left[j] -= 1
            if left[j] == 0:
                ready.append(j)
    return out


def forth(ops, urge, eng):
    n = len(ops)
    after, left, users, opens = [[] for _ in ops], [len(o["base"]) for o in ops], {}, [None] * n
    for i, o in enumerate(ops):
        for j in o["base"]:
            after[j].append(i)
        for r in o["r"] + o["w"]:
            if r[0][0] == "P" and i not in users.setdefault(r[0], []):
                users[r[0]].append(i)
    for t, u in users.items():
        opens[u[0]] = t
    fin, deps, order, bank = [None] * n, [list(o["base"]) for o in ops], [], {}
    free, held = {e: 0.0 for e in ("v", "a", "p", "g", "s", None)}, [[] for _ in range(8)]
    est = [0.0] * n
    ready = [i for i in range(n) if left[i] == 0]
    while ready:
        idle = min([(max([fin[j] + SYNC for j in u] + [0.0]), b) for b, u in enumerate(held) if all(fin[j] is not None for j in u)] or [(None, None)])
        can = []
        for i in ready:
            if not opens[i] or idle[0] is not None:
                can.append((max(est[i], free[eng[i]], idle[0] if opens[i] else 0.0), i))
        t0, e0 = min(can)[0], eng[min(can)[1]]
        _, t, i = max((urge[i] - LATE * (t - t0), t, i) for t, i in can if eng[i] == e0 and t <= t0 + SLACK)
        ready.remove(i)
        if opens[i]:
            deps[i] += held[idle[1]]
            held[idle[1]] = users[opens[i]]
            bank[opens[i]] = "P%d" % idle[1]
        if e0:
            free[e0] = t + ops[i]["busy"][e0]
        fin[i] = t + ops[i]["busy"][e0] + ops[i]["lat"]
        order.append(i)
        for j in after[i]:
            est[j] = max(est[j], fin[i] + (0.0 if e0 == "p" == eng[j] or (e0 is None and "after" in ops[i]) else SYNC))
            left[j] -= 1
            if left[j] == 0:
                ready.append(j)
    return order, bank, deps


def stage(tag):
    if tag == "c":
        return tag, 0
    return (tag[0], int(tag[1])) if len(tag) == 2 else (tag[:-2] + tag[-1], int(tag[-2]))


def when(tag):
    s, rd = stage(tag)
    return TIME.get(s, TIME[s.strip("T")]) + 60 * rd


def engines(ops):
    eng, seen = [], {}
    for o in ops:
        if len(o["ways"]) == 2:
            k = seen[o["tag"]] = seen.get(o["tag"], -1) + 1
            eng.append("v" if VEE.get(o["tag"], VEE.get(stage(o["tag"])[0], 0)) >> k & 1 else "a")
        elif "after" in o and eng[o["after"]] == "v":
            eng.append(None)
            o["busy"][None] = 0.0
        else:
            eng.append(next(iter(o["ways"])))
    return eng


def plan(ops):
    eng = engines(ops)
    order, bank, deps = forth(ops, back(ops, {i: -(when(o["tag"]) + i * 1e-3) for i, o in enumerate(ops)}, eng), eng)
    order, eng, bank, deps = refine(ops, order, eng, bank)
    for o, d in zip(ops, deps):
        o["deps"] = sorted({ops[j]["after"] if eng[j] is None and "after" in ops[j] else j for j in d})
    return order, eng, bank


def refine(ops, order, eng, bank):
    n, eng = len(ops), list(eng)
    base, after, users = [o["base"] for o in ops], [[] for _ in ops], {}
    for i, o in enumerate(ops):
        for j in base[i]:
            after[j].append(i)
        for r in o["r"] + o["w"]:
            if r[0][0] == "P" and i not in users.setdefault(r[0], []):
                users[r[0]].append(i)
    opens = {u[0]: t for t, u in users.items()}
    pos = {i: k for k, i in enumerate(order)}
    seq = {e: [i for i in order if eng[i] == e] for e in "vapgs"}
    for b in range(8):
        seq[b] = sorted([t for t in bank if bank[t] == "P%d" % b], key=lambda t: pos[users[t][0]])
    ways = [[dict({None: 0.0}, **{e: w[1] + cy * (w[2] * (PC / CY if e == "p" else 1) + w[3] * ga + w[4] * sca) for e, w in o["ways"].items() if e}) for o in ops]
            for cy, ga, sca, _, _, _ in PACES]
    lats = [[o["lat"] * (p[4] if o["kind"] in "dr" else 1.0) for o in ops] for p in PACES]
    half = {o["after"]: i for i, o in enumerate(ops) if "after" in o}
    flex = [i for i, o in enumerate(ops) if len(o["ways"]) == 2]
    pe, count, seed = [e == "p" for e in eng], [len(d) for d in base], [SEED]

    def rnd(k):
        seed[0] = (seed[0] * 6364136223846793005 + 1442695040888963407) % 2 ** 64
        return (seed[0] >> 33) % k

    def times(limit):
        left, nxt, prv, dep, more = list(count), [-1] * n, [-1] * n, list(base), {}
        for e, q in seq.items():
            if isinstance(e, str):
                for a, b in zip(q, q[1:]):
                    nxt[a], prv[b] = b, a
                    left[b] += 1
            else:
                for a, b in zip(q, q[1:]):
                    f = users[b][0]
                    dep[f] = dep[f] + users[a]
                    left[f] += len(users[a])
                    for x in users[a]:
                        more[x] = more.get(x, after[x]) + [f]
        todo = [i for i in range(n) if not left[i]]
        for i in todo:
            for j in more[i] if i in more else after[i]:
                left[j] -= 1
                if not left[j]:
                    todo.append(j)
            j = nxt[i]
            if j >= 0:
                left[j] -= 1
                if not left[j]:
                    todo.append(j)
        if len(todo) < n:
            return None
        mean, runs = 0.0, []
        for way, lat, pace in zip(ways, lats, PACES):
            sync, end, fin, by = pace[3], [0.0] * n, [0.0] * n, [-1] * n
            for i in todo:
                e, t, w = eng[i], -1e9, -1
                if pe[i]:
                    for j in dep[i]:
                        x = fin[j] - sync if pe[j] else fin[j]
                        if x > t:
                            t, w = x, j
                else:
                    for j in dep[i]:
                        if fin[j] > t:
                            t, w = fin[j], j
                if e or ops[i]["kind"] == "x":
                    t += sync
                p = prv[i]
                if p >= 0 and end[p] >= t:
                    t, w = end[p], p
                by[i] = w
                end[i] = t = max(t, 0.0) + way[i][e]
                fin[i] = t + lat[i]
            mean += max(fin) * pace[5]
            if not runs and mean > limit:
                return None
            runs.append((fin, end, by, mean))
        return mean, runs, prv, todo, dep

    tags = sorted({o["tag"] for o in ops})
    runs = [[i for i, o in enumerate(ops) if o["tag"].strip("T") == t] for t in tags if t[0] not in "cT" or len(t) == 3 and t[0] == "c"]
    runs += [[i for i, o in enumerate(ops) if o["tag"].strip("T")[0] in x and len(o["tag"]) > 2 and o["tag"][-2:] == "%d%d" % (rd, h)]
             for x in ("vh", "fvh", "cfvh", "vhd", "ga", "ab", "bc") for rd in range(2) for h in range(NCH)]
    cur = times(1e9)
    best = (cur, dict((e, list(q)) for e, q in seq.items()), list(eng))
    for step in range(STEPS):
        k = rnd(len(PACES))
        (fin, end, by, _), prv, way = cur[1][k], cur[2], ways[k]
        i, chain = fin.index(max(fin)), []
        while i >= 0:
            chain.append(i)
            i = by[i]
        old, x = {}, rnd(100)

        def put(e, item, p):
            old.setdefault(e, list(seq[e]))
            seq[e].insert(p, item)

        def take(e, item):
            old.setdefault(e, list(seq[e]))
            seq[e].remove(item)
        was = list(eng)
        if x < 12:
            can = [i for i in chain if len(ops[i]["ways"]) == 2] if x < 7 else flex
            if not can:
                continue
            i = can[rnd(len(can))]
            e, f = eng[i], "a" if eng[i] == "v" else "v"
            take(e, i)
            put(f, i, sum(1 for j in seq[f] if end[j] - 0.5 * way[j][f] < end[i] - way[i][e]))
            eng[i] = f
            if i in half and f == "a":
                e = eng[half[i]] = next(iter(ops[half[i]]["ways"]))
                put(e, half[i], sum(1 for j in seq["v"] if end[j] < end[i] + 100) if e == "v" else min(seq["a"].index(i) + 1 + rnd(2), len(seq["a"])))
            elif i in half:
                take(eng[half[i]], half[i])
                eng[half[i]] = None
        elif x < 22:
            can = [i for i in chain if i in opens and by[i] >= 0 and by[i] != prv[i] and by[i] not in base[i]] or list(opens)
            i = can[rnd(len(can))]
            take([b for b in range(8) if opens[i] in seq[b]][0], opens[i])
            b = rnd(8)
            put(b, opens[i], sum(1 for t in seq[b] if end[users[t][0]] < end[i]))
        elif x < 22 + LEFT:
            i = rnd(n)
            e = eng[i]
            if by[i] < 0 or by[i] != prv[i]:
                continue
            ready = max([fin[j] for j in cur[4][i]] + [0.0])
            p = sum(1 for j in seq[e] if end[j] - way[j][e] < ready + 100)
            if p >= seq[e].index(i):
                continue
            take(e, i)
            put(e, i, p)
        elif x < 22 + LEFT + WHOLE:
            new = {}
            for i in runs[rnd(len(runs))]:
                e = eng[i]
                ready = max([new.get(j, fin[j]) for j in cur[4][i]] + [0.0]) + 100
                if e and ready < end[i] - way[i][e] - 200:
                    take(e, i)
                    put(e, i, sum(1 for j in seq[e] if new.get(j, end[j]) - way[j][e] < ready))
                    new[i] = ready + way[i][e]
                elif not e:
                    new[i] = ready - 100
        else:
            can = [i for i in chain if by[i] >= 0 and by[i] == prv[i]]
            if not can:
                continue
            i = can[rnd(len(can))]
            e, d = eng[i], (1, 1, 1, 2, 3, 5, 8, 13)[rnd(8)]
            p = seq[e].index(i)
            if rnd(2):
                take(e, i)
                put(e, i, max(0, p - d))
            else:
                take(e, prv[i])
                put(e, prv[i], p - 1 + d)
        rise = -(HEAT * (1 - step / STEPS) + 2) * math.log((rnd(10 ** 6) + 1) / 1e6)
        new = times(cur[1][0][3] + rise + 150)
        if new is not None and new[0] - cur[0] <= rise:
            cur = new
            if cur[0] < best[0][0]:
                best = (cur, dict((e, list(q)) for e, q in seq.items()), list(eng))
        else:
            seq.update(old)
            eng[:] = was
    cur, seq, eng = best
    return cur[3], eng, {t: "P%d" % b for b in range(8) for t in seq[b]}, cur[4]


def rank_program(g, core, T, topo):
    rank = T.rank_of(core)
    if rank is None:
        return
    ops, Q = build(g, core, T, topo, rank)
    if "order" not in PLAN:
        hazards(ops)
        PLAN["order"], PLAN["eng"], PLAN["bank"] = plan(ops)
        pos = {i: k for k, i in enumerate(PLAN["order"])}
        eng = PLAN["eng"]
        need = PLAN["need"] = []
        for i, o in enumerate(ops):
            last = {}
            for j in o["deps"]:
                if eng[i] is None or eng[j] == "p" == eng[i]:
                    continue
                k = eng[j] if ops[j]["kind"] == "c" else j
                if k not in last or pos[j] > pos[last[k]]:
                    last[k] = j
            need.append(sorted(last.values()))
    need = PLAN["need"]
    wanted = {j for x in need for j in x}
    count, done, waited, nd = {e: 0 for e in Q}, {}, {e: {} for e in Q}, 0
    for i in PLAN["order"]:
        o, e = ops[i], PLAN["eng"][i]
        if o["kind"] == "x":
            done[i] = o["sem"]
            continue
        if e is None:
            continue
        for j in need[i]:
            name, val = done[j]
            if waited[e].get(name, 0) < val:
                Q[e].wait_ge(T.sem[name], val)
                waited[e][name] = val
        ins = o["ways"][e][0]()
        if o["kind"] == "d":
            done[i] = ("d%d" % nd, 16)
            ins.then_inc(T.sem["d%d" % nd], 16)
            nd += 1
        elif o["kind"] == "r":
            done[i] = o["sem"]
        elif i in wanted:
            count[e] += 1
            done[i] = ("q" + e, count[e])
            ins.then_inc(T.sem["q" + e], 1)
    final = {}
    for name, val in done.values():
        final[name] = max(final.get(name, 0), val)
    for name in sorted(final):
        if all(waited[e].get(name, 0) < final[name] for e in Q):
            g.sync.wait_ge(T.sem[name], final[name])
